import numpy as np
import ml_dtypes


def mxq(x, axis, fmt="e4m3"):
    dtype, down = {"e4m3": (ml_dtypes.float8_e4m3fn, 7), "e5m2": (ml_dtypes.float8_e5m2, 14)}[fmt]
    v = np.moveaxis(np.asarray(x, np.float32).astype(ml_dtypes.bfloat16).astype(np.float64), axis, -1)
    blocks = v.reshape(v.shape[:-1] + (-1, 32))
    amax = np.abs(blocks).max(-1, keepdims=True)
    byte = np.maximum(np.where(amax > 0, np.frexp(amax)[1] - 1 + 127, 0) - down, 1)
    scale = np.exp2(byte - 127.0)
    codes = (blocks / scale).astype(np.float32).astype(dtype).astype(np.float64)
    return np.moveaxis((codes * scale).reshape(v.shape), -1, axis)


WIDE = False


def mx_kscale(k):
    if not WIDE:
        return np.ones(k)
    levels = np.array([18, -18])
    if k % 512:
        return np.exp2(np.random.permutation(np.resize(levels, k // 32))).repeat(32)
    a = np.empty((k // 512, 16))
    for p in range(k // 512):
        a[p, :8] = np.random.permutation(np.resize(levels, 8))
        for g in range(8):
            far = levels[np.abs(levels - a[p, g]) >= 10]
            a[p, g + 8] = far[np.random.randint(len(far))]
    return np.exp2(a.ravel()).repeat(32)


def f64(x):
    return np.asarray(x).astype(np.float64)


def striped(idx):
    return np.tile(np.asarray(idx).reshape(-1, 16).T, (8, 1)).astype(np.uint16)


def unstriped(offs):
    return offs[:16].T.reshape(-1).astype(np.int64)

def planes(y):
    n, m = y.shape
    v = y.astype(np.float32).astype(ml_dtypes.bfloat16).astype(np.float64).reshape(n // 32, 32, m)
    top = np.abs(v).max(1)
    byte = np.clip(np.where(top > 0, np.frexp(top)[1] - 1 + 127 - 7, 1), 1, 254)
    codes = (v * np.exp2(127.0 - byte)[:, None, :]).reshape(n, m).astype(np.float32).astype(ml_dtypes.float8_e4m3fn).view(np.uint8)
    words = codes.reshape(n // 512, 128, 4, m).transpose(0, 1, 3, 2)
    return np.ascontiguousarray(words), np.ascontiguousarray(byte.astype(np.uint8).reshape(n // 512, 16, m))


def setup_inputs():
    n = np.random.standard_normal
    uni = np.random.uniform
    idx = np.random.permutation(2048)[:512]
    xT_ = np.random.randint(-12, 13, (512, 512)) / 8.0
    f_d = mx_kscale(512)
    f_r = mx_kscale(512)
    return {
        "xT": (xT_ * f_d[:, None]).astype(np.float32),
        "wT": (n((512, 2048)) / np.sqrt(512) / f_d[:, None]).astype(np.float32),
        "us": (uni(0.75, 1.3, (512, 1))).astype(np.float32),
        "ts": np.tile(uni(0.75, 1.3, 2048), (128, 1)).astype(np.float32),
        "wt": (uni(0.75, 1.3, (512, 1)) / np.sqrt(512) * f_r[:, None]).astype(np.float32),
        "x2": (np.square(xT_) / f_r[None, :]).astype(np.float32),
        "y": (n((512, 512))).astype(np.float32),
        "offs": striped(idx),
    }


def reference(xT, wT, us, ts, wt, x2, y, offs):
    idx = unstriped(offs)
    wT_i = f64(wT)[:, idx]
    ts_i = f64(ts)[:1][:, idx]
    a = mxq(f64(xT), 0, "e4m3").T @ mxq(wT_i, 0, "e4m3")
    z = f64(us) * ts_i * a
    g = f64(wt) * np.square(ts_i * f64(us) * (z - f64(y)))
    F = mxq(f64(x2), 1, "e4m3") @ mxq(g, 0, "e5m2")
    out_0 = np.zeros((512, 2048))
    out_0[:, idx] = F
    return (out_0,) + planes(out_0)

@@ -1,0 +1,256 @@
+from contextlib import ExitStack
+
+import concourse.mybir as mybir
+from concourse.masks import make_identity
+
+D, R, I, T = 512, 512, 512, 2048
+FLOPS = 2 * 2 * D * R * I
+
+F32 = mybir.dt.float32
+BF16 = mybir.dt.bfloat16
+U32 = mybir.dt.uint32
+I32 = mybir.dt.int32
+U16 = mybir.dt.uint16
+U8 = mybir.dt.uint8
+E4M3X4 = mybir.dt.float8_e4m3fn_x4
+E5M2X4 = mybir.dt.float8_e5m2_x4
+MULT = mybir.AluOpType.mult
+SUBTRACT = mybir.AluOpType.subtract
+COPY = mybir.ActivationFunctionType.Copy
+SQUARE = mybir.ActivationFunctionType.Square
+
+P = 128
+LANES = 4
+SLOT_CHUNK = 128
+SLOT_CHUNKS = I // SLOT_CHUNK
+COL_CHUNK = 256
+COL_CHUNKS = T // COL_CHUNK
+
+
+def tile_attend_gfisher_sq_pl_kernel(tc, xT, wT, us, ts, wt, x2, y, offs, out_0, out_1, out_2):
+    nc = tc.nc
+    with ExitStack() as ctx:
+        keep = ctx.enter_context(tc.tile_pool(name="keep", bufs=1))
+        sums = ctx.enter_context(tc.psum_pool(name="sums", bufs=4))
+        turns = ctx.enter_context(tc.psum_pool(name="turns", bufs=4))
+
+        def sbuf(name, shape, dtype):
+            return keep.tile(shape, dtype, name=name, align_bytes=64)
+
+        def slots(c):
+            return slice(c * SLOT_CHUNK, (c + 1) * SLOT_CHUNK)
+
+        offsets = keep.tile([P, I // 16], U16, name="offsets")
+        w_rows = wT.rearrange("(p j) c -> p j c", j=LANES)
+        x_rows = xT.rearrange("(p j) r -> p j r", j=LANES)
+        x2_rows = x2.rearrange("(p j) r -> p j r", j=LANES)
+        out_rows = out_0.rearrange("(p j) c -> p j c", j=LANES)
+
+        w_window = [sbuf(f"w_window{j}", [P, T], F32) for j in range(LANES)]
+        x_pair = [sbuf(f"x_pair{h}", [P, 2, R], F32) for h in range(2)]
+        x2_pair = [sbuf(f"x2_pair{h}", [P, 2, R], F32) for h in range(2)]
+        y_sb = sbuf("y_sb", [P, LANES, I], F32)
+        us_sb = sbuf("us_sb", [P, LANES], F32)
+        wt_sb = sbuf("wt_sb", [P, LANES], F32)
+        ts_window = sbuf("ts_window", [P, T], F32)
+
+        ts_columns = sbuf("ts_columns", [P, T // P], F32)
+        nc.sync.dma_start(ts_columns[:], ts[0:1, :].rearrange("o (k c) -> (o k) c", k=P))
+        nc.sync.dma_start(w_window[0][:], w_rows[:, 0, :])
+        nc.sync.dma_start(offsets[:], offs)
+        nc.scalar.dma_start(us_sb[:], us.rearrange("(s t) o -> s (t o)", t=LANES))
+        nc.scalar.dma_start(wt_sb[:], wt.rearrange("(s t) o -> s (t o)", t=LANES))
+        for j in range(1, LANES):
+            nc.sync.dma_start(w_window[j][:], w_rows[:, j, :])
+        for h in range(2):
+            nc.sync.dma_start(x_pair[h][:], x_rows[:, 2 * h : 2 * h + 2, :])
+        nc.sync.dma_start(y_sb[:], y.rearrange("(s t) i -> s t i", t=LANES))
+        for h in range(2):
+            nc.sync.dma_start(x2_pair[h][:], x2_rows[:, 2 * h : 2 * h + 2, :])
+
+        identity = sbuf("identity", [P, P], F32)
+        make_identity(nc, identity[:])
+        out_window = [sbuf(f"out_window{j}", [P, T], F32) for j in range(LANES)]
+        for j in range(LANES):
+            nc.gpsimd.memset(out_window[j][:], 0.0)
+
+        window_by_row = ts_window[:].rearrange("p (k c) -> p k c", k=P)
+        for b in range(T // P // 4):
+            bank = turns.tile([P, 4, P], F32, tag="turn", name=f"ts_spread{b}")
+            for c in range(4):
+                column = ts_columns[:, 4 * b + c : 4 * b + c + 1]
+                nc.tensor.transpose(bank[:, c, :], column.to_broadcast([P, P]), identity[:])
+            copy = nc.scalar.copy if b % 2 else nc.vector.tensor_copy
+            copy(window_by_row[:, :, 4 * b : 4 * b + 4], bank[:].rearrange("p c k -> p k c"))
+        ts_all = sbuf("ts_all", [P, I], F32)
+        ts_squared = sbuf("ts_squared", [P, I], F32)
+        nc.vector.tensor_copy(ts_all[:], ts_window[:].indirect(offsets[:]))
+        nc.scalar.activation(ts_squared[:], ts_all[:], SQUARE)
+
+        us_squared = sbuf("us_squared", [P, LANES], F32)
+        row_factor = sbuf("row_factor", [P, LANES], F32)
+        nc.vector.tensor_tensor(us_squared[:], us_sb[:], us_sb[:], MULT)
+        nc.vector.tensor_tensor(row_factor[:], us_squared[:], wt_sb[:], MULT)
+        factor_by_lane = sbuf("factor_by_lane", [P, LANES, I], F32)
+        for t in range(LANES):
+            nc.scalar.activation(factor_by_lane[:, t, :], ts_squared[:], COPY, scale=row_factor[:, t : t + 1])
+
+        w_grouped = sbuf("w_grouped", [P, I, LANES], BF16)
+        for j in range(LANES):
+            nc.vector.tensor_copy(w_grouped[:, :, j], w_window[j][:].indirect(offsets[:]))
+        w_codes = sbuf("w_codes", [P, I], U32)
+        w_scales = sbuf("w_scales", [P, I], U8)
+        nc.vector.quantize_mx(w_codes[:].bitcast(E4M3X4), w_scales[:], w_grouped[:].rearrange("p i j -> p (i j)"))
+
+        x_grouped = sbuf("x_grouped", [P, LANES, P, LANES], BF16)
+        x_copy = [nc.scalar.copy, nc.vector.tensor_copy]
+        for h in range(2):
+            x_copy[h](
+                x_grouped[:, :, :, 2 * h : 2 * h + 2].rearrange("p t s e -> p s e t"),
+                x_pair[h][:].rearrange("p e (s t) -> p s e t", t=LANES),
+            )
+        factor = [sbuf(f"factor{c}", [P, SLOT_CHUNK, LANES], F32) for c in range(SLOT_CHUNKS)]
+        for c in range(SLOT_CHUNKS):
+            nc.scalar.copy(factor[c][:], factor_by_lane[:, :, slots(c)].rearrange("p t i -> p i t"))
+        x_codes = sbuf("x_codes", [P, LANES, P], U32)
+        x_scales = sbuf("x_scales", [P, LANES, P], U8)
+        z = sbuf("z", [P, LANES, I], F32)
+        scores = []
+        for t in range(LANES):
+            nc.vector.quantize_mx(
+                x_codes[:, t, :].bitcast(E4M3X4), x_scales[:, t, :], x_grouped[:, t, :, :].rearrange("p s j -> p (s j)")
+            )
+            bank = sums.tile([P, I], F32, tag="sum", name=f"scores{t}")
+            nc.tensor.matmul_mx(
+                bank[:],
+                lhsT=x_codes[:, t, :].bitcast(E4M3X4),
+                lhsT_scale=x_scales[:, t, :],
+                rhs=w_codes[:].bitcast(E4M3X4),
+                rhs_scale=w_scales[:],
+                start=True,
+                stop=True,
+            )
+            scores.append(bank)
+        for t in range(LANES):
+            nc.vector.scalar_tensor_tensor(z[:, t, :], scores[t][:], us_sb[:, t : t + 1], ts_all[:], MULT, MULT)
+
+        x2_banks = []
+        for j in range(LANES):
+            bank = turns.tile([P, LANES, P], F32, tag="turn", name=f"x2_turned{j}")
+            rows = x2_pair[j // 2][:, j % 2, :].rearrange("p (s t) -> p t s", t=LANES)
+            for t in range(LANES):
+                nc.tensor.transpose(bank[:, t, :], rows[:, t, :], identity[:])
+            x2_banks.append(bank)
+        x2_grouped = [sbuf(f"x2_grouped{j}", [P, P, LANES], BF16) for j in range(LANES)]
+        x2_codes = [sbuf(f"x2_codes{j}", [P, P], U32) for j in range(LANES)]
+        x2_scales = [sbuf(f"x2_scales{j}", [P, P], U8) for j in range(LANES)]
+
+        def group_x2(j):
+            nc.scalar.copy(x2_grouped[j][:], x2_banks[j][:].rearrange("s t p -> s p t"))
+
+        def quantise_x2(j):
+            nc.vector.quantize_mx(
+                x2_codes[j][:].bitcast(E4M3X4), x2_scales[j][:], x2_grouped[j][:].rearrange("s p t -> s (p t)")
+            )
+
+        error = [sbuf(f"error{c}", [P, LANES, SLOT_CHUNK], F32) for c in range(SLOT_CHUNKS)]
+        squared = [sbuf(f"squared{c}", [P, SLOT_CHUNK, LANES], F32) for c in range(SLOT_CHUNKS)]
+        g_grouped = [sbuf(f"g_grouped{c}", [P, SLOT_CHUNK, LANES], BF16) for c in range(SLOT_CHUNKS)]
+        g_codes = sbuf("g_codes", [P, I], U32)
+        g_scales = sbuf("g_scales", [P, I], U8)
+
+        def subtract_targets(c):
+            nc.vector.tensor_tensor(error[c][:], z[:, :, slots(c)], y_sb[:, :, slots(c)], SUBTRACT)
+            nc.scalar.activation(squared[c][:], error[c][:].rearrange("p t i -> p i t"), SQUARE)
+
+        def weigh(c):
+            nc.vector.tensor_tensor(g_grouped[c][:], squared[c][:], factor[c][:], MULT)
+
+        def quantise_g(c):
+            nc.vector.quantize_mx(
+                g_codes[:, slots(c)].bitcast(E5M2X4), g_scales[:, slots(c)], g_grouped[c][:].rearrange("p i t -> p (i t)")
+            )
+
+        subtract_targets(0)
+        subtract_targets(1)
+        subtract_targets(2)
+        weigh(0)
+        subtract_targets(3)
+        group_x2(0)
+        weigh(1)
+        quantise_g(0)
+        weigh(2)
+        quantise_g(1)
+        weigh(3)
+        quantise_x2(0)
+        quantise_g(2)
+        quantise_g(3)
+
+        fisher = [sbuf(f"fisher{j}", [P, I], F32) for j in range(LANES)]
+
+        def second_product(j):
+            bank = sums.tile([P, I], F32, tag="sum", name=f"fisher_sum{j}")
+            nc.tensor.matmul_mx(
+                bank[:],
+                lhsT=x2_codes[j][:].bitcast(E4M3X4),
+                lhsT_scale=x2_scales[j][:],
+                rhs=g_codes[:].bitcast(E5M2X4),
+                rhs_scale=g_scales[:],
+                start=True,
+                stop=True,
+            )
+            nc.scalar.copy(fisher[j][:], bank[:])
+
+        for j in range(1, LANES):
+            group_x2(j)
+        second_product(0)
+        for j in range(1, LANES):
+            quantise_x2(j)
+            second_product(j)
+
+        out_pairs = [sbuf(f"out_pairs{k}", [P, 2, COL_CHUNK, 2], BF16) for k in range(COL_CHUNKS)]
+        out_grouped = [sbuf(f"out_grouped{k}", [P, COL_CHUNK * LANES], BF16) for k in range(COL_CHUNKS)]
+        out_codes = sbuf("out_codes", [P, T], U32)
+        out_scales = sbuf("out_scales", [P, T], U8)
+        words_out = out_1.rearrange("a p c l -> p (a c l)").bitcast(I32)
+        scales_out = out_2.rearrange("a q c -> q (a c)").bitcast(I32)
+
+        def columns(k):
+            return slice(k * COL_CHUNK, (k + 1) * COL_CHUNK)
+
+        def round_lane(copy, j, k):
+            copy(out_pairs[k][:, j // 2, :, j % 2], out_window[j][:, columns(k)])
+
+        def join_pairs(copy, k):
+            copy(
+                out_grouped[k][:].bitcast(F32).rearrange("p (c u) -> p c u", u=2),
+                out_pairs[k][:].rearrange("p u c e -> p u (c e)").bitcast(F32).rearrange("p u c -> p c u"),
+            )
+
+        def quantise_out(k):
+            nc.vector.quantize_mx(out_codes[:, columns(k)].bitcast(E4M3X4), out_scales[:, columns(k)], out_grouped[k][:])
+
+        def store_words(first, end):
+            cols = slice(first * COL_CHUNK, end * COL_CHUNK)
+            nc.sync.dma_start(words_out[:, cols], out_codes[:, cols].bitcast(I32))
+
+        for j in range(LANES):
+            nc.vector.tensor_copy(out_window[j][:].indirect(offsets[:]), fisher[j][:])
+            nc.sync.dma_start(out_rows[:, j, :], out_window[j][:])
+            for k in range(COL_CHUNKS):
+                round_lane(nc.scalar.copy, j, k)
+        scalar_joins = 2
+        for k in range(COL_CHUNKS - scalar_joins, COL_CHUNKS):
+            join_pairs(nc.scalar.copy, k)
+        join_pairs(nc.vector.tensor_copy, 0)
+        for k in range(COL_CHUNKS):
+            if k + 1 < COL_CHUNKS - scalar_joins:
+                join_pairs(nc.vector.tensor_copy, k + 1)
+            quantise_out(k)
+            if k >= COL_CHUNKS - 2:
+                store_words(k, k + 1)
+            elif k % 2:
+                store_words(k - 1, k + 1)
+        for q in range(4):
+            queue = nc.scalar if q % 2 else nc.sync
+            queue.dma_start(scales_out[4 * q : 4 * q + 4, :], out_scales[32 * q : 32 * q + 4, :].bitcast(I32))

@@ -72,7 +72,7 @@ def tile_attend_gfisher_sq_pl_kernel(tc, xT, wT, us, ts, wt, x2, y, offs, out_0,
         make_identity(nc, identity[:])
         out_window = [sbuf(f"out_window{j}", [P, T], F32) for j in range(LANES)]
         for j in range(LANES):
-            nc.gpsimd.memset(out_window[j][:], 0.0)
+            nc.vector.memset(out_window[j][:], 0.0)
 
         window_by_row = ts_window[:].rearrange("p (k c) -> p k c", k=P)
         for b in range(T // P // 4):
@@ -80,8 +80,7 @@ def tile_attend_gfisher_sq_pl_kernel(tc, xT, wT, us, ts, wt, x2, y, offs, out_0,
             for c in range(4):
                 column = ts_columns[:, 4 * b + c : 4 * b + c + 1]
                 nc.tensor.transpose(bank[:, c, :], column.to_broadcast([P, P]), identity[:])
-            copy = nc.scalar.copy if b % 2 else nc.vector.tensor_copy
-            copy(window_by_row[:, :, 4 * b : 4 * b + 4], bank[:].rearrange("p c k -> p k c"))
+            nc.scalar.copy(window_by_row[:, :, 4 * b : 4 * b + 4], bank[:].rearrange("p c k -> p k c"))
         ts_all = sbuf("ts_all", [P, I], F32)
         ts_squared = sbuf("ts_squared", [P, I], F32)
         nc.vector.tensor_copy(ts_all[:], ts_window[:].indirect(offsets[:]))
@@ -211,9 +210,9 @@ def tile_attend_gfisher_sq_pl_kernel(tc, xT, wT, us, ts, wt, x2, y, offs, out_0,
         out_pairs = [sbuf(f"out_pairs{k}", [P, 2, COL_CHUNK, 2], BF16) for k in range(COL_CHUNKS)]
         out_grouped = [sbuf(f"out_grouped{k}", [P, COL_CHUNK * LANES], BF16) for k in range(COL_CHUNKS)]
         out_codes = sbuf("out_codes", [P, T], U32)
-        out_scales = sbuf("out_scales", [P, T], U8)
+        out_scales = sbuf("out_scales", [P, T // 4], U8)
         words_out = out_1.rearrange("a p c l -> p (a c l)").bitcast(I32)
-        scales_out = out_2.rearrange("a q c -> q (a c)").bitcast(I32)
+        scales_out = out_2.rearrange("a q c -> q (a c)").bitcast(I32).rearrange("q (g c) -> g q c", g=4)
 
         def columns(k):
             return slice(k * COL_CHUNK, (k + 1) * COL_CHUNK)
@@ -228,7 +227,9 @@ def tile_attend_gfisher_sq_pl_kernel(tc, xT, wT, us, ts, wt, x2, y, offs, out_0,
             )
 
         def quantise_out(k):
-            nc.vector.quantize_mx(out_codes[:, columns(k)].bitcast(E4M3X4), out_scales[:, columns(k)], out_grouped[k][:])
+            group, place = divmod(k * COL_CHUNK, T // 4)
+            plane = out_scales[4 * group :, place : place + COL_CHUNK]
+            nc.vector.quantize_mx(out_codes[:, columns(k)].bitcast(E4M3X4), plane, out_grouped[k][:])
 
         def store_words(first, end):
             cols = slice(first * COL_CHUNK, end * COL_CHUNK)
@@ -253,4 +254,4 @@ def tile_attend_gfisher_sq_pl_kernel(tc, xT, wT, us, ts, wt, x2, y, offs, out_0,
                 store_words(k - 1, k + 1)
         for q in range(4):
             queue = nc.scalar if q % 2 else nc.sync
-            queue.dma_start(scales_out[4 * q : 4 * q + 4, :], out_scales[32 * q : 32 * q + 4, :].bitcast(I32))
+            queue.dma_start(scales_out[:, 4 * q : 4 * q + 4, :], out_scales[32 * q : 32 * q + 16, :].bitcast(I32))

@@ -21,6 +21,7 @@ SQUARE = mybir.ActivationFunctionType.Square
 
 P = 128
 LANES = 4
+X_VECTOR_SHARE = 88
 SLOT_CHUNK = 128
 SLOT_CHUNKS = I // SLOT_CHUNK
 COL_CHUNK = 256
@@ -34,8 +35,8 @@ def tile_attend_gfisher_sq_pl_kernel(tc, xT, wT, us, ts, wt, x2, y, offs, out_0,
         sums = ctx.enter_context(tc.psum_pool(name="sums", bufs=4))
         turns = ctx.enter_context(tc.psum_pool(name="turns", bufs=4))
 
-        def sbuf(name, shape, dtype):
-            return keep.tile(shape, dtype, name=name, align_bytes=64)
+        def sbuf(name, shape, dtype, on=None):
+            return keep.tile(shape, dtype, name=name, tag=on or name, align_bytes=64)
 
         def slots(c):
             return slice(c * SLOT_CHUNK, (c + 1) * SLOT_CHUNK)
@@ -72,7 +73,7 @@ def tile_attend_gfisher_sq_pl_kernel(tc, xT, wT, us, ts, wt, x2, y, offs, out_0,
         make_identity(nc, identity[:])
         out_window = [sbuf(f"out_window{j}", [P, T], F32) for j in range(LANES)]
         for j in range(LANES):
-            nc.vector.memset(out_window[j][:], 0.0)
+            nc.gpsimd.memset(out_window[j][:], 0.0)
 
         window_by_row = ts_window[:].rearrange("p (k c) -> p k c", k=P)
         for b in range(T // P // 4):
@@ -80,7 +81,10 @@ def tile_attend_gfisher_sq_pl_kernel(tc, xT, wT, us, ts, wt, x2, y, offs, out_0,
             for c in range(4):
                 column = ts_columns[:, 4 * b + c : 4 * b + c + 1]
                 nc.tensor.transpose(bank[:, c, :], column.to_broadcast([P, P]), identity[:])
-            nc.scalar.copy(window_by_row[:, :, 4 * b : 4 * b + 4], bank[:].rearrange("p c k -> p k c"))
+            copy = nc.scalar.copy if b % 2 else nc.vector.tensor_copy
+            copy(window_by_row[:, :, 4 * b : 4 * b + 4], bank[:].rearrange("p c k -> p k c"))
+        w_first = sbuf("w_first", [P, I], BF16)
+        nc.vector.tensor_copy(w_first[:], w_window[0][:].indirect(offsets[:]))
         ts_all = sbuf("ts_all", [P, I], F32)
         ts_squared = sbuf("ts_squared", [P, I], F32)
         nc.vector.tensor_copy(ts_all[:], ts_window[:].indirect(offsets[:]))
@@ -90,27 +94,41 @@ def tile_attend_gfisher_sq_pl_kernel(tc, xT, wT, us, ts, wt, x2, y, offs, out_0,
         row_factor = sbuf("row_factor", [P, LANES], F32)
         nc.vector.tensor_tensor(us_squared[:], us_sb[:], us_sb[:], MULT)
         nc.vector.tensor_tensor(row_factor[:], us_squared[:], wt_sb[:], MULT)
-        factor_by_lane = sbuf("factor_by_lane", [P, LANES, I], F32)
-        for t in range(LANES):
-            nc.scalar.activation(factor_by_lane[:, t, :], ts_squared[:], COPY, scale=row_factor[:, t : t + 1])
+        factor = []
 
-        w_grouped = sbuf("w_grouped", [P, I, LANES], BF16)
-        for j in range(LANES):
+        def make_factor(half, by_lane_on=None, factor_on=None):
+            by_lane = sbuf(f"factor_by_lane{half}", [P, LANES, I // 2], F32, on=by_lane_on)
+            for t in range(LANES):
+                squares = ts_squared[:, half * I // 2 : (half + 1) * I // 2]
+                nc.scalar.activation(by_lane[:, t, :], squares, COPY, scale=row_factor[:, t : t + 1])
+            grouped = sbuf(f"factor{half}", [P, 2, SLOT_CHUNK, LANES], F32, on=factor_on)
+            for c in range(2):
+                nc.scalar.copy(grouped[:, c], by_lane[:, :, slots(c)].rearrange("p t i -> p i t"))
+                factor.append(grouped[:, c])
+
+        make_factor(0)
+
+        w_grouped = sbuf("w_grouped", [P, I, LANES], BF16, on="ts_window")
+        nc.vector.tensor_copy(w_grouped[:, :, 1], w_window[1][:].indirect(offsets[:]))
+        nc.vector.tensor_copy(w_grouped[:, :, 0], w_first[:])
+        for j in range(2, LANES):
             nc.vector.tensor_copy(w_grouped[:, :, j], w_window[j][:].indirect(offsets[:]))
         w_codes = sbuf("w_codes", [P, I], U32)
         w_scales = sbuf("w_scales", [P, I], U8)
         nc.vector.quantize_mx(w_codes[:].bitcast(E4M3X4), w_scales[:], w_grouped[:].rearrange("p i j -> p (i j)"))
 
-        x_grouped = sbuf("x_grouped", [P, LANES, P, LANES], BF16)
-        x_copy = [nc.scalar.copy, nc.vector.tensor_copy]
-        for h in range(2):
-            x_copy[h](
-                x_grouped[:, :, :, 2 * h : 2 * h + 2].rearrange("p t s e -> p s e t"),
-                x_pair[h][:].rearrange("p e (s t) -> p s e t", t=LANES),
+        x_grouped = sbuf("x_grouped", [P, LANES, P, LANES], BF16, on="factor_by_lane0")
+
+        def deal_x(copy, h, first, end):
+            copy(
+                x_grouped[:, :, first:end, 2 * h : 2 * h + 2].rearrange("p t s e -> p s e t"),
+                x_pair[h][:].rearrange("p e (s t) -> p s e t", t=LANES)[:, first:end],
             )
-        factor = [sbuf(f"factor{c}", [P, SLOT_CHUNK, LANES], F32) for c in range(SLOT_CHUNKS)]
-        for c in range(SLOT_CHUNKS):
-            nc.scalar.copy(factor[c][:], factor_by_lane[:, :, slots(c)].rearrange("p t i -> p i t"))
+
+        deal_x(nc.scalar.copy, 0, 0, P)
+        deal_x(nc.vector.tensor_copy, 1, 0, X_VECTOR_SHARE)
+        deal_x(nc.scalar.copy, 1, X_VECTOR_SHARE, P)
+        make_factor(1, by_lane_on="x_pair0", factor_on="x_pair1")
         x_codes = sbuf("x_codes", [P, LANES, P], U32)
         x_scales = sbuf("x_scales", [P, LANES, P], U8)
         z = sbuf("z", [P, LANES, I], F32)
@@ -135,77 +153,101 @@ def tile_attend_gfisher_sq_pl_kernel(tc, xT, wT, us, ts, wt, x2, y, offs, out_0,
 
         x2_banks = []
         for j in range(LANES):
-            bank = turns.tile([P, LANES, P], F32, tag="turn", name=f"x2_turned{j}")
+            bank = sums.tile([P, LANES, P], F32, tag="sum", name=f"x2_turned{j}")
             rows = x2_pair[j // 2][:, j % 2, :].rearrange("p (s t) -> p t s", t=LANES)
             for t in range(LANES):
                 nc.tensor.transpose(bank[:, t, :], rows[:, t, :], identity[:])
             x2_banks.append(bank)
-        x2_grouped = [sbuf(f"x2_grouped{j}", [P, P, LANES], BF16) for j in range(LANES)]
-        x2_codes = [sbuf(f"x2_codes{j}", [P, P], U32) for j in range(LANES)]
-        x2_scales = [sbuf(f"x2_scales{j}", [P, P], U8) for j in range(LANES)]
+        x2_grouped = [sbuf(f"x2_grouped{j}", [P, P, LANES], BF16)[:] for j in range(2)]
+        x2_codes = [sbuf(f"x2_codes{j}", [P, P], U32)[:] for j in range(2)]
+        x2_scales = [sbuf(f"x2_scales{j}", [P, P], U8)[:] for j in range(2)]
 
         def group_x2(j):
-            nc.scalar.copy(x2_grouped[j][:], x2_banks[j][:].rearrange("s t p -> s p t"))
+            nc.scalar.copy(x2_grouped[j], x2_banks[j][:].rearrange("s t p -> s p t"))
 
         def quantise_x2(j):
             nc.vector.quantize_mx(
-                x2_codes[j][:].bitcast(E4M3X4), x2_scales[j][:], x2_grouped[j][:].rearrange("s p t -> s (p t)")
+                x2_codes[j].bitcast(E4M3X4), x2_scales[j], x2_grouped[j].rearrange("s p t -> s (p t)")
             )
 
         error = [sbuf(f"error{c}", [P, LANES, SLOT_CHUNK], F32) for c in range(SLOT_CHUNKS)]
         squared = [sbuf(f"squared{c}", [P, SLOT_CHUNK, LANES], F32) for c in range(SLOT_CHUNKS)]
         g_grouped = [sbuf(f"g_grouped{c}", [P, SLOT_CHUNK, LANES], BF16) for c in range(SLOT_CHUNKS)]
-        g_codes = sbuf("g_codes", [P, I], U32)
-        g_scales = sbuf("g_scales", [P, I], U8)
+        half = I // 2
+        padded_codes = sbuf("padded_codes", [P, half + I], U32)
+        padded_scales = sbuf("padded_scales", [P, half + I], U8)
+        nc.gpsimd.memset(padded_codes[:, :half], 0)
+        nc.gpsimd.memset(padded_scales[:, :half], 0)
+        g_codes = padded_codes[:, half:]
+        g_scales = padded_scales[:, half:]
 
         def subtract_targets(c):
             nc.vector.tensor_tensor(error[c][:], z[:, :, slots(c)], y_sb[:, :, slots(c)], SUBTRACT)
             nc.scalar.activation(squared[c][:], error[c][:].rearrange("p t i -> p i t"), SQUARE)
 
         def weigh(c):
-            nc.vector.tensor_tensor(g_grouped[c][:], squared[c][:], factor[c][:], MULT)
+            nc.vector.tensor_tensor(g_grouped[c][:], squared[c][:], factor[c], MULT)
 
         def quantise_g(c):
             nc.vector.quantize_mx(
                 g_codes[:, slots(c)].bitcast(E5M2X4), g_scales[:, slots(c)], g_grouped[c][:].rearrange("p i t -> p (i t)")
             )
 
+        group_x2(0)
         subtract_targets(0)
         subtract_targets(1)
         subtract_targets(2)
         weigh(0)
         subtract_targets(3)
-        group_x2(0)
+        group_x2(1)
         weigh(1)
         quantise_g(0)
+        quantise_x2(0)
         weigh(2)
         quantise_g(1)
-        weigh(3)
-        quantise_x2(0)
-        quantise_g(2)
-        quantise_g(3)
 
-        fisher = [sbuf(f"fisher{j}", [P, I], F32) for j in range(LANES)]
-
-        def second_product(j):
-            bank = sums.tile([P, I], F32, tag="sum", name=f"fisher_sum{j}")
+        def second_product(j, codes, scales):
+            bank = turns.tile([P, I], F32, tag="turn", name="fisher_sum")
             nc.tensor.matmul_mx(
                 bank[:],
-                lhsT=x2_codes[j][:].bitcast(E4M3X4),
-                lhsT_scale=x2_scales[j][:],
-                rhs=g_codes[:].bitcast(E5M2X4),
-                rhs_scale=g_scales[:],
+                lhsT=x2_codes[j].bitcast(E4M3X4),
+                lhsT_scale=x2_scales[j],
+                rhs=codes.bitcast(E5M2X4),
+                rhs_scale=scales,
                 start=True,
                 stop=True,
             )
-            nc.scalar.copy(fisher[j][:], bank[:])
+            return bank
 
-        for j in range(1, LANES):
+        early_sum = second_product(0, padded_codes[:, :I], padded_scales[:, :I])
+        weigh(3)
+        quantise_g(2)
+        quantise_g(3)
+        early = sbuf("early", [P, half], F32)
+        nc.scalar.copy(early[:], early_sum[:, half:])
+
+        x2_grouped_rest = sbuf("x2_grouped_rest", [P, 2, P, LANES], BF16, on=f"error{SLOT_CHUNKS - 1}")
+        for j in range(2, LANES):
+            x2_grouped.append(x2_grouped_rest[:, j - 2])
             group_x2(j)
-        second_product(0)
+        late = sbuf("late", [P, half], F32)
+        nc.scalar.copy(late[:], second_product(0, g_codes, g_scales)[:, half:])
+        pieces = [[(late, slice(half // 16, I // 16))]]
+        quantise_x2(1)
+        rest_codes = sbuf("rest_codes", [P, 2, P], U32)
+        rest_scales = sbuf("rest_scales", [P, 2, P], U8)
+        x2_codes.extend([rest_codes[:, 0], rest_codes[:, 1]])
+        x2_scales.extend([rest_scales[:, 0], rest_scales[:, 1]])
+        nc.vector.tensor_copy(out_window[0][:].indirect(offsets[:, : half // 16]), early[:])
+        nc.vector.quantize_mx(
+            rest_codes[:].rearrange("s j p -> s (j p)").bitcast(E4M3X4),
+            rest_scales[:].rearrange("s j p -> s (j p)"),
+            x2_grouped_rest[:].rearrange("s j p t -> s (j p t)"),
+        )
         for j in range(1, LANES):
-            quantise_x2(j)
-            second_product(j)
+            fisher = sbuf(f"fisher{j}", [P, I], F32)
+            nc.scalar.copy(fisher[:], second_product(j, g_codes, g_scales)[:])
+            pieces.append([(fisher, slice(0, I // 16))])
 
         out_pairs = [sbuf(f"out_pairs{k}", [P, 2, COL_CHUNK, 2], BF16) for k in range(COL_CHUNKS)]
         out_grouped = [sbuf(f"out_grouped{k}", [P, COL_CHUNK * LANES], BF16) for k in range(COL_CHUNKS)]
@@ -236,7 +278,8 @@ def tile_attend_gfisher_sq_pl_kernel(tc, xT, wT, us, ts, wt, x2, y, offs, out_0,
             nc.sync.dma_start(words_out[:, cols], out_codes[:, cols].bitcast(I32))
 
         for j in range(LANES):
-            nc.vector.tensor_copy(out_window[j][:].indirect(offsets[:]), fisher[j][:])
+            for values, entries in pieces[j]:
+                nc.vector.tensor_copy(out_window[j][:].indirect(offsets[:, entries]), values[:])
             nc.sync.dma_start(out_rows[:, j, :], out_window[j][:])
             for k in range(COL_CHUNKS):
                 round_lane(nc.scalar.copy, j, k)

@@ -72,7 +72,8 @@ def tile_attend_gfisher_sq_pl_kernel(tc, xT, wT, us, ts, wt, x2, y, offs, out_0,
         identity = sbuf("identity", [P, P], F32)
         make_identity(nc, identity[:])
         out_window = [sbuf(f"out_window{j}", [P, T], F32) for j in range(LANES)]
-        for j in range(LANES):
+        nc.vector.memset(out_window[0][:], 0.0)
+        for j in range(1, LANES):
             nc.gpsimd.memset(out_window[j][:], 0.0)
 
         window_by_row = ts_window[:].rearrange("p (k c) -> p k c", k=P)
@@ -172,7 +173,7 @@ def tile_attend_gfisher_sq_pl_kernel(tc, xT, wT, us, ts, wt, x2, y, offs, out_0,
 
         error = [sbuf(f"error{c}", [P, LANES, SLOT_CHUNK], F32) for c in range(SLOT_CHUNKS)]
         squared = [sbuf(f"squared{c}", [P, SLOT_CHUNK, LANES], F32) for c in range(SLOT_CHUNKS)]
-        g_grouped = [sbuf(f"g_grouped{c}", [P, SLOT_CHUNK, LANES], BF16) for c in range(SLOT_CHUNKS)]
+        g_grouped = [sbuf(f"g_grouped{h}", [P, 2, SLOT_CHUNK, LANES], BF16) for h in range(2)]
         half = I // 2
         padded_codes = sbuf("padded_codes", [P, half + I], U32)
         padded_scales = sbuf("padded_scales", [P, half + I], U8)
@@ -186,11 +187,12 @@ def tile_attend_gfisher_sq_pl_kernel(tc, xT, wT, us, ts, wt, x2, y, offs, out_0,
             nc.scalar.activation(squared[c][:], error[c][:].rearrange("p t i -> p i t"), SQUARE)
 
         def weigh(c):
-            nc.vector.tensor_tensor(g_grouped[c][:], squared[c][:], factor[c], MULT)
+            nc.vector.tensor_tensor(g_grouped[c // 2][:, c % 2], squared[c][:], factor[c], MULT)
 
-        def quantise_g(c):
+        def quantise_g(h):
+            cols = slice(h * half, (h + 1) * half)
             nc.vector.quantize_mx(
-                g_codes[:, slots(c)].bitcast(E5M2X4), g_scales[:, slots(c)], g_grouped[c][:].rearrange("p i t -> p (i t)")
+                g_codes[:, cols].bitcast(E5M2X4), g_scales[:, cols], g_grouped[h][:].rearrange("p c i t -> p (c i t)")
             )
 
         group_x2(0)
@@ -201,10 +203,8 @@ def tile_attend_gfisher_sq_pl_kernel(tc, xT, wT, us, ts, wt, x2, y, offs, out_0,
         subtract_targets(3)
         group_x2(1)
         weigh(1)
-        quantise_g(0)
         quantise_x2(0)
-        weigh(2)
-        quantise_g(1)
+        quantise_g(0)
 
         def second_product(j, codes, scales):
             bank = turns.tile([P, I], F32, tag="turn", name="fisher_sum")
@@ -220,25 +220,23 @@ def tile_attend_gfisher_sq_pl_kernel(tc, xT, wT, us, ts, wt, x2, y, offs, out_0,
             return bank
 
         early_sum = second_product(0, padded_codes[:, :I], padded_scales[:, :I])
+        weigh(2)
         weigh(3)
-        quantise_g(2)
-        quantise_g(3)
+        quantise_x2(1)
+        quantise_g(1)
         early = sbuf("early", [P, half], F32)
         nc.scalar.copy(early[:], early_sum[:, half:])
-
         x2_grouped_rest = sbuf("x2_grouped_rest", [P, 2, P, LANES], BF16, on=f"error{SLOT_CHUNKS - 1}")
         for j in range(2, LANES):
             x2_grouped.append(x2_grouped_rest[:, j - 2])
             group_x2(j)
         late = sbuf("late", [P, half], F32)
         nc.scalar.copy(late[:], second_product(0, g_codes, g_scales)[:, half:])
-        pieces = [[(late, slice(half // 16, I // 16))]]
-        quantise_x2(1)
+        pieces = [[(early, slice(0, half // 16)), (late, slice(half // 16, I // 16))]]
         rest_codes = sbuf("rest_codes", [P, 2, P], U32)
         rest_scales = sbuf("rest_scales", [P, 2, P], U8)
         x2_codes.extend([rest_codes[:, 0], rest_codes[:, 1]])
         x2_scales.extend([rest_scales[:, 0], rest_scales[:, 1]])
-        nc.vector.tensor_copy(out_window[0][:].indirect(offsets[:, : half // 16]), early[:])
         nc.vector.quantize_mx(
             rest_codes[:].rearrange("s j p -> s (j p)").bitcast(E4M3X4),
             rest_scales[:].rearrange("s j p -> s (j p)"),

@@ -21,11 +21,12 @@ SQUARE = mybir.ActivationFunctionType.Square
 
 P = 128
 LANES = 4
-X_VECTOR_SHARE = 88
+X_VECTOR_SHARE = 96
 SLOT_CHUNK = 128
 SLOT_CHUNKS = I // SLOT_CHUNK
-COL_CHUNK = 256
-COL_CHUNKS = T // COL_CHUNK
+COL_WIDTHS = [128, 128, 256, 256, 256, 256, 256, 128, 128, 256]
+COL_CHUNKS = len(COL_WIDTHS)
+COL_STARTS = [sum(COL_WIDTHS[:k]) for k in range(COL_CHUNKS + 1)]
 
 
 def tile_attend_gfisher_sq_pl_kernel(tc, xT, wT, us, ts, wt, x2, y, offs, out_0, out_1, out_2):
@@ -104,7 +105,10 @@ def tile_attend_gfisher_sq_pl_kernel(tc, xT, wT, us, ts, wt, x2, y, offs, out_0,
                 nc.scalar.activation(by_lane[:, t, :], squares, COPY, scale=row_factor[:, t : t + 1])
             grouped = sbuf(f"factor{half}", [P, 2, SLOT_CHUNK, LANES], F32, on=factor_on)
             for c in range(2):
-                nc.scalar.copy(grouped[:, c], by_lane[:, :, slots(c)].rearrange("p t i -> p i t"))
+                nc.scalar.copy(
+                    grouped[:, c].rearrange("p (q i) t -> p q t i", i=4),
+                    by_lane[:, :, slots(c)].rearrange("p t (q i) -> p q t i", i=4),
+                )
                 factor.append(grouped[:, c])
 
         make_factor(0)
@@ -120,15 +124,16 @@ def tile_attend_gfisher_sq_pl_kernel(tc, xT, wT, us, ts, wt, x2, y, offs, out_0,
 
         x_grouped = sbuf("x_grouped", [P, LANES, P, LANES], BF16, on="factor_by_lane0")
 
-        def deal_x(copy, h, first, end):
+        def deal_x(copy, h, tiles, first, end):
             copy(
-                x_grouped[:, :, first:end, 2 * h : 2 * h + 2].rearrange("p t s e -> p s e t"),
-                x_pair[h][:].rearrange("p e (s t) -> p s e t", t=LANES)[:, first:end],
+                x_grouped[:, tiles, first:end, 2 * h : 2 * h + 2].rearrange("p t s e -> p s e t"),
+                x_pair[h][:].rearrange("p e (s t) -> p s e t", t=LANES)[:, first:end, :, tiles],
             )
 
-        deal_x(nc.scalar.copy, 0, 0, P)
-        deal_x(nc.vector.tensor_copy, 1, 0, X_VECTOR_SHARE)
-        deal_x(nc.scalar.copy, 1, X_VECTOR_SHARE, P)
+        deal_x(nc.scalar.copy, 0, slice(0, 4), 0, P)
+        deal_x(nc.vector.tensor_copy, 1, slice(0, 2), 0, P)
+        deal_x(nc.vector.tensor_copy, 1, slice(2, 4), 0, X_VECTOR_SHARE)
+        deal_x(nc.scalar.copy, 1, slice(2, 4), X_VECTOR_SHARE, P)
         make_factor(1, by_lane_on="x_pair0", factor_on="x_pair1")
         x_codes = sbuf("x_codes", [P, LANES, P], U32)
         x_scales = sbuf("x_scales", [P, LANES, P], U8)
@@ -150,7 +155,10 @@ def tile_attend_gfisher_sq_pl_kernel(tc, xT, wT, us, ts, wt, x2, y, offs, out_0,
             )
             scores.append(bank)
         for t in range(LANES):
-            nc.vector.scalar_tensor_tensor(z[:, t, :], scores[t][:], us_sb[:, t : t + 1], ts_all[:], MULT, MULT)
+            for cols in [slice(0, I)] if t + 1 < LANES else [slice(0, I // 2), slice(I // 2, I)]:
+                nc.vector.scalar_tensor_tensor(
+                    z[:, t, cols], scores[t][:, cols], us_sb[:, t : t + 1], ts_all[:, cols], MULT, MULT
+                )
 
         x2_banks = []
         for j in range(LANES):
@@ -159,7 +167,7 @@ def tile_attend_gfisher_sq_pl_kernel(tc, xT, wT, us, ts, wt, x2, y, offs, out_0,
             for t in range(LANES):
                 nc.tensor.transpose(bank[:, t, :], rows[:, t, :], identity[:])
             x2_banks.append(bank)
-        x2_grouped = [sbuf(f"x2_grouped{j}", [P, P, LANES], BF16)[:] for j in range(2)]
+        x2_grouped = []
         x2_codes = [sbuf(f"x2_codes{j}", [P, P], U32)[:] for j in range(2)]
         x2_scales = [sbuf(f"x2_scales{j}", [P, P], U8)[:] for j in range(2)]
 
@@ -184,7 +192,11 @@ def tile_attend_gfisher_sq_pl_kernel(tc, xT, wT, us, ts, wt, x2, y, offs, out_0,
 
         def subtract_targets(c):
             nc.vector.tensor_tensor(error[c][:], z[:, :, slots(c)], y_sb[:, :, slots(c)], SUBTRACT)
-            nc.scalar.activation(squared[c][:], error[c][:].rearrange("p t i -> p i t"), SQUARE)
+            nc.scalar.activation(
+                squared[c][:].rearrange("p (q i) t -> p q t i", i=4),
+                error[c][:].rearrange("p t (q i) -> p q t i", i=4),
+                SQUARE,
+            )
 
         def weigh(c):
             nc.vector.tensor_tensor(g_grouped[c // 2][:, c % 2], squared[c][:], factor[c], MULT)
@@ -195,12 +207,14 @@ def tile_attend_gfisher_sq_pl_kernel(tc, xT, wT, us, ts, wt, x2, y, offs, out_0,
                 g_codes[:, cols].bitcast(E5M2X4), g_scales[:, cols], g_grouped[h][:].rearrange("p c i t -> p (c i t)")
             )
 
-        group_x2(0)
         subtract_targets(0)
         subtract_targets(1)
+        x2_grouped.append(sbuf("x2_grouped0", [P, P, LANES], BF16, on="error1")[:])
+        group_x2(0)
         subtract_targets(2)
         weigh(0)
         subtract_targets(3)
+        x2_grouped.append(sbuf("x2_grouped1", [P, P, LANES], BF16, on="error3")[:])
         group_x2(1)
         weigh(1)
         quantise_x2(0)
@@ -226,7 +240,7 @@ def tile_attend_gfisher_sq_pl_kernel(tc, xT, wT, us, ts, wt, x2, y, offs, out_0,
         quantise_g(1)
         early = sbuf("early", [P, half], F32)
         nc.scalar.copy(early[:], early_sum[:, half:])
-        x2_grouped_rest = sbuf("x2_grouped_rest", [P, 2, P, LANES], BF16, on=f"error{SLOT_CHUNKS - 1}")
+        x2_grouped_rest = sbuf("x2_grouped_rest", [P, 2, P, LANES], BF16, on="squared2")
         for j in range(2, LANES):
             x2_grouped.append(x2_grouped_rest[:, j - 2])
             group_x2(j)
@@ -247,15 +261,15 @@ def tile_attend_gfisher_sq_pl_kernel(tc, xT, wT, us, ts, wt, x2, y, offs, out_0,
             nc.scalar.copy(fisher[:], second_product(j, g_codes, g_scales)[:])
             pieces.append([(fisher, slice(0, I // 16))])
 
-        out_pairs = [sbuf(f"out_pairs{k}", [P, 2, COL_CHUNK, 2], BF16) for k in range(COL_CHUNKS)]
-        out_grouped = [sbuf(f"out_grouped{k}", [P, COL_CHUNK * LANES], BF16) for k in range(COL_CHUNKS)]
+        out_pairs = [sbuf(f"out_pairs{k}", [P, 2, COL_WIDTHS[k], 2], BF16) for k in range(COL_CHUNKS)]
+        out_grouped = [sbuf(f"out_grouped{k}", [P, COL_WIDTHS[k] * LANES], BF16) for k in range(COL_CHUNKS)]
         out_codes = sbuf("out_codes", [P, T], U32)
         out_scales = sbuf("out_scales", [P, T // 4], U8)
         words_out = out_1.rearrange("a p c l -> p (a c l)").bitcast(I32)
         scales_out = out_2.rearrange("a q c -> q (a c)").bitcast(I32).rearrange("q (g c) -> g q c", g=4)
 
         def columns(k):
-            return slice(k * COL_CHUNK, (k + 1) * COL_CHUNK)
+            return slice(COL_STARTS[k], COL_STARTS[k + 1])
 
         def round_lane(copy, j, k):
             copy(out_pairs[k][:, j // 2, :, j % 2], out_window[j][:, columns(k)])
@@ -267,12 +281,12 @@ def tile_attend_gfisher_sq_pl_kernel(tc, xT, wT, us, ts, wt, x2, y, offs, out_0,
             )
 
         def quantise_out(k):
-            group, place = divmod(k * COL_CHUNK, T // 4)
-            plane = out_scales[4 * group :, place : place + COL_CHUNK]
+            group, place = divmod(COL_STARTS[k], T // 4)
+            plane = out_scales[4 * group :, place : place + COL_WIDTHS[k]]
             nc.vector.quantize_mx(out_codes[:, columns(k)].bitcast(E4M3X4), plane, out_grouped[k][:])
 
         def store_words(first, end):
-            cols = slice(first * COL_CHUNK, end * COL_CHUNK)
+            cols = slice(COL_STARTS[first], COL_STARTS[end])
             nc.sync.dma_start(words_out[:, cols], out_codes[:, cols].bitcast(I32))
 
         for j in range(LANES):
@@ -285,14 +299,14 @@ def tile_attend_gfisher_sq_pl_kernel(tc, xT, wT, us, ts, wt, x2, y, offs, out_0,
         for k in range(COL_CHUNKS - scalar_joins, COL_CHUNKS):
             join_pairs(nc.scalar.copy, k)
         join_pairs(nc.vector.tensor_copy, 0)
+        stored = 0
         for k in range(COL_CHUNKS):
             if k + 1 < COL_CHUNKS - scalar_joins:
                 join_pairs(nc.vector.tensor_copy, k + 1)
             quantise_out(k)
-            if k >= COL_CHUNKS - 2:
-                store_words(k, k + 1)
-            elif k % 2:
-                store_words(k - 1, k + 1)
+            if COL_STARTS[k + 1] % (T // 4) == 0 or k == COL_CHUNKS - 2:
+                store_words(stored, k + 1)
+                stored = k + 1
         for q in range(4):
             queue = nc.scalar if q % 2 else nc.sync
             queue.dma_start(scales_out[:, 4 * q : 4 * q + 4, :], out_scales[32 * q : 32 * q + 16, :].bitcast(I32))

@@ -21,10 +21,11 @@ SQUARE = mybir.ActivationFunctionType.Square
 
 P = 128
 LANES = 4
-X_VECTOR_SHARE = 96
+X_VECTOR_SHARE = 16
+PAIRS_PLACE = 8192
 SLOT_CHUNK = 128
 SLOT_CHUNKS = I // SLOT_CHUNK
-COL_WIDTHS = [128, 128, 256, 256, 256, 256, 256, 128, 128, 256]
+COL_WIDTHS = [128, 128, 256, 256, 256, 512, 256, 256]
 COL_CHUNKS = len(COL_WIDTHS)
 COL_STARTS = [sum(COL_WIDTHS[:k]) for k in range(COL_CHUNKS + 1)]
 
@@ -33,11 +34,15 @@ def tile_attend_gfisher_sq_pl_kernel(tc, xT, wT, us, ts, wt, x2, y, offs, out_0,
     nc = tc.nc
     with ExitStack() as ctx:
         keep = ctx.enter_context(tc.tile_pool(name="keep", bufs=1))
-        sums = ctx.enter_context(tc.psum_pool(name="sums", bufs=4))
+        placed = ctx.enter_context(tc.tile_pool(name="placed", bufs=1))
+        sums = ctx.enter_context(tc.psum_pool(name="sums", bufs=1))
         turns = ctx.enter_context(tc.psum_pool(name="turns", bufs=4))
 
         def sbuf(name, shape, dtype, on=None):
             return keep.tile(shape, dtype, name=name, tag=on or name, align_bytes=64)
+
+        def placed_at(name, shape, dtype, offset):
+            return placed.tile(shape, dtype, name=name, align_bytes=64, offset=offset)
 
         def slots(c):
             return slice(c * SLOT_CHUNK, (c + 1) * SLOT_CHUNK)
@@ -49,7 +54,7 @@ def tile_attend_gfisher_sq_pl_kernel(tc, xT, wT, us, ts, wt, x2, y, offs, out_0,
         out_rows = out_0.rearrange("(p j) c -> p j c", j=LANES)
 
         w_window = [sbuf(f"w_window{j}", [P, T], F32) for j in range(LANES)]
-        x_pair = [sbuf(f"x_pair{h}", [P, 2, R], F32) for h in range(2)]
+        x_sb = placed_at("x_sb", [P, LANES, R], F32, 0)
         x2_pair = [sbuf(f"x2_pair{h}", [P, 2, R], F32) for h in range(2)]
         y_sb = sbuf("y_sb", [P, LANES, I], F32)
         us_sb = sbuf("us_sb", [P, LANES], F32)
@@ -64,11 +69,12 @@ def tile_attend_gfisher_sq_pl_kernel(tc, xT, wT, us, ts, wt, x2, y, offs, out_0,
         nc.scalar.dma_start(wt_sb[:], wt.rearrange("(s t) o -> s (t o)", t=LANES))
         for j in range(1, LANES):
             nc.sync.dma_start(w_window[j][:], w_rows[:, j, :])
+        nc.sync.dma_start(x_sb[:], x_rows)
+        y_rows = y.rearrange("(s t) i -> s t i", t=LANES)
+        nc.sync.dma_start(x2_pair[0][:], x2_rows[:, 0:2, :])
         for h in range(2):
-            nc.sync.dma_start(x_pair[h][:], x_rows[:, 2 * h : 2 * h + 2, :])
-        nc.sync.dma_start(y_sb[:], y.rearrange("(s t) i -> s t i", t=LANES))
-        for h in range(2):
-            nc.sync.dma_start(x2_pair[h][:], x2_rows[:, 2 * h : 2 * h + 2, :])
+            nc.sync.dma_start(y_sb[:, 2 * h : 2 * h + 2, :], y_rows[:, 2 * h : 2 * h + 2, :])
+        nc.sync.dma_start(x2_pair[1][:], x2_rows[:, 2:4, :])
 
         identity = sbuf("identity", [P, P], F32)
         make_identity(nc, identity[:])
@@ -98,12 +104,14 @@ def tile_attend_gfisher_sq_pl_kernel(tc, xT, wT, us, ts, wt, x2, y, offs, out_0,
         nc.vector.tensor_tensor(row_factor[:], us_squared[:], wt_sb[:], MULT)
         factor = []
 
-        def make_factor(half, by_lane_on=None, factor_on=None):
-            by_lane = sbuf(f"factor_by_lane{half}", [P, LANES, I // 2], F32, on=by_lane_on)
+        def factor_by_lane(half):
+            by_lane = sbuf(f"factor_by_lane{half}", [P, LANES, I // 2], F32)
             for t in range(LANES):
                 squares = ts_squared[:, half * I // 2 : (half + 1) * I // 2]
                 nc.scalar.activation(by_lane[:, t, :], squares, COPY, scale=row_factor[:, t : t + 1])
-            grouped = sbuf(f"factor{half}", [P, 2, SLOT_CHUNK, LANES], F32, on=factor_on)
+            return by_lane
+
+        def group_factor(grouped, by_lane):
             for c in range(2):
                 nc.scalar.copy(
                     grouped[:, c].rearrange("p (q i) t -> p q t i", i=4),
@@ -111,7 +119,8 @@ def tile_attend_gfisher_sq_pl_kernel(tc, xT, wT, us, ts, wt, x2, y, offs, out_0,
                 )
                 factor.append(grouped[:, c])
 
-        make_factor(0)
+        group_factor(sbuf("factor0", [P, 2, SLOT_CHUNK, LANES], F32), factor_by_lane(0))
+        late_by_lane = factor_by_lane(1)
 
         w_grouped = sbuf("w_grouped", [P, I, LANES], BF16, on="ts_window")
         nc.vector.tensor_copy(w_grouped[:, :, 1], w_window[1][:].indirect(offsets[:]))
@@ -124,26 +133,30 @@ def tile_attend_gfisher_sq_pl_kernel(tc, xT, wT, us, ts, wt, x2, y, offs, out_0,
 
         x_grouped = sbuf("x_grouped", [P, LANES, P, LANES], BF16, on="factor_by_lane0")
 
-        def deal_x(copy, h, tiles, first, end):
+        def deal_x(copy, tiles, first, end):
             copy(
-                x_grouped[:, tiles, first:end, 2 * h : 2 * h + 2].rearrange("p t s e -> p s e t"),
-                x_pair[h][:].rearrange("p e (s t) -> p s e t", t=LANES)[:, first:end, :, tiles],
+                x_grouped[:, tiles, first:end, :].rearrange("p t s j -> p s j t"),
+                x_sb[:].rearrange("p j (s t) -> p s j t", t=LANES)[:, first:end, :, tiles],
             )
 
-        deal_x(nc.scalar.copy, 0, slice(0, 4), 0, P)
-        deal_x(nc.vector.tensor_copy, 1, slice(0, 2), 0, P)
-        deal_x(nc.vector.tensor_copy, 1, slice(2, 4), 0, X_VECTOR_SHARE)
-        deal_x(nc.scalar.copy, 1, slice(2, 4), X_VECTOR_SHARE, P)
-        make_factor(1, by_lane_on="x_pair0", factor_on="x_pair1")
+        deal_x(nc.vector.tensor_copy, slice(0, 2), 0, 80)
+        deal_x(nc.scalar.copy, slice(0, 2), 80, P)
+        deal_x(nc.vector.tensor_copy, slice(2, 4), 0, 48)
+        deal_x(nc.scalar.copy, slice(2, 4), 48, P)
+        x2_words = placed_at("x2_words", [P, 2, 2, P, 2], BF16, 0)
+        nc.scalar.copy(x2_words[:], x2_pair[0][:].rearrange("p j (s u e) -> p j u s e", u=2, e=2))
+        group_factor(placed_at("factor1", [P, 2, SLOT_CHUNK, LANES], F32, 2048), late_by_lane)
         x_codes = sbuf("x_codes", [P, LANES, P], U32)
         x_scales = sbuf("x_scales", [P, LANES, P], U8)
         z = sbuf("z", [P, LANES, I], F32)
+        half = I // 2
+        z_early = {(0, 0): sbuf("z00", [P, half], F32), (0, 1): sbuf("z01", [P, half], F32)}
         scores = []
         for t in range(LANES):
             nc.vector.quantize_mx(
                 x_codes[:, t, :].bitcast(E4M3X4), x_scales[:, t, :], x_grouped[:, t, :, :].rearrange("p s j -> p (s j)")
             )
-            bank = sums.tile([P, I], F32, tag="sum", name=f"scores{t}")
+            bank = sums.tile([P, I], F32, tag=f"sum{t}", name=f"scores{t}")
             nc.tensor.matmul_mx(
                 bank[:],
                 lhsT=x_codes[:, t, :].bitcast(E4M3X4),
@@ -155,34 +168,47 @@ def tile_attend_gfisher_sq_pl_kernel(tc, xT, wT, us, ts, wt, x2, y, offs, out_0,
             )
             scores.append(bank)
         for t in range(LANES):
-            for cols in [slice(0, I)] if t + 1 < LANES else [slice(0, I // 2), slice(I // 2, I)]:
+            if t in (1, 2):
+                nc.vector.scalar_tensor_tensor(z[:, t, :], scores[t][:], us_sb[:, t : t + 1], ts_all[:], MULT, MULT)
+                continue
+            for h in (1, 0) if t == 1 else (0, 1):
+                cols = slice(h * half, (h + 1) * half)
+                target = z_early[t, h][:] if (t, h) in z_early else z[:, t, cols]
                 nc.vector.scalar_tensor_tensor(
-                    z[:, t, cols], scores[t][:, cols], us_sb[:, t : t + 1], ts_all[:, cols], MULT, MULT
+                    target, scores[t][:, cols], us_sb[:, t : t + 1], ts_all[:, cols], MULT, MULT
                 )
 
+        words = x2_words[:].rearrange("p j u s e -> p (j u) (s e)").bitcast(F32)
+        word_bank = sums.tile([P, 2, 2, P], F32, tag="sum0", name="x2_turned_words")
+        for j in range(2):
+            for u in range(2):
+                nc.tensor.transpose(word_bank[:, j, u, :], words[:, 2 * j + u, :], identity[:])
         x2_banks = []
-        for j in range(LANES):
-            bank = sums.tile([P, LANES, P], F32, tag="sum", name=f"x2_turned{j}")
-            rows = x2_pair[j // 2][:, j % 2, :].rearrange("p (s t) -> p t s", t=LANES)
+        for j in range(2):
+            bank = sums.tile([P, LANES, P], F32, tag=f"sum{3 * j}", name=f"x2_turned{j}")
+            rows = x2_pair[1][:, j, :].rearrange("p (s t) -> p t s", t=LANES)
             for t in range(LANES):
                 nc.tensor.transpose(bank[:, t, :], rows[:, t, :], identity[:])
             x2_banks.append(bank)
-        x2_grouped = []
-        x2_codes = [sbuf(f"x2_codes{j}", [P, P], U32)[:] for j in range(2)]
-        x2_scales = [sbuf(f"x2_scales{j}", [P, P], U8)[:] for j in range(2)]
+        first_grouped = sbuf("first_grouped", [P, 2 * P * LANES], BF16)
+        nc.scalar.copy(
+            first_grouped[:].bitcast(F32).rearrange("s (j p u) -> s j p u", j=2, u=2),
+            word_bank[:].rearrange("s j u p -> s j p u"),
+        )
+        first_codes = sbuf("first_codes", [P, 2 * P], U32)
+        first_scales = sbuf("first_scales", [P, 2 * P], U8)
+        x2_codes = [first_codes[:, :P], first_codes[:, P:]]
+        x2_scales = [first_scales[:, :P], first_scales[:, P:]]
 
-        def group_x2(j):
-            nc.scalar.copy(x2_grouped[j], x2_banks[j][:].rearrange("s t p -> s p t"))
-
-        def quantise_x2(j):
-            nc.vector.quantize_mx(
-                x2_codes[j].bitcast(E4M3X4), x2_scales[j], x2_grouped[j].rearrange("s p t -> s (p t)")
-            )
-
-        error = [sbuf(f"error{c}", [P, LANES, SLOT_CHUNK], F32) for c in range(SLOT_CHUNKS)]
+        error = [sbuf(f"error{h}", [P, LANES, I // 2], F32) for h in range(2)]
+        gpsimd_tiles = [1, 1]
+        for t in range(2):
+            for h in range(2):
+                if t < gpsimd_tiles[h]:
+                    cols = slice(h * I // 2, (h + 1) * I // 2)
+                    nc.gpsimd.tensor_tensor(error[h][:, t, :], z_early[t, h][:], y_sb[:, t, cols], SUBTRACT)
         squared = [sbuf(f"squared{c}", [P, SLOT_CHUNK, LANES], F32) for c in range(SLOT_CHUNKS)]
         g_grouped = [sbuf(f"g_grouped{h}", [P, 2, SLOT_CHUNK, LANES], BF16) for h in range(2)]
-        half = I // 2
         padded_codes = sbuf("padded_codes", [P, half + I], U32)
         padded_scales = sbuf("padded_scales", [P, half + I], U8)
         nc.gpsimd.memset(padded_codes[:, :half], 0)
@@ -191,34 +217,33 @@ def tile_attend_gfisher_sq_pl_kernel(tc, xT, wT, us, ts, wt, x2, y, offs, out_0,
         g_scales = padded_scales[:, half:]
 
         def subtract_targets(c):
-            nc.vector.tensor_tensor(error[c][:], z[:, :, slots(c)], y_sb[:, :, slots(c)], SUBTRACT)
+            first = gpsimd_tiles[c // 2]
+            errors = error[c // 2][:, :, slots(c % 2)]
+            nc.vector.tensor_tensor(errors[:, first:], z[:, first:, slots(c)], y_sb[:, first:, slots(c)], SUBTRACT)
             nc.scalar.activation(
                 squared[c][:].rearrange("p (q i) t -> p q t i", i=4),
-                error[c][:].rearrange("p t (q i) -> p q t i", i=4),
+                errors.rearrange("p t (q i) -> p q t i", i=4),
                 SQUARE,
             )
 
         def weigh(c):
             nc.vector.tensor_tensor(g_grouped[c // 2][:, c % 2], squared[c][:], factor[c], MULT)
 
-        def quantise_g(h):
-            cols = slice(h * half, (h + 1) * half)
+        def quantise_g(first, end):
+            cols = slice(first * SLOT_CHUNK, end * SLOT_CHUNK)
+            values = g_grouped[first // 2][:, first % 2 : first % 2 + end - first]
             nc.vector.quantize_mx(
-                g_codes[:, cols].bitcast(E5M2X4), g_scales[:, cols], g_grouped[h][:].rearrange("p c i t -> p (c i t)")
+                g_codes[:, cols].bitcast(E5M2X4), g_scales[:, cols], values.rearrange("p c i t -> p (c i t)")
             )
 
         subtract_targets(0)
         subtract_targets(1)
-        x2_grouped.append(sbuf("x2_grouped0", [P, P, LANES], BF16, on="error1")[:])
-        group_x2(0)
         subtract_targets(2)
         weigh(0)
         subtract_targets(3)
-        x2_grouped.append(sbuf("x2_grouped1", [P, P, LANES], BF16, on="error3")[:])
-        group_x2(1)
         weigh(1)
-        quantise_x2(0)
-        quantise_g(0)
+        nc.vector.quantize_mx(first_codes[:].bitcast(E4M3X4), first_scales[:], first_grouped[:])
+        quantise_g(0, 2)
 
         def second_product(j, codes, scales):
             bank = turns.tile([P, I], F32, tag="turn", name="fisher_sum")
@@ -236,32 +261,31 @@ def tile_attend_gfisher_sq_pl_kernel(tc, xT, wT, us, ts, wt, x2, y, offs, out_0,
         early_sum = second_product(0, padded_codes[:, :I], padded_scales[:, :I])
         weigh(2)
         weigh(3)
-        quantise_x2(1)
-        quantise_g(1)
-        early = sbuf("early", [P, half], F32)
+        quantise_g(2, 3)
+        quantise_g(3, 4)
+        early = sbuf("early", [P, half], F32, on="squared3")
         nc.scalar.copy(early[:], early_sum[:, half:])
-        x2_grouped_rest = sbuf("x2_grouped_rest", [P, 2, P, LANES], BF16, on="squared2")
-        for j in range(2, LANES):
-            x2_grouped.append(x2_grouped_rest[:, j - 2])
-            group_x2(j)
+        rest_grouped = []
+        for j, freed in enumerate(["squared2", "g_grouped1"]):
+            rest_grouped.append(sbuf(f"rest_grouped{j}", [P, P, LANES], BF16, on=freed))
+            nc.scalar.copy(rest_grouped[j][:], x2_banks[j][:].rearrange("s t p -> s p t"))
         late = sbuf("late", [P, half], F32)
         nc.scalar.copy(late[:], second_product(0, g_codes, g_scales)[:, half:])
         pieces = [[(early, slice(0, half // 16)), (late, slice(half // 16, I // 16))]]
-        rest_codes = sbuf("rest_codes", [P, 2, P], U32)
+        rest_codes = placed_at("rest_codes", [P, 32, P], U32, PAIRS_PLACE)[:, 0:2]
         rest_scales = sbuf("rest_scales", [P, 2, P], U8)
         x2_codes.extend([rest_codes[:, 0], rest_codes[:, 1]])
         x2_scales.extend([rest_scales[:, 0], rest_scales[:, 1]])
-        nc.vector.quantize_mx(
-            rest_codes[:].rearrange("s j p -> s (j p)").bitcast(E4M3X4),
-            rest_scales[:].rearrange("s j p -> s (j p)"),
-            x2_grouped_rest[:].rearrange("s j p t -> s (j p t)"),
-        )
+        for j in range(2):
+            nc.vector.quantize_mx(
+                rest_codes[:, j].bitcast(E4M3X4), rest_scales[:, j], rest_grouped[j][:].rearrange("s p t -> s (p t)")
+            )
         for j in range(1, LANES):
             fisher = sbuf(f"fisher{j}", [P, I], F32)
             nc.scalar.copy(fisher[:], second_product(j, g_codes, g_scales)[:])
             pieces.append([(fisher, slice(0, I // 16))])
 
-        out_pairs = [sbuf(f"out_pairs{k}", [P, 2, COL_WIDTHS[k], 2], BF16) for k in range(COL_CHUNKS)]
+        out_pairs = [placed_at(f"out_pairs{k}", [P, 2, COL_WIDTHS[k], 2], BF16, PAIRS_PLACE + 8 * COL_STARTS[k]) for k in range(COL_CHUNKS)]
         out_grouped = [sbuf(f"out_grouped{k}", [P, COL_WIDTHS[k] * LANES], BF16) for k in range(COL_CHUNKS)]
         out_codes = sbuf("out_codes", [P, T], U32)
         out_scales = sbuf("out_scales", [P, T // 4], U8)

@@ -16,6 +16,7 @@ E4M3X4 = mybir.dt.float8_e4m3fn_x4
 E5M2X4 = mybir.dt.float8_e5m2_x4
 MULT = mybir.AluOpType.mult
 SUBTRACT = mybir.AluOpType.subtract
+ADD = mybir.AluOpType.add
 COPY = mybir.ActivationFunctionType.Copy
 SQUARE = mybir.ActivationFunctionType.Square
 
@@ -25,7 +26,10 @@ X_VECTOR_SHARE = 16
 PAIRS_PLACE = 8192
 SLOT_CHUNK = 128
 SLOT_CHUNKS = I // SLOT_CHUNK
-COL_WIDTHS = [128, 128, 256, 256, 256, 512, 256, 256]
+COL_WIDTHS = [128, 128, 256, 256, 256, 256, 256, 256, 128, 128]
+VECTOR_DIRECT = [0, 1]
+PAIRED = [2, 3, 4, 5, 6, 7]
+SCALAR_DIRECT = [8, 9]
 COL_CHUNKS = len(COL_WIDTHS)
 COL_STARTS = [sum(COL_WIDTHS[:k]) for k in range(COL_CHUNKS + 1)]
 
@@ -125,11 +129,17 @@ def tile_attend_gfisher_sq_pl_kernel(tc, xT, wT, us, ts, wt, x2, y, offs, out_0,
         w_grouped = sbuf("w_grouped", [P, I, LANES], BF16, on="ts_window")
         nc.vector.tensor_copy(w_grouped[:, :, 1], w_window[1][:].indirect(offsets[:]))
         nc.vector.tensor_copy(w_grouped[:, :, 0], w_first[:])
-        for j in range(2, LANES):
-            nc.vector.tensor_copy(w_grouped[:, :, j], w_window[j][:].indirect(offsets[:]))
+        nc.vector.tensor_copy(w_grouped[:, :, 2], w_window[2][:].indirect(offsets[:]))
+        for h in range(2):
+            entries = offsets[:, h * I // 32 : (h + 1) * I // 32]
+            nc.vector.tensor_copy(w_grouped[:, h * I // 2 : (h + 1) * I // 2, 3], w_window[3][:].indirect(entries))
         w_codes = sbuf("w_codes", [P, I], U32)
         w_scales = sbuf("w_scales", [P, I], U8)
-        nc.vector.quantize_mx(w_codes[:].bitcast(E4M3X4), w_scales[:], w_grouped[:].rearrange("p i j -> p (i j)"))
+        for h in range(2):
+            cols = slice(h * I // 2, (h + 1) * I // 2)
+            nc.vector.quantize_mx(
+                w_codes[:, cols].bitcast(E4M3X4), w_scales[:, cols], w_grouped[:, cols].rearrange("p i j -> p (i j)")
+            )
 
         x_grouped = sbuf("x_grouped", [P, LANES, P, LANES], BF16, on="factor_by_lane0")
 
@@ -208,7 +218,8 @@ def tile_attend_gfisher_sq_pl_kernel(tc, xT, wT, us, ts, wt, x2, y, offs, out_0,
                     cols = slice(h * I // 2, (h + 1) * I // 2)
                     nc.gpsimd.tensor_tensor(error[h][:, t, :], z_early[t, h][:], y_sb[:, t, cols], SUBTRACT)
         squared = [sbuf(f"squared{c}", [P, SLOT_CHUNK, LANES], F32) for c in range(SLOT_CHUNKS)]
-        g_grouped = [sbuf(f"g_grouped{h}", [P, 2, SLOT_CHUNK, LANES], BF16) for h in range(2)]
+        g_first = sbuf("g_first", [P, 2, SLOT_CHUNK, LANES], BF16)
+        g_grouped = [g_first[:, 0], g_first[:, 1]]
         padded_codes = sbuf("padded_codes", [P, half + I], U32)
         padded_scales = sbuf("padded_scales", [P, half + I], U8)
         nc.gpsimd.memset(padded_codes[:, :half], 0)
@@ -226,24 +237,21 @@ def tile_attend_gfisher_sq_pl_kernel(tc, xT, wT, us, ts, wt, x2, y, offs, out_0,
                 SQUARE,
             )
 
-        def weigh(c):
-            nc.vector.tensor_tensor(g_grouped[c // 2][:, c % 2], squared[c][:], factor[c], MULT)
+        def weigh(engine, c):
+            engine.tensor_tensor(g_grouped[c], squared[c][:], factor[c], MULT)
 
-        def quantise_g(first, end):
+        def quantise_g(first, end, values):
             cols = slice(first * SLOT_CHUNK, end * SLOT_CHUNK)
-            values = g_grouped[first // 2][:, first % 2 : first % 2 + end - first]
-            nc.vector.quantize_mx(
-                g_codes[:, cols].bitcast(E5M2X4), g_scales[:, cols], values.rearrange("p c i t -> p (c i t)")
-            )
+            nc.vector.quantize_mx(g_codes[:, cols].bitcast(E5M2X4), g_scales[:, cols], values)
 
         subtract_targets(0)
         subtract_targets(1)
         subtract_targets(2)
-        weigh(0)
+        weigh(nc.vector, 0)
         subtract_targets(3)
-        weigh(1)
+        weigh(nc.vector, 1)
         nc.vector.quantize_mx(first_codes[:].bitcast(E4M3X4), first_scales[:], first_grouped[:])
-        quantise_g(0, 2)
+        quantise_g(0, 2, g_first[:].rearrange("p c i t -> p (c i t)"))
 
         def second_product(j, codes, scales):
             bank = turns.tile([P, I], F32, tag="turn", name="fisher_sum")
@@ -258,34 +266,48 @@ def tile_attend_gfisher_sq_pl_kernel(tc, xT, wT, us, ts, wt, x2, y, offs, out_0,
             )
             return bank
 
-        early_sum = second_product(0, padded_codes[:, :I], padded_scales[:, :I])
-        weigh(2)
-        weigh(3)
-        quantise_g(2, 3)
-        quantise_g(3, 4)
-        early = sbuf("early", [P, half], F32, on="squared3")
-        nc.scalar.copy(early[:], early_sum[:, half:])
-        rest_grouped = []
-        for j, freed in enumerate(["squared2", "g_grouped1"]):
-            rest_grouped.append(sbuf(f"rest_grouped{j}", [P, P, LANES], BF16, on=freed))
-            nc.scalar.copy(rest_grouped[j][:], x2_banks[j][:].rearrange("s t p -> s p t"))
-        late = sbuf("late", [P, half], F32)
-        nc.scalar.copy(late[:], second_product(0, g_codes, g_scales)[:, half:])
-        pieces = [[(early, slice(0, half // 16)), (late, slice(half // 16, I // 16))]]
+        early_sums = [second_product(j, padded_codes[:, :I], padded_scales[:, :I]) for j in range(2)]
         rest_codes = placed_at("rest_codes", [P, 32, P], U32, PAIRS_PLACE)[:, 0:2]
         rest_scales = sbuf("rest_scales", [P, 2, P], U8)
         x2_codes.extend([rest_codes[:, 0], rest_codes[:, 1]])
         x2_scales.extend([rest_scales[:, 0], rest_scales[:, 1]])
-        for j in range(2):
-            nc.vector.quantize_mx(
-                rest_codes[:, j].bitcast(E4M3X4), rest_scales[:, j], rest_grouped[j][:].rearrange("s p t -> s (p t)")
-            )
-        for j in range(1, LANES):
-            fisher = sbuf(f"fisher{j}", [P, I], F32)
-            nc.scalar.copy(fisher[:], second_product(j, g_codes, g_scales)[:])
-            pieces.append([(fisher, slice(0, I // 16))])
 
-        out_pairs = [placed_at(f"out_pairs{k}", [P, 2, COL_WIDTHS[k], 2], BF16, PAIRS_PLACE + 8 * COL_STARTS[k]) for k in range(COL_CHUNKS)]
+        def group_rest(j, freed):
+            grouped = sbuf(f"rest_grouped{j}", [P, P, LANES], BF16, on=freed)
+            nc.scalar.copy(grouped[:], x2_banks[j][:].rearrange("s t p -> s p t"))
+            return grouped[:].rearrange("s p t -> s (p t)")
+
+        def quantise_rest(j, grouped):
+            nc.vector.quantize_mx(rest_codes[:, j].bitcast(E4M3X4), rest_scales[:, j], grouped)
+
+        def leave_bank(name, bank, cols, on=None):
+            values = sbuf(name, [P, cols.stop - cols.start], F32, on=on)
+            nc.scalar.copy(values[:], bank[:, cols])
+            return values
+
+        upper = slice(half, I)
+        rest_grouped = group_rest(0, "error1")
+        g_grouped.append(sbuf("g_third", [P, SLOT_CHUNK, LANES], BF16)[:])
+        weigh(nc.vector, 2)
+        quantise_rest(0, rest_grouped)
+        quantise_g(2, 3, g_grouped[2].rearrange("p i t -> p (i t)"))
+        early = [leave_bank("early0", early_sums[0], upper, on="squared2")]
+        g_grouped.append(sbuf("g_fourth", [P, SLOT_CHUNK, LANES], BF16, on="g_third")[:])
+        weigh(nc.gpsimd, 3)
+        early.append(leave_bank("early1", early_sums[1], upper, on="squared3"))
+        quantise_g(3, 4, g_grouped[3].rearrange("p i t -> p (i t)"))
+        rest_grouped = group_rest(1, "g_third")
+        late = [leave_bank(f"late{j}", second_product(j, g_codes, g_scales), upper) for j in range(2)]
+        quantise_rest(1, rest_grouped)
+        whole = [leave_bank(f"fisher{j}", second_product(j, g_codes, g_scales), slice(0, I)) for j in range(2, LANES)]
+        first_entries, last_entries = slice(0, half // 16), slice(half // 16, I // 16)
+        for j in range(2):
+            nc.vector.tensor_copy(out_window[j][:].indirect(offsets[:, first_entries]), early[j][:])
+        pieces = [(late[0], last_entries), (late[1], last_entries)] + [(f, slice(0, I // 16)) for f in whole]
+
+        out_pairs = placed_at("out_pairs", [P, T * LANES], BF16, PAIRS_PLACE)
+        pair_lanes = out_pairs[:].rearrange("p (u c e) -> p u c e", u=2, e=2)
+        pair_words = out_pairs[:].bitcast(F32).rearrange("p (u c) -> p c u", u=2)
         out_grouped = [sbuf(f"out_grouped{k}", [P, COL_WIDTHS[k] * LANES], BF16) for k in range(COL_CHUNKS)]
         out_codes = sbuf("out_codes", [P, T], U32)
         out_scales = sbuf("out_scales", [P, T // 4], U8)
@@ -295,13 +317,13 @@ def tile_attend_gfisher_sq_pl_kernel(tc, xT, wT, us, ts, wt, x2, y, offs, out_0,
         def columns(k):
             return slice(COL_STARTS[k], COL_STARTS[k + 1])
 
-        def round_lane(copy, j, k):
-            copy(out_pairs[k][:, j // 2, :, j % 2], out_window[j][:, columns(k)])
+        def round_lane(j, cols):
+            nc.scalar.copy(pair_lanes[:, j // 2, cols, j % 2], out_window[j][:, cols])
 
         def join_pairs(copy, k):
             copy(
                 out_grouped[k][:].bitcast(F32).rearrange("p (c u) -> p c u", u=2),
-                out_pairs[k][:].rearrange("p u c e -> p u (c e)").bitcast(F32).rearrange("p u c -> p c u"),
+                pair_words[:, columns(k)],
             )
 
         def quantise_out(k):
@@ -314,21 +336,34 @@ def tile_attend_gfisher_sq_pl_kernel(tc, xT, wT, us, ts, wt, x2, y, offs, out_0,
             nc.sync.dma_start(words_out[:, cols], out_codes[:, cols].bitcast(I32))
 
         for j in range(LANES):
-            for values, entries in pieces[j]:
-                nc.vector.tensor_copy(out_window[j][:].indirect(offsets[:, entries]), values[:])
-            nc.sync.dma_start(out_rows[:, j, :], out_window[j][:])
-            for k in range(COL_CHUNKS):
-                round_lane(nc.scalar.copy, j, k)
-        scalar_joins = 2
-        for k in range(COL_CHUNKS - scalar_joins, COL_CHUNKS):
-            join_pairs(nc.scalar.copy, k)
-        join_pairs(nc.vector.tensor_copy, 0)
+            values, entries = pieces[j]
+            nc.vector.tensor_copy(out_window[j][:].indirect(offsets[:, entries]), values[:])
+            (nc.scalar if j == LANES - 1 else nc.sync).dma_start(out_rows[:, j, :], out_window[j][:])
+            last = j + 1 == LANES
+            for k in VECTOR_DIRECT + SCALAR_DIRECT:
+                lanes = out_grouped[k][:].rearrange("p (c l) -> p c l", l=LANES)
+                values = out_window[j][:, columns(k)]
+                if last:
+                    if k in VECTOR_DIRECT:
+                        nc.vector.tensor_copy(lanes[:, :, j], values)
+                elif j == 2:
+                    both = values.unsqueeze(2).to_broadcast([P, COL_WIDTHS[k], 2])
+                    nc.gpsimd.tensor_scalar(lanes[:, :, 2:4], both, 1.0, 0.0, MULT, ADD)
+                else:
+                    nc.gpsimd.tensor_scalar(lanes[:, :, j], values, 1.0, 0.0, MULT, ADD)
+            all_paired = slice(COL_STARTS[PAIRED[0]], COL_STARTS[PAIRED[-1] + 1])
+            for cols in [columns(k) for k in PAIRED] if last else [all_paired]:
+                round_lane(j, cols)
+        join_pairs(nc.scalar.copy, PAIRED[-1])
+        for k in SCALAR_DIRECT:
+            lanes = out_grouped[k][:].rearrange("p (c l) -> p c l", l=LANES)
+            nc.scalar.copy(lanes[:, :, LANES - 1], out_window[LANES - 1][:, columns(k)])
         stored = 0
         for k in range(COL_CHUNKS):
-            if k + 1 < COL_CHUNKS - scalar_joins:
+            if k + 1 in PAIRED[:-1]:
                 join_pairs(nc.vector.tensor_copy, k + 1)
             quantise_out(k)
-            if COL_STARTS[k + 1] % (T // 4) == 0 or k == COL_CHUNKS - 2:
+            if COL_STARTS[k + 1] % (T // 4) == 0 or k == COL_CHUNKS - 3:
                 store_words(stored, k + 1)
                 stored = k + 1
         for q in range(4):

@@ -15,23 +15,31 @@ U8 = mybir.dt.uint8
 E4M3X4 = mybir.dt.float8_e4m3fn_x4
 E5M2X4 = mybir.dt.float8_e5m2_x4
 MULT = mybir.AluOpType.mult
-SUBTRACT = mybir.AluOpType.subtract
 ADD = mybir.AluOpType.add
+SUBTRACT = mybir.AluOpType.subtract
 COPY = mybir.ActivationFunctionType.Copy
 SQUARE = mybir.ActivationFunctionType.Square
 
 P = 128
 LANES = 4
-X_VECTOR_SHARE = 16
-PAIRS_PLACE = 8192
+LINE = 4
+HALF = I // 2
 SLOT_CHUNK = 128
-SLOT_CHUNKS = I // SLOT_CHUNK
+SCALE_GROUP = T // 4
+
+VECTOR_DEALS = [80, 48]
+LAST_SLOTS = 32
 COL_WIDTHS = [128, 128, 256, 256, 256, 256, 256, 256, 128, 128]
-VECTOR_DIRECT = [0, 1]
-PAIRED = [2, 3, 4, 5, 6, 7]
-SCALAR_DIRECT = [8, 9]
-COL_CHUNKS = len(COL_WIDTHS)
-COL_STARTS = [sum(COL_WIDTHS[:k]) for k in range(COL_CHUNKS + 1)]
+COL_STARTS = [sum(COL_WIDTHS[:k]) for k in range(len(COL_WIDTHS) + 1)]
+DIRECT_CHUNKS = [0, 1]
+VECTOR_JOINED = [2, 3, 4, 5, 6]
+SCALAR_JOINED = [7, 8, 9]
+GPSIMD_PAIRED = 384
+
+X_PLACE = 0
+PAIRS_PLACE = X_PLACE + LANES * R * 4
+G_PLACE = PAIRS_PLACE + T * LANES * 2
+G_BYTES = SLOT_CHUNK * LANES * 2
 
 
 def tile_attend_gfisher_sq_pl_kernel(tc, xT, wT, us, ts, wt, x2, y, offs, out_0, out_1, out_2):
@@ -51,21 +59,45 @@ def tile_attend_gfisher_sq_pl_kernel(tc, xT, wT, us, ts, wt, x2, y, offs, out_0,
         def slots(c):
             return slice(c * SLOT_CHUNK, (c + 1) * SLOT_CHUNK)
 
+        def half_slots(h):
+            return slice(h * HALF, (h + 1) * HALF)
+
+        def half_entries(h):
+            return slice(h * HALF // 16, (h + 1) * HALF // 16)
+
+        def interleave(instruction, grouped, by_lane, *function):
+            instruction(
+                grouped.rearrange("p (q i) t -> p q t i", i=LINE),
+                by_lane.rearrange("p t (q i) -> p q t i", i=LINE),
+                *function,
+            )
+
+        def product(bank, stationary_codes, stationary_scales, moving_codes, moving_scales):
+            nc.tensor.matmul_mx(
+                bank[:],
+                lhsT=stationary_codes,
+                lhsT_scale=stationary_scales,
+                rhs=moving_codes,
+                rhs_scale=moving_scales,
+                start=True,
+                stop=True,
+            )
+
         offsets = keep.tile([P, I // 16], U16, name="offsets")
         w_rows = wT.rearrange("(p j) c -> p j c", j=LANES)
-        x_rows = xT.rearrange("(p j) r -> p j r", j=LANES)
         x2_rows = x2.rearrange("(p j) r -> p j r", j=LANES)
+        y_rows = y.rearrange("(s t) i -> s t i", t=LANES)
         out_rows = out_0.rearrange("(p j) c -> p j c", j=LANES)
 
         w_window = [sbuf(f"w_window{j}", [P, T], F32) for j in range(LANES)]
-        x_sb = placed_at("x_sb", [P, LANES, R], F32, 0)
+        x_sb = placed_at("x_sb", [P, LANES, R], F32, X_PLACE)
         x2_pair = [sbuf(f"x2_pair{h}", [P, 2, R], F32) for h in range(2)]
         y_sb = sbuf("y_sb", [P, LANES, I], F32)
         us_sb = sbuf("us_sb", [P, LANES], F32)
         wt_sb = sbuf("wt_sb", [P, LANES], F32)
         ts_window = sbuf("ts_window", [P, T], F32)
-
         ts_columns = sbuf("ts_columns", [P, T // P], F32)
+
         nc.sync.dma_start(ts_columns[:], ts[0:1, :].rearrange("o (k c) -> (o k) c", k=P))
         nc.sync.dma_start(w_window[0][:], w_rows[:, 0, :])
         nc.sync.dma_start(offsets[:], offs)
@@ -73,8 +105,7 @@ def tile_attend_gfisher_sq_pl_kernel(tc, xT, wT, us, ts, wt, x2, y, offs, out_0,
         nc.scalar.dma_start(wt_sb[:], wt.rearrange("(s t) o -> s (t o)", t=LANES))
         for j in range(1, LANES):
             nc.sync.dma_start(w_window[j][:], w_rows[:, j, :])
-        nc.sync.dma_start(x_sb[:], x_rows)
-        y_rows = y.rearrange("(s t) i -> s t i", t=LANES)
+        nc.sync.dma_start(x_sb[:], xT.rearrange("(p j) r -> p j r", j=LANES))
         nc.sync.dma_start(x2_pair[0][:], x2_rows[:, 0:2, :])
         for h in range(2):
             nc.sync.dma_start(y_sb[:, 2 * h : 2 * h + 2, :], y_rows[:, 2 * h : 2 * h + 2, :])
@@ -108,19 +139,17 @@ def tile_attend_gfisher_sq_pl_kernel(tc, xT, wT, us, ts, wt, x2, y, offs, out_0,
         nc.vector.tensor_tensor(row_factor[:], us_squared[:], wt_sb[:], MULT)
         factor = []
 
-        def factor_by_lane(half):
-            by_lane = sbuf(f"factor_by_lane{half}", [P, LANES, I // 2], F32)
+        def factor_by_lane(h):
+            by_lane = sbuf(f"factor_by_lane{h}", [P, LANES, HALF], F32)
             for t in range(LANES):
-                squares = ts_squared[:, half * I // 2 : (half + 1) * I // 2]
-                nc.scalar.activation(by_lane[:, t, :], squares, COPY, scale=row_factor[:, t : t + 1])
+                nc.scalar.activation(
+                    by_lane[:, t, :], ts_squared[:, half_slots(h)], COPY, scale=row_factor[:, t : t + 1]
+                )
             return by_lane
 
         def group_factor(grouped, by_lane):
             for c in range(2):
-                nc.scalar.copy(
-                    grouped[:, c].rearrange("p (q i) t -> p q t i", i=4),
-                    by_lane[:, :, slots(c)].rearrange("p t (q i) -> p q t i", i=4),
-                )
+                interleave(nc.scalar.copy, grouped[:, c], by_lane[:, :, slots(c)])
                 factor.append(grouped[:, c])
 
         group_factor(sbuf("factor0", [P, 2, SLOT_CHUNK, LANES], F32), factor_by_lane(0))
@@ -131,15 +160,12 @@ def tile_attend_gfisher_sq_pl_kernel(tc, xT, wT, us, ts, wt, x2, y, offs, out_0,
         nc.vector.tensor_copy(w_grouped[:, :, 0], w_first[:])
         nc.vector.tensor_copy(w_grouped[:, :, 2], w_window[2][:].indirect(offsets[:]))
         for h in range(2):
-            entries = offsets[:, h * I // 32 : (h + 1) * I // 32]
-            nc.vector.tensor_copy(w_grouped[:, h * I // 2 : (h + 1) * I // 2, 3], w_window[3][:].indirect(entries))
+            nc.vector.tensor_copy(w_grouped[:, half_slots(h), 3], w_window[3][:].indirect(offsets[:, half_entries(h)]))
         w_codes = sbuf("w_codes", [P, I], U32)
         w_scales = sbuf("w_scales", [P, I], U8)
         for h in range(2):
-            cols = slice(h * I // 2, (h + 1) * I // 2)
-            nc.vector.quantize_mx(
-                w_codes[:, cols].bitcast(E4M3X4), w_scales[:, cols], w_grouped[:, cols].rearrange("p i j -> p (i j)")
-            )
+            values = w_grouped[:, half_slots(h)].rearrange("p i j -> p (i j)")
+            nc.vector.quantize_mx(w_codes[:, half_slots(h)].bitcast(E4M3X4), w_scales[:, half_slots(h)], values)
 
         x_grouped = sbuf("x_grouped", [P, LANES, P, LANES], BF16, on="factor_by_lane0")
 
@@ -149,57 +175,49 @@ def tile_attend_gfisher_sq_pl_kernel(tc, xT, wT, us, ts, wt, x2, y, offs, out_0,
                 x_sb[:].rearrange("p j (s t) -> p s j t", t=LANES)[:, first:end, :, tiles],
             )
 
-        deal_x(nc.vector.tensor_copy, slice(0, 2), 0, 80)
-        deal_x(nc.scalar.copy, slice(0, 2), 80, P)
-        deal_x(nc.vector.tensor_copy, slice(2, 4), 0, 48)
-        deal_x(nc.scalar.copy, slice(2, 4), 48, P)
-        x2_words = placed_at("x2_words", [P, 2, 2, P, 2], BF16, 0)
+        for pair, share in enumerate(VECTOR_DEALS):
+            tiles = slice(2 * pair, 2 * pair + 2)
+            deal_x(nc.vector.tensor_copy, tiles, 0, share)
+            deal_x(nc.scalar.copy, tiles, share, P)
+
+        x2_words = placed_at("x2_words", [P, 2, 2, P, 2], BF16, X_PLACE)
         nc.scalar.copy(x2_words[:], x2_pair[0][:].rearrange("p j (s u e) -> p j u s e", u=2, e=2))
-        group_factor(placed_at("factor1", [P, 2, SLOT_CHUNK, LANES], F32, 2048), late_by_lane)
+        group_factor(placed_at("factor1", [P, 2, SLOT_CHUNK, LANES], F32, X_PLACE + 2 * R * 2), late_by_lane)
+
         x_codes = sbuf("x_codes", [P, LANES, P], U32)
         x_scales = sbuf("x_scales", [P, LANES, P], U8)
-        z = sbuf("z", [P, LANES, I], F32)
-        half = I // 2
-        z_early = {(0, 0): sbuf("z00", [P, half], F32), (0, 1): sbuf("z01", [P, half], F32)}
+        z_rest = sbuf("z_rest", [P, LANES - 1, I], F32)
+        z_first = [sbuf(f"z_first{h}", [P, HALF], F32) for h in range(2)]
         scores = []
         for t in range(LANES):
-            nc.vector.quantize_mx(
-                x_codes[:, t, :].bitcast(E4M3X4), x_scales[:, t, :], x_grouped[:, t, :, :].rearrange("p s j -> p (s j)")
-            )
+            values = x_grouped[:, t, :, :].rearrange("p s j -> p (s j)")
+            nc.vector.quantize_mx(x_codes[:, t, :].bitcast(E4M3X4), x_scales[:, t, :], values)
             bank = sums.tile([P, I], F32, tag=f"sum{t}", name=f"scores{t}")
-            nc.tensor.matmul_mx(
-                bank[:],
-                lhsT=x_codes[:, t, :].bitcast(E4M3X4),
-                lhsT_scale=x_scales[:, t, :],
-                rhs=w_codes[:].bitcast(E4M3X4),
-                rhs_scale=w_scales[:],
-                start=True,
-                stop=True,
-            )
+            product(bank, x_codes[:, t, :].bitcast(E4M3X4), x_scales[:, t, :], w_codes[:].bitcast(E4M3X4), w_scales[:])
             scores.append(bank)
-        for t in range(LANES):
-            if t in (1, 2):
-                nc.vector.scalar_tensor_tensor(z[:, t, :], scores[t][:], us_sb[:, t : t + 1], ts_all[:], MULT, MULT)
-                continue
-            for h in (1, 0) if t == 1 else (0, 1):
-                cols = slice(h * half, (h + 1) * half)
-                target = z_early[t, h][:] if (t, h) in z_early else z[:, t, cols]
-                nc.vector.scalar_tensor_tensor(
-                    target, scores[t][:, cols], us_sb[:, t : t + 1], ts_all[:, cols], MULT, MULT
-                )
+
+        def scale_scores(target, t, cols):
+            nc.vector.scalar_tensor_tensor(target, scores[t][:, cols], us_sb[:, t : t + 1], ts_all[:, cols], MULT, MULT)
+
+        for h in range(2):
+            scale_scores(z_first[h][:], 0, half_slots(h))
+        for t in range(1, LANES - 1):
+            scale_scores(z_rest[:, t - 1, :], t, slice(0, I))
+        for h in range(2):
+            scale_scores(z_rest[:, LANES - 2, half_slots(h)], LANES - 1, half_slots(h))
 
         words = x2_words[:].rearrange("p j u s e -> p (j u) (s e)").bitcast(F32)
         word_bank = sums.tile([P, 2, 2, P], F32, tag="sum0", name="x2_turned_words")
         for j in range(2):
             for u in range(2):
                 nc.tensor.transpose(word_bank[:, j, u, :], words[:, 2 * j + u, :], identity[:])
-        x2_banks = []
-        for j in range(2):
-            bank = sums.tile([P, LANES, P], F32, tag=f"sum{3 * j}", name=f"x2_turned{j}")
+        rest_banks = []
+        for j, tag in enumerate(["sum0", f"sum{LANES - 1}"]):
+            bank = sums.tile([P, LANES, P], F32, tag=tag, name=f"x2_turned{j}")
             rows = x2_pair[1][:, j, :].rearrange("p (s t) -> p t s", t=LANES)
             for t in range(LANES):
                 nc.tensor.transpose(bank[:, t, :], rows[:, t, :], identity[:])
-            x2_banks.append(bank)
+            rest_banks.append(bank)
         first_grouped = sbuf("first_grouped", [P, 2 * P * LANES], BF16)
         nc.scalar.copy(
             first_grouped[:].bitcast(F32).rearrange("s (j p u) -> s j p u", j=2, u=2),
@@ -210,162 +228,145 @@ def tile_attend_gfisher_sq_pl_kernel(tc, xT, wT, us, ts, wt, x2, y, offs, out_0,
         x2_codes = [first_codes[:, :P], first_codes[:, P:]]
         x2_scales = [first_scales[:, :P], first_scales[:, P:]]
 
-        error = [sbuf(f"error{h}", [P, LANES, I // 2], F32) for h in range(2)]
-        gpsimd_tiles = [1, 1]
-        for t in range(2):
-            for h in range(2):
-                if t < gpsimd_tiles[h]:
-                    cols = slice(h * I // 2, (h + 1) * I // 2)
-                    nc.gpsimd.tensor_tensor(error[h][:, t, :], z_early[t, h][:], y_sb[:, t, cols], SUBTRACT)
-        squared = [sbuf(f"squared{c}", [P, SLOT_CHUNK, LANES], F32) for c in range(SLOT_CHUNKS)]
+        error = [sbuf(f"error{h}", [P, LANES, HALF], F32) for h in range(2)]
+        for h in range(2):
+            nc.gpsimd.tensor_tensor(error[h][:, 0, :], z_first[h][:], y_sb[:, 0, half_slots(h)], SUBTRACT)
+        squared = [[(sbuf(f"squared{c}", [P, SLOT_CHUNK, LANES], F32), slice(0, SLOT_CHUNK))] for c in range(3)]
+        cut = SLOT_CHUNK - LAST_SLOTS
+        squared.append(
+            [
+                (sbuf("squared3", [P, cut, LANES], F32), slice(0, cut)),
+                (sbuf("squared_last", [P, LAST_SLOTS, LANES], F32), slice(cut, SLOT_CHUNK)),
+            ]
+        )
         g_first = sbuf("g_first", [P, 2, SLOT_CHUNK, LANES], BF16)
         g_grouped = [g_first[:, 0], g_first[:, 1]]
-        padded_codes = sbuf("padded_codes", [P, half + I], U32)
-        padded_scales = sbuf("padded_scales", [P, half + I], U8)
-        nc.gpsimd.memset(padded_codes[:, :half], 0)
-        nc.gpsimd.memset(padded_scales[:, :half], 0)
-        g_codes = padded_codes[:, half:]
-        g_scales = padded_scales[:, half:]
+        padded_codes = sbuf("padded_codes", [P, HALF + I], U32)
+        padded_scales = sbuf("padded_scales", [P, HALF + I], U8)
+        nc.gpsimd.memset(padded_codes[:, :HALF], 0)
+        nc.gpsimd.memset(padded_scales[:, :HALF], 0)
+        g_codes = padded_codes[:, HALF:]
+        g_scales = padded_scales[:, HALF:]
 
-        def subtract_targets(c):
-            first = gpsimd_tiles[c // 2]
+        def subtract_and_square(c):
             errors = error[c // 2][:, :, slots(c % 2)]
-            nc.vector.tensor_tensor(errors[:, first:], z[:, first:, slots(c)], y_sb[:, first:, slots(c)], SUBTRACT)
-            nc.scalar.activation(
-                squared[c][:].rearrange("p (q i) t -> p q t i", i=4),
-                errors.rearrange("p t (q i) -> p q t i", i=4),
-                SQUARE,
-            )
+            nc.vector.tensor_tensor(errors[:, 1:], z_rest[:, :, slots(c)], y_sb[:, 1:, slots(c)], SUBTRACT)
+            for squares, part in squared[c]:
+                interleave(nc.scalar.activation, squares[:], errors[:, :, part], SQUARE)
 
         def weigh(engine, c):
-            engine.tensor_tensor(g_grouped[c], squared[c][:], factor[c], MULT)
+            for squares, part in squared[c]:
+                engine.tensor_tensor(g_grouped[c][:, part], squares[:], factor[c][:, part], MULT)
 
-        def quantise_g(first, end, values):
-            cols = slice(first * SLOT_CHUNK, end * SLOT_CHUNK)
+        def quantise_g(cols, values):
             nc.vector.quantize_mx(g_codes[:, cols].bitcast(E5M2X4), g_scales[:, cols], values)
-
-        subtract_targets(0)
-        subtract_targets(1)
-        subtract_targets(2)
-        weigh(nc.vector, 0)
-        subtract_targets(3)
-        weigh(nc.vector, 1)
-        nc.vector.quantize_mx(first_codes[:].bitcast(E4M3X4), first_scales[:], first_grouped[:])
-        quantise_g(0, 2, g_first[:].rearrange("p c i t -> p (c i t)"))
 
         def second_product(j, codes, scales):
             bank = turns.tile([P, I], F32, tag="turn", name="fisher_sum")
-            nc.tensor.matmul_mx(
-                bank[:],
-                lhsT=x2_codes[j].bitcast(E4M3X4),
-                lhsT_scale=x2_scales[j],
-                rhs=codes.bitcast(E5M2X4),
-                rhs_scale=scales,
-                start=True,
-                stop=True,
-            )
+            product(bank, x2_codes[j].bitcast(E4M3X4), x2_scales[j], codes.bitcast(E5M2X4), scales)
             return bank
-
-        early_sums = [second_product(j, padded_codes[:, :I], padded_scales[:, :I]) for j in range(2)]
-        rest_codes = placed_at("rest_codes", [P, 32, P], U32, PAIRS_PLACE)[:, 0:2]
-        rest_scales = sbuf("rest_scales", [P, 2, P], U8)
-        x2_codes.extend([rest_codes[:, 0], rest_codes[:, 1]])
-        x2_scales.extend([rest_scales[:, 0], rest_scales[:, 1]])
-
-        def group_rest(j, freed):
-            grouped = sbuf(f"rest_grouped{j}", [P, P, LANES], BF16, on=freed)
-            nc.scalar.copy(grouped[:], x2_banks[j][:].rearrange("s t p -> s p t"))
-            return grouped[:].rearrange("s p t -> s (p t)")
-
-        def quantise_rest(j, grouped):
-            nc.vector.quantize_mx(rest_codes[:, j].bitcast(E4M3X4), rest_scales[:, j], grouped)
 
         def leave_bank(name, bank, cols, on=None):
             values = sbuf(name, [P, cols.stop - cols.start], F32, on=on)
             nc.scalar.copy(values[:], bank[:, cols])
             return values
 
-        upper = slice(half, I)
-        rest_grouped = group_rest(0, "error1")
-        g_grouped.append(sbuf("g_third", [P, SLOT_CHUNK, LANES], BF16)[:])
+        subtract_and_square(0)
+        subtract_and_square(1)
+        subtract_and_square(2)
+        weigh(nc.vector, 0)
+        subtract_and_square(3)
+        weigh(nc.vector, 1)
+        nc.vector.quantize_mx(first_codes[:].bitcast(E4M3X4), first_scales[:], first_grouped[:])
+        quantise_g(half_slots(0), g_first[:].rearrange("p c i t -> p (c i t)"))
+        early_sums = [second_product(j, padded_codes[:, :I], padded_scales[:, :I]) for j in range(2)]
+
+        rest_codes = placed_at("rest_codes", [P, T * LANES * 2 // (P * 4), P], U32, PAIRS_PLACE)[:, 0:2]
+        rest_scales = sbuf("rest_scales", [P, 2, P], U8)
+        x2_codes.extend([rest_codes[:, 0], rest_codes[:, 1]])
+        x2_scales.extend([rest_scales[:, 0], rest_scales[:, 1]])
+
+        def group_rest(j, grouped):
+            nc.scalar.copy(grouped[:], rest_banks[j][:].rearrange("s t p -> s p t"))
+            return grouped[:].rearrange("s p t -> s (p t)")
+
+        def quantise_rest(j, grouped):
+            nc.vector.quantize_mx(rest_codes[:, j].bitcast(E4M3X4), rest_scales[:, j], grouped)
+
+        rest_grouped = group_rest(0, sbuf("rest_grouped0", [P, P, LANES], BF16, on="error1"))
+        g_grouped.append(placed_at("g_third", [P, SLOT_CHUNK, LANES], BF16, G_PLACE + G_BYTES // 2)[:])
         weigh(nc.vector, 2)
         quantise_rest(0, rest_grouped)
-        quantise_g(2, 3, g_grouped[2].rearrange("p i t -> p (i t)"))
-        early = [leave_bank("early0", early_sums[0], upper, on="squared2")]
-        g_grouped.append(sbuf("g_fourth", [P, SLOT_CHUNK, LANES], BF16, on="g_third")[:])
+        quantise_g(slots(2), g_grouped[2].rearrange("p i t -> p (i t)"))
+        early = [leave_bank("early0", early_sums[0], half_slots(1), on="squared2")]
+        g_grouped.append(placed_at("g_fourth", [P, SLOT_CHUNK, LANES], BF16, G_PLACE)[:])
+        rest_grouped = group_rest(1, placed_at("rest_grouped1", [P, P, LANES], BF16, G_PLACE + G_BYTES))
         weigh(nc.gpsimd, 3)
-        early.append(leave_bank("early1", early_sums[1], upper, on="squared3"))
-        quantise_g(3, 4, g_grouped[3].rearrange("p i t -> p (i t)"))
-        rest_grouped = group_rest(1, "g_third")
-        late = [leave_bank(f"late{j}", second_product(j, g_codes, g_scales), upper) for j in range(2)]
+        early.append(leave_bank("early1", early_sums[1], half_slots(1), on="squared3"))
+        quantise_g(slots(3), g_grouped[3].rearrange("p i t -> p (i t)"))
+        late = [leave_bank(f"late{j}", second_product(j, g_codes, g_scales), half_slots(1)) for j in range(2)]
         quantise_rest(1, rest_grouped)
         whole = [leave_bank(f"fisher{j}", second_product(j, g_codes, g_scales), slice(0, I)) for j in range(2, LANES)]
-        first_entries, last_entries = slice(0, half // 16), slice(half // 16, I // 16)
         for j in range(2):
-            nc.vector.tensor_copy(out_window[j][:].indirect(offsets[:, first_entries]), early[j][:])
-        pieces = [(late[0], last_entries), (late[1], last_entries)] + [(f, slice(0, I // 16)) for f in whole]
+            nc.vector.tensor_copy(out_window[j][:].indirect(offsets[:, half_entries(0)]), early[j][:])
+        last_pieces = [(values, half_entries(1)) for values in late] + [(values, slice(0, I // 16)) for values in whole]
 
         out_pairs = placed_at("out_pairs", [P, T * LANES], BF16, PAIRS_PLACE)
         pair_lanes = out_pairs[:].rearrange("p (u c e) -> p u c e", u=2, e=2)
         pair_words = out_pairs[:].bitcast(F32).rearrange("p (u c) -> p c u", u=2)
-        out_grouped = [sbuf(f"out_grouped{k}", [P, COL_WIDTHS[k] * LANES], BF16) for k in range(COL_CHUNKS)]
+        out_grouped = [sbuf(f"out_grouped{k}", [P, width * LANES], BF16) for k, width in enumerate(COL_WIDTHS)]
         out_codes = sbuf("out_codes", [P, T], U32)
-        out_scales = sbuf("out_scales", [P, T // 4], U8)
+        out_scales = sbuf("out_scales", [P, SCALE_GROUP], U8)
         words_out = out_1.rearrange("a p c l -> p (a c l)").bitcast(I32)
         scales_out = out_2.rearrange("a q c -> q (a c)").bitcast(I32).rearrange("q (g c) -> g q c", g=4)
 
         def columns(k):
             return slice(COL_STARTS[k], COL_STARTS[k + 1])
 
-        def round_lane(j, cols):
-            nc.scalar.copy(pair_lanes[:, j // 2, cols, j % 2], out_window[j][:, cols])
+        def round_on_gpsimd(rounded, values):
+            nc.gpsimd.tensor_scalar(rounded, values, 1.0, 0.0, MULT, ADD)
 
         def join_pairs(copy, k):
-            copy(
-                out_grouped[k][:].bitcast(F32).rearrange("p (c u) -> p c u", u=2),
-                pair_words[:, columns(k)],
-            )
+            copy(out_grouped[k][:].bitcast(F32).rearrange("p (c u) -> p c u", u=2), pair_words[:, columns(k)])
 
         def quantise_out(k):
-            group, place = divmod(COL_STARTS[k], T // 4)
+            group, place = divmod(COL_STARTS[k], SCALE_GROUP)
             plane = out_scales[4 * group :, place : place + COL_WIDTHS[k]]
             nc.vector.quantize_mx(out_codes[:, columns(k)].bitcast(E4M3X4), plane, out_grouped[k][:])
 
-        def store_words(first, end):
-            cols = slice(COL_STARTS[first], COL_STARTS[end])
-            nc.sync.dma_start(words_out[:, cols], out_codes[:, cols].bitcast(I32))
-
+        paired = VECTOR_JOINED + SCALAR_JOINED
         for j in range(LANES):
-            values, entries = pieces[j]
+            last = j == LANES - 1
+            values, entries = last_pieces[j]
             nc.vector.tensor_copy(out_window[j][:].indirect(offsets[:, entries]), values[:])
-            (nc.scalar if j == LANES - 1 else nc.sync).dma_start(out_rows[:, j, :], out_window[j][:])
-            last = j + 1 == LANES
-            for k in VECTOR_DIRECT + SCALAR_DIRECT:
+            queue = nc.scalar if last else nc.sync
+            queue.dma_start(out_rows[:, j, :], out_window[j][:])
+            for k in DIRECT_CHUNKS:
                 lanes = out_grouped[k][:].rearrange("p (c l) -> p c l", l=LANES)
-                values = out_window[j][:, columns(k)]
+                window_part = out_window[j][:, columns(k)]
                 if last:
-                    if k in VECTOR_DIRECT:
-                        nc.vector.tensor_copy(lanes[:, :, j], values)
-                elif j == 2:
-                    both = values.unsqueeze(2).to_broadcast([P, COL_WIDTHS[k], 2])
-                    nc.gpsimd.tensor_scalar(lanes[:, :, 2:4], both, 1.0, 0.0, MULT, ADD)
+                    nc.vector.tensor_copy(lanes[:, :, j], window_part)
+                elif j == LANES - 2:
+                    round_on_gpsimd(lanes[:, :, j:], window_part.unsqueeze(2).to_broadcast([P, COL_WIDTHS[k], 2]))
                 else:
-                    nc.gpsimd.tensor_scalar(lanes[:, :, j], values, 1.0, 0.0, MULT, ADD)
-            all_paired = slice(COL_STARTS[PAIRED[0]], COL_STARTS[PAIRED[-1] + 1])
-            for cols in [columns(k) for k in PAIRED] if last else [all_paired]:
-                round_lane(j, cols)
-        join_pairs(nc.scalar.copy, PAIRED[-1])
-        for k in SCALAR_DIRECT:
-            lanes = out_grouped[k][:].rearrange("p (c l) -> p c l", l=LANES)
-            nc.scalar.copy(lanes[:, :, LANES - 1], out_window[LANES - 1][:, columns(k)])
+                    round_on_gpsimd(lanes[:, :, j], window_part)
+            scalar_end = T
+            if j < 2:
+                scalar_end = T - GPSIMD_PAIRED
+                round_on_gpsimd(pair_lanes[:, 0, scalar_end:, j], out_window[j][:, scalar_end:])
+            for cols in [columns(k) for k in paired] if last else [slice(COL_STARTS[paired[0]], scalar_end)]:
+                nc.scalar.copy(pair_lanes[:, j // 2, cols, j % 2], out_window[j][:, cols])
+        for k in SCALAR_JOINED:
+            join_pairs(nc.scalar.copy, k)
         stored = 0
-        for k in range(COL_CHUNKS):
-            if k + 1 in PAIRED[:-1]:
+        for k in range(len(COL_WIDTHS)):
+            if k + 1 in VECTOR_JOINED:
                 join_pairs(nc.vector.tensor_copy, k + 1)
             quantise_out(k)
-            if COL_STARTS[k + 1] % (T // 4) == 0 or k == COL_CHUNKS - 3:
-                store_words(stored, k + 1)
-                stored = k + 1
+            done = COL_STARTS[k + 1]
+            if done % SCALE_GROUP == 0 or done == T - SCALE_GROUP // 2:
+                nc.sync.dma_start(words_out[:, stored:done], out_codes[:, stored:done].bitcast(I32))
+                stored = done
         for q in range(4):
             queue = nc.scalar if q % 2 else nc.sync
             queue.dma_start(scales_out[:, 4 * q : 4 * q + 4, :], out_scales[32 * q : 32 * q + 16, :].bitcast(I32))

@@ -27,7 +27,7 @@ HALF = I // 2
 SLOT_CHUNK = 128
 SCALE_GROUP = T // 4
 
-VECTOR_DEALS = [80, 48]
+VECTOR_DEALS = [96, 72]
 LAST_SLOTS = 32
 COL_WIDTHS = [128, 128, 256, 256, 256, 256, 256, 256, 128, 128]
 COL_STARTS = [sum(COL_WIDTHS[:k]) for k in range(len(COL_WIDTHS) + 1)]
@@ -38,8 +38,6 @@ GPSIMD_PAIRED = 384
 
 X_PLACE = 0
 PAIRS_PLACE = X_PLACE + LANES * R * 4
-G_PLACE = PAIRS_PLACE + T * LANES * 2
-G_BYTES = SLOT_CHUNK * LANES * 2
 
 
 def tile_attend_gfisher_sq_pl_kernel(tc, xT, wT, us, ts, wt, x2, y, offs, out_0, out_1, out_2):
@@ -47,8 +45,10 @@ def tile_attend_gfisher_sq_pl_kernel(tc, xT, wT, us, ts, wt, x2, y, offs, out_0,
     with ExitStack() as ctx:
         keep = ctx.enter_context(tc.tile_pool(name="keep", bufs=1))
         placed = ctx.enter_context(tc.tile_pool(name="placed", bufs=1))
-        sums = ctx.enter_context(tc.psum_pool(name="sums", bufs=1))
-        turns = ctx.enter_context(tc.psum_pool(name="turns", bufs=4))
+        banks = ctx.enter_context(tc.psum_pool(name="banks", bufs=1))
+
+        def psum(name, shape, bank):
+            return banks.tile(shape, F32, name=name, tag=f"bank{bank}")
 
         def sbuf(name, shape, dtype, on=None):
             return keep.tile(shape, dtype, name=name, tag=on or name, align_bytes=64)
@@ -74,7 +74,7 @@ def tile_attend_gfisher_sq_pl_kernel(tc, xT, wT, us, ts, wt, x2, y, offs, out_0,
 
         def product(bank, stationary_codes, stationary_scales, moving_codes, moving_scales):
             nc.tensor.matmul_mx(
-                bank[:],
+                bank,
                 lhsT=stationary_codes,
                 lhsT_scale=stationary_scales,
                 rhs=moving_codes,
@@ -91,7 +91,8 @@ def tile_attend_gfisher_sq_pl_kernel(tc, xT, wT, us, ts, wt, x2, y, offs, out_0,
 
         w_window = [sbuf(f"w_window{j}", [P, T], F32) for j in range(LANES)]
         x_sb = placed_at("x_sb", [P, LANES, R], F32, X_PLACE)
-        x2_pair = [sbuf(f"x2_pair{h}", [P, 2, R], F32) for h in range(2)]
+        x2_plane = [sbuf(f"x2_plane{j}", [P, R], F32) for j in range(2)]
+        x2_rest = sbuf("x2_rest", [P, 2, R], F32)
         y_sb = sbuf("y_sb", [P, LANES, I], F32)
         us_sb = sbuf("us_sb", [P, LANES], F32)
         wt_sb = sbuf("wt_sb", [P, LANES], F32)
@@ -106,10 +107,10 @@ def tile_attend_gfisher_sq_pl_kernel(tc, xT, wT, us, ts, wt, x2, y, offs, out_0,
         for j in range(1, LANES):
             nc.sync.dma_start(w_window[j][:], w_rows[:, j, :])
         nc.sync.dma_start(x_sb[:], xT.rearrange("(p j) r -> p j r", j=LANES))
-        nc.sync.dma_start(x2_pair[0][:], x2_rows[:, 0:2, :])
         for h in range(2):
             nc.sync.dma_start(y_sb[:, 2 * h : 2 * h + 2, :], y_rows[:, 2 * h : 2 * h + 2, :])
-        nc.sync.dma_start(x2_pair[1][:], x2_rows[:, 2:4, :])
+            nc.sync.dma_start(x2_plane[h][:], x2_rows[:, h, :])
+        nc.sync.dma_start(x2_rest[:], x2_rows[:, 2:4, :])
 
         identity = sbuf("identity", [P, P], F32)
         make_identity(nc, identity[:])
@@ -120,7 +121,7 @@ def tile_attend_gfisher_sq_pl_kernel(tc, xT, wT, us, ts, wt, x2, y, offs, out_0,
 
         window_by_row = ts_window[:].rearrange("p (k c) -> p k c", k=P)
         for b in range(T // P // 4):
-            bank = turns.tile([P, 4, P], F32, tag="turn", name=f"ts_spread{b}")
+            bank = psum(f"ts_spread{b}", [P, 4, P], 4 + b)
             for c in range(4):
                 column = ts_columns[:, 4 * b + c : 4 * b + c + 1]
                 nc.tensor.transpose(bank[:, c, :], column.to_broadcast([P, P]), identity[:])
@@ -133,27 +134,22 @@ def tile_attend_gfisher_sq_pl_kernel(tc, xT, wT, us, ts, wt, x2, y, offs, out_0,
         nc.vector.tensor_copy(ts_all[:], ts_window[:].indirect(offsets[:]))
         nc.scalar.activation(ts_squared[:], ts_all[:], SQUARE)
 
+        ts_turned = psum("ts_turned", [P, 2, P], 0)
+        for c in range(2):
+            nc.tensor.transpose(ts_turned[:, c, :], ts_all[:, slots(2 + c)], identity[:])
+        ts_by_slot = sbuf("ts_by_slot", [P, 2], F32)
+        nc.scalar.copy(ts_by_slot[:], ts_turned[:, :, 0])
+
         us_squared = sbuf("us_squared", [P, LANES], F32)
         row_factor = sbuf("row_factor", [P, LANES], F32)
         nc.vector.tensor_tensor(us_squared[:], us_sb[:], us_sb[:], MULT)
         nc.vector.tensor_tensor(row_factor[:], us_squared[:], wt_sb[:], MULT)
-        factor = []
-
-        def factor_by_lane(h):
-            by_lane = sbuf(f"factor_by_lane{h}", [P, LANES, HALF], F32)
-            for t in range(LANES):
-                nc.scalar.activation(
-                    by_lane[:, t, :], ts_squared[:, half_slots(h)], COPY, scale=row_factor[:, t : t + 1]
-                )
-            return by_lane
-
-        def group_factor(grouped, by_lane):
-            for c in range(2):
-                interleave(nc.scalar.copy, grouped[:, c], by_lane[:, :, slots(c)])
-                factor.append(grouped[:, c])
-
-        group_factor(sbuf("factor0", [P, 2, SLOT_CHUNK, LANES], F32), factor_by_lane(0))
-        late_by_lane = factor_by_lane(1)
+        by_lane = sbuf("factor_by_lane", [P, LANES, HALF], F32)
+        for t in range(LANES):
+            nc.scalar.activation(by_lane[:, t, :], ts_squared[:, half_slots(0)], COPY, scale=row_factor[:, t : t + 1])
+        factor_first = sbuf("factor_first", [P, 2, SLOT_CHUNK, LANES], F32)
+        for c in range(2):
+            interleave(nc.scalar.copy, factor_first[:, c], by_lane[:, :, slots(c)])
 
         w_grouped = sbuf("w_grouped", [P, I, LANES], BF16, on="ts_window")
         nc.vector.tensor_copy(w_grouped[:, :, 1], w_window[1][:].indirect(offsets[:]))
@@ -167,7 +163,17 @@ def tile_attend_gfisher_sq_pl_kernel(tc, xT, wT, us, ts, wt, x2, y, offs, out_0,
             values = w_grouped[:, half_slots(h)].rearrange("p i j -> p (i j)")
             nc.vector.quantize_mx(w_codes[:, half_slots(h)].bitcast(E4M3X4), w_scales[:, half_slots(h)], values)
 
-        x_grouped = sbuf("x_grouped", [P, LANES, P, LANES], BF16, on="factor_by_lane0")
+        factor_second = sbuf("factor_second", [P, 2, SLOT_CHUNK, LANES], F32, on="w_first")
+        for c in range(2):
+            nc.gpsimd.tensor_tensor(
+                factor_second[:, c],
+                ts_squared[:, slots(2 + c)].unsqueeze(2).to_broadcast([P, SLOT_CHUNK, LANES]),
+                row_factor[:].unsqueeze(1).to_broadcast([P, SLOT_CHUNK, LANES]),
+                MULT,
+            )
+        factor = [factor_first[:, 0], factor_first[:, 1], factor_second[:, 0], factor_second[:, 1]]
+
+        x_grouped = sbuf("x_grouped", [P, LANES, P, LANES], BF16, on="factor_by_lane")
 
         def deal_x(copy, tiles, first, end):
             copy(
@@ -180,57 +186,76 @@ def tile_attend_gfisher_sq_pl_kernel(tc, xT, wT, us, ts, wt, x2, y, offs, out_0,
             deal_x(nc.vector.tensor_copy, tiles, 0, share)
             deal_x(nc.scalar.copy, tiles, share, P)
 
-        x2_words = placed_at("x2_words", [P, 2, 2, P, 2], BF16, X_PLACE)
-        nc.scalar.copy(x2_words[:], x2_pair[0][:].rearrange("p j (s u e) -> p j u s e", u=2, e=2))
-        group_factor(placed_at("factor1", [P, 2, SLOT_CHUNK, LANES], F32, X_PLACE + 2 * R * 2), late_by_lane)
+        x2_words = placed_at("x2_words", [P, 2, P, 2], BF16, X_PLACE)
+        nc.scalar.copy(
+            x2_words[:].rearrange("p u s e -> p s u e"), x2_plane[0][:].rearrange("p (s u e) -> p s u e", u=2, e=2)
+        )
 
         x_codes = sbuf("x_codes", [P, LANES, P], U32)
         x_scales = sbuf("x_scales", [P, LANES, P], U8)
-        z_rest = sbuf("z_rest", [P, LANES - 1, I], F32)
-        z_first = [sbuf(f"z_first{h}", [P, HALF], F32) for h in range(2)]
+        z_rest = sbuf("z_rest", [P, LANES - 1, HALF], F32)
+        z_first = sbuf("z_first", [P, HALF], F32)
         scores = []
         for t in range(LANES):
             values = x_grouped[:, t, :, :].rearrange("p s j -> p (s j)")
             nc.vector.quantize_mx(x_codes[:, t, :].bitcast(E4M3X4), x_scales[:, t, :], values)
-            bank = sums.tile([P, I], F32, tag=f"sum{t}", name=f"scores{t}")
-            product(bank, x_codes[:, t, :].bitcast(E4M3X4), x_scales[:, t, :], w_codes[:].bitcast(E4M3X4), w_scales[:])
+            bank = psum(f"scores{t}", [P, HALF], t)
+            product(
+                bank[:],
+                x_codes[:, t, :].bitcast(E4M3X4),
+                x_scales[:, t, :],
+                w_codes[:, half_slots(0)].bitcast(E4M3X4),
+                w_scales[:, half_slots(0)],
+            )
             scores.append(bank)
+        by_slot = []
+        for c in range(2):
+            bank = psum(f"scores_by_slot{c}", [P, R], 4 + c)
+            product(
+                bank[:],
+                w_codes[:, slots(2 + c)].bitcast(E4M3X4),
+                w_scales[:, slots(2 + c)],
+                x_codes[:].rearrange("p t s -> p (t s)").bitcast(E4M3X4),
+                x_scales[:].rearrange("p t s -> p (t s)"),
+            )
+            scaled = sbuf(f"scaled_by_slot{c}", [P, LANES, P], F32)
+            nc.scalar.activation(
+                scaled[:].rearrange("i t s -> i (t s)"), bank[:], COPY, scale=ts_by_slot[:, c : c + 1]
+            )
+            by_slot.append(scaled)
 
         def scale_scores(target, t, cols):
             nc.vector.scalar_tensor_tensor(target, scores[t][:, cols], us_sb[:, t : t + 1], ts_all[:, cols], MULT, MULT)
 
-        for h in range(2):
-            scale_scores(z_first[h][:], 0, half_slots(h))
+        scale_scores(z_first[:], 0, half_slots(0))
         for t in range(1, LANES - 1):
-            scale_scores(z_rest[:, t - 1, :], t, slice(0, I))
-        for h in range(2):
-            scale_scores(z_rest[:, LANES - 2, half_slots(h)], LANES - 1, half_slots(h))
+            scale_scores(z_rest[:, t - 1, :], t, half_slots(0))
+        for c in range(2):
+            scale_scores(z_rest[:, LANES - 2, slots(c)], LANES - 1, slots(c))
 
-        words = x2_words[:].rearrange("p j u s e -> p (j u) (s e)").bitcast(F32)
-        word_bank = sums.tile([P, 2, 2, P], F32, tag="sum0", name="x2_turned_words")
-        for j in range(2):
-            for u in range(2):
-                nc.tensor.transpose(word_bank[:, j, u, :], words[:, 2 * j + u, :], identity[:])
-        rest_banks = []
-        for j, tag in enumerate(["sum0", f"sum{LANES - 1}"]):
-            bank = sums.tile([P, LANES, P], F32, tag=tag, name=f"x2_turned{j}")
-            rows = x2_pair[1][:, j, :].rearrange("p (s t) -> p t s", t=LANES)
+        def turn_back(c, bank):
+            turned = psum(f"turned_back{c}", [P, LANES, SLOT_CHUNK], bank)
             for t in range(LANES):
-                nc.tensor.transpose(bank[:, t, :], rows[:, t, :], identity[:])
-            rest_banks.append(bank)
-        first_grouped = sbuf("first_grouped", [P, 2 * P * LANES], BF16)
-        nc.scalar.copy(
-            first_grouped[:].bitcast(F32).rearrange("s (j p u) -> s j p u", j=2, u=2),
-            word_bank[:].rearrange("s j u p -> s j p u"),
-        )
-        first_codes = sbuf("first_codes", [P, 2 * P], U32)
-        first_scales = sbuf("first_scales", [P, 2 * P], U8)
-        x2_codes = [first_codes[:, :P], first_codes[:, P:]]
-        x2_scales = [first_scales[:, :P], first_scales[:, P:]]
+                nc.tensor.transpose(turned[:, t, :], by_slot[c][:, t, :], identity[:])
+            return turned
 
-        error = [sbuf(f"error{h}", [P, LANES, HALF], F32) for h in range(2)]
-        for h in range(2):
-            nc.gpsimd.tensor_tensor(error[h][:, 0, :], z_first[h][:], y_sb[:, 0, half_slots(h)], SUBTRACT)
+        def turn_x2(name, plane, bank):
+            turned = psum(name, [P, LANES, P], bank)
+            rows = plane.rearrange("p (s t) -> p t s", t=LANES)
+            for t in range(LANES):
+                nc.tensor.transpose(turned[:, t, :], rows[:, t, :], identity[:])
+            return turned
+
+        turned_back = [turn_back(0, 7)]
+        words = x2_words[:].rearrange("p u s e -> p u (s e)").bitcast(F32)
+        word_bank = psum("x2_turned_words", [P, 2, P], 4)
+        for u in range(2):
+            nc.tensor.transpose(word_bank[:, u, :], words[:, u, :], identity[:])
+        turned_back.append(turn_back(1, 0))
+        x2_turned = [None, turn_x2("x2_turned1", x2_plane[1][:], 5)]
+
+        error_first = sbuf("error_first", [P, LANES, HALF], F32)
+        nc.gpsimd.tensor_tensor(error_first[:, 0, :], z_first[:], y_sb[:, 0, half_slots(0)], SUBTRACT)
         squared = [[(sbuf(f"squared{c}", [P, SLOT_CHUNK, LANES], F32), slice(0, SLOT_CHUNK))] for c in range(3)]
         cut = SLOT_CHUNK - LAST_SLOTS
         squared.append(
@@ -248,11 +273,22 @@ def tile_attend_gfisher_sq_pl_kernel(tc, xT, wT, us, ts, wt, x2, y, offs, out_0,
         g_codes = padded_codes[:, HALF:]
         g_scales = padded_scales[:, HALF:]
 
-        def subtract_and_square(c):
-            errors = error[c // 2][:, :, slots(c % 2)]
-            nc.vector.tensor_tensor(errors[:, 1:], z_rest[:, :, slots(c)], y_sb[:, 1:, slots(c)], SUBTRACT)
+        def square(c, errors):
             for squares, part in squared[c]:
                 interleave(nc.scalar.activation, squares[:], errors[:, :, part], SQUARE)
+
+        def subtract(c):
+            errors = error_first[:, :, slots(c)]
+            nc.vector.tensor_tensor(errors[:, 1:], z_rest[:, :, slots(c)], y_sb[:, 1:, slots(c)], SUBTRACT)
+            return errors
+
+        def scale_and_subtract(c, on=None):
+            errors = sbuf(f"error{c}", [P, LANES, SLOT_CHUNK], F32, on=on)
+            for t in range(LANES):
+                nc.vector.scalar_tensor_tensor(
+                    errors[:, t, :], turned_back[c - 2][:, t, :], us_sb[:, t : t + 1], y_sb[:, t, slots(c)], MULT, SUBTRACT
+                )
+            return errors[:]
 
         def weigh(engine, c):
             for squares, part in squared[c]:
@@ -261,54 +297,75 @@ def tile_attend_gfisher_sq_pl_kernel(tc, xT, wT, us, ts, wt, x2, y, offs, out_0,
         def quantise_g(cols, values):
             nc.vector.quantize_mx(g_codes[:, cols].bitcast(E5M2X4), g_scales[:, cols], values)
 
-        def second_product(j, codes, scales):
-            bank = turns.tile([P, I], F32, tag="turn", name="fisher_sum")
-            product(bank, x2_codes[j].bitcast(E4M3X4), x2_scales[j], codes.bitcast(E5M2X4), scales)
-            return bank
+        def second_product(name, j, codes, scales, bank):
+            sums = psum(name, [P, I], bank)
+            product(sums[:], x2_codes[j].bitcast(E4M3X4), x2_scales[j], codes.bitcast(E5M2X4), scales)
+            return sums
 
         def leave_bank(name, bank, cols, on=None):
             values = sbuf(name, [P, cols.stop - cols.start], F32, on=on)
             nc.scalar.copy(values[:], bank[:, cols])
             return values
 
-        subtract_and_square(0)
-        subtract_and_square(1)
-        subtract_and_square(2)
+        x2_grouped = [sbuf(f"x2_grouped{j}", [P, P * LANES], BF16) for j in range(2)]
+        first_codes = [sbuf(f"x2_codes{j}", [P, P], U32) for j in range(2)]
+        first_scales = [sbuf(f"x2_scales{j}", [P, P], U8) for j in range(2)]
+        x2_codes = [codes[:] for codes in first_codes]
+        x2_scales = [scales[:] for scales in first_scales]
+
+        def quantise_x2(j):
+            nc.vector.quantize_mx(x2_codes[j].bitcast(E4M3X4), x2_scales[j], x2_grouped[j][:])
+
+        square(0, subtract(0))
+        square(1, subtract(1))
+        nc.scalar.copy(
+            x2_grouped[0][:].bitcast(F32).rearrange("s (p u) -> s p u", u=2), word_bank[:].rearrange("s u p -> s p u")
+        )
+        square(2, scale_and_subtract(2))
+        nc.scalar.copy(
+            x2_grouped[1][:].rearrange("s (p t) -> s p t", t=LANES), x2_turned[1][:].rearrange("s t p -> s p t")
+        )
         weigh(nc.vector, 0)
-        subtract_and_square(3)
         weigh(nc.vector, 1)
-        nc.vector.quantize_mx(first_codes[:].bitcast(E4M3X4), first_scales[:], first_grouped[:])
+        quantise_x2(0)
         quantise_g(half_slots(0), g_first[:].rearrange("p c i t -> p (c i t)"))
-        early_sums = [second_product(j, padded_codes[:, :I], padded_scales[:, :I]) for j in range(2)]
+        early_sums = [second_product("early_sum0", 0, padded_codes[:, :I], padded_scales[:, :I], 2)]
+        quantise_x2(1)
+        early_sums.append(second_product("early_sum1", 1, padded_codes[:, :I], padded_scales[:, :I], 3))
+        last_errors = scale_and_subtract(3, on="squared1")
+        early = [leave_bank("early0", early_sums[0], half_slots(1), on="x2_grouped1")]
+        square(3, last_errors)
+        g_second = sbuf("g_second", [P, 2, SLOT_CHUNK, LANES], BF16, on="g_first")
+        g_grouped.extend([g_second[:, 0], g_second[:, 1]])
+        weigh(nc.gpsimd, 2)
+        weigh(nc.gpsimd, 3)
+        early.append(leave_bank("early1", early_sums[1], half_slots(1), on="squared3"))
+        x2_turned.append(turn_x2("x2_turned2", x2_rest[:, 0, :], 0))
+        x2_turned.append(turn_x2("x2_turned3", x2_rest[:, 1, :], 2))
+        nc.vector.tensor_copy(out_window[0][:].indirect(offsets[:, half_entries(0)]), early[0][:])
+        quantise_g(half_slots(1), g_second[:].rearrange("p c i t -> p (c i t)"))
+        nc.vector.tensor_copy(out_window[1][:].indirect(offsets[:, half_entries(0)]), early[1][:])
 
         rest_codes = placed_at("rest_codes", [P, T * LANES * 2 // (P * 4), P], U32, PAIRS_PLACE)[:, 0:2]
         rest_scales = sbuf("rest_scales", [P, 2, P], U8)
         x2_codes.extend([rest_codes[:, 0], rest_codes[:, 1]])
         x2_scales.extend([rest_scales[:, 0], rest_scales[:, 1]])
-
-        def group_rest(j, grouped):
-            nc.scalar.copy(grouped[:], rest_banks[j][:].rearrange("s t p -> s p t"))
-            return grouped[:].rearrange("s p t -> s (p t)")
-
-        def quantise_rest(j, grouped):
-            nc.vector.quantize_mx(rest_codes[:, j].bitcast(E4M3X4), rest_scales[:, j], grouped)
-
-        rest_grouped = group_rest(0, sbuf("rest_grouped0", [P, P, LANES], BF16, on="error1"))
-        g_grouped.append(placed_at("g_third", [P, SLOT_CHUNK, LANES], BF16, G_PLACE + G_BYTES // 2)[:])
-        weigh(nc.vector, 2)
-        quantise_rest(0, rest_grouped)
-        quantise_g(slots(2), g_grouped[2].rearrange("p i t -> p (i t)"))
-        early = [leave_bank("early0", early_sums[0], half_slots(1), on="squared2")]
-        g_grouped.append(placed_at("g_fourth", [P, SLOT_CHUNK, LANES], BF16, G_PLACE)[:])
-        rest_grouped = group_rest(1, placed_at("rest_grouped1", [P, P, LANES], BF16, G_PLACE + G_BYTES))
-        weigh(nc.gpsimd, 3)
-        early.append(leave_bank("early1", early_sums[1], half_slots(1), on="squared3"))
-        quantise_g(slots(3), g_grouped[3].rearrange("p i t -> p (i t)"))
-        late = [leave_bank(f"late{j}", second_product(j, g_codes, g_scales), half_slots(1)) for j in range(2)]
-        quantise_rest(1, rest_grouped)
-        whole = [leave_bank(f"fisher{j}", second_product(j, g_codes, g_scales), slice(0, I)) for j in range(2, LANES)]
+        rest_grouped = sbuf("rest_grouped", [P, 2, P, LANES], BF16, on="g_first")
         for j in range(2):
-            nc.vector.tensor_copy(out_window[j][:].indirect(offsets[:, half_entries(0)]), early[j][:])
+            nc.scalar.copy(rest_grouped[:, j], x2_turned[2 + j][:].rearrange("s t p -> s p t"))
+        late = [
+            leave_bank(f"late{j}", second_product(f"late_sum{j}", j, g_codes, g_scales, bank), half_slots(1))
+            for j, bank in enumerate([1, 6])
+        ]
+        nc.vector.quantize_mx(
+            rest_codes.rearrange("s j p -> s (j p)").bitcast(E4M3X4),
+            rest_scales[:].rearrange("s j p -> s (j p)"),
+            rest_grouped[:].rearrange("s j p t -> s (j p t)"),
+        )
+        whole = [
+            leave_bank(f"fisher{j}", second_product(f"whole_sum{j}", j, g_codes, g_scales, bank), slice(0, I))
+            for j, bank in [(2, 4), (3, 7)]
+        ]
         last_pieces = [(values, half_entries(1)) for values in late] + [(values, slice(0, I // 16)) for values in whole]
 
         out_pairs = placed_at("out_pairs", [P, T * LANES], BF16, PAIRS_PLACE)

@@ -22,6 +22,7 @@ SQUARE = mybir.ActivationFunctionType.Square
 
 P = 128
 LANES = 4
+BANK_BYTES = 2048
 LINE = 4
 HALF = I // 2
 SLOT_CHUNK = 128
@@ -29,6 +30,7 @@ SCALE_GROUP = T // 4
 
 VECTOR_DEALS = [96, 72]
 LAST_SLOTS = 32
+GPSIMD_WEIGHS = 96
 COL_WIDTHS = [128, 128, 256, 256, 256, 256, 256, 256, 128, 128]
 COL_STARTS = [sum(COL_WIDTHS[:k]) for k in range(len(COL_WIDTHS) + 1)]
 DIRECT_CHUNKS = [0, 1]
@@ -48,7 +50,7 @@ def tile_attend_gfisher_sq_pl_kernel(tc, xT, wT, us, ts, wt, x2, y, offs, out_0,
         banks = ctx.enter_context(tc.psum_pool(name="banks", bufs=1))
 
         def psum(name, shape, bank):
-            return banks.tile(shape, F32, name=name, tag=f"bank{bank}")
+            return banks.tile(shape, F32, name=name, offset=bank * BANK_BYTES)
 
         def sbuf(name, shape, dtype, on=None):
             return keep.tile(shape, dtype, name=name, tag=on or name, align_bytes=64)
@@ -107,9 +109,10 @@ def tile_attend_gfisher_sq_pl_kernel(tc, xT, wT, us, ts, wt, x2, y, offs, out_0,
         for j in range(1, LANES):
             nc.sync.dma_start(w_window[j][:], w_rows[:, j, :])
         nc.sync.dma_start(x_sb[:], xT.rearrange("(p j) r -> p j r", j=LANES))
-        for h in range(2):
-            nc.sync.dma_start(y_sb[:, 2 * h : 2 * h + 2, :], y_rows[:, 2 * h : 2 * h + 2, :])
-            nc.sync.dma_start(x2_plane[h][:], x2_rows[:, h, :])
+        nc.sync.dma_start(y_sb[:, 0:2, :], y_rows[:, 0:2, :])
+        for j in range(2):
+            nc.sync.dma_start(x2_plane[j][:], x2_rows[:, j, :])
+        nc.sync.dma_start(y_sb[:, 2:4, :], y_rows[:, 2:4, :])
         nc.sync.dma_start(x2_rest[:], x2_rows[:, 2:4, :])
 
         identity = sbuf("identity", [P, P], F32)
@@ -127,16 +130,19 @@ def tile_attend_gfisher_sq_pl_kernel(tc, xT, wT, us, ts, wt, x2, y, offs, out_0,
                 nc.tensor.transpose(bank[:, c, :], column.to_broadcast([P, P]), identity[:])
             copy = nc.scalar.copy if b % 2 else nc.vector.tensor_copy
             copy(window_by_row[:, :, 4 * b : 4 * b + 4], bank[:].rearrange("p c k -> p k c"))
-        w_first = sbuf("w_first", [P, I], BF16)
-        nc.vector.tensor_copy(w_first[:], w_window[0][:].indirect(offsets[:]))
-        ts_all = sbuf("ts_all", [P, I], F32)
-        ts_squared = sbuf("ts_squared", [P, I], F32)
-        nc.vector.tensor_copy(ts_all[:], ts_window[:].indirect(offsets[:]))
-        nc.scalar.activation(ts_squared[:], ts_all[:], SQUARE)
+        w_pair = sbuf("w_pair", [P, 2, I], BF16)
+        nc.vector.tensor_copy(w_pair[:, 0], w_window[0][:].indirect(offsets[:]))
+        ts_first = sbuf("ts_first", [P, HALF], F32)
+        ts_second = w_pair[:, 1].bitcast(F32)
+        ts_squared = [sbuf(f"ts_squared{h}", [P, HALF], F32) for h in range(2)]
+        for h, values in [(1, ts_second), (0, ts_first[:])]:
+            nc.vector.tensor_copy(values, ts_window[:].indirect(offsets[:, half_entries(h)]))
+            nc.scalar.activation(ts_squared[h][:], values, SQUARE)
 
         ts_turned = psum("ts_turned", [P, 2, P], 0)
         for c in range(2):
-            nc.tensor.transpose(ts_turned[:, c, :], ts_all[:, slots(2 + c)], identity[:])
+            nc.tensor.transpose(ts_turned[:, c, :], ts_second[:, slots(c)], identity[:])
+        nc.vector.tensor_copy(w_pair[:, 1], w_window[1][:].indirect(offsets[:]))
         ts_by_slot = sbuf("ts_by_slot", [P, 2], F32)
         nc.scalar.copy(ts_by_slot[:], ts_turned[:, :, 0])
 
@@ -146,14 +152,13 @@ def tile_attend_gfisher_sq_pl_kernel(tc, xT, wT, us, ts, wt, x2, y, offs, out_0,
         nc.vector.tensor_tensor(row_factor[:], us_squared[:], wt_sb[:], MULT)
         by_lane = sbuf("factor_by_lane", [P, LANES, HALF], F32)
         for t in range(LANES):
-            nc.scalar.activation(by_lane[:, t, :], ts_squared[:, half_slots(0)], COPY, scale=row_factor[:, t : t + 1])
+            nc.scalar.activation(by_lane[:, t, :], ts_squared[0][:], COPY, scale=row_factor[:, t : t + 1])
+        w_grouped = sbuf("w_grouped", [P, I, LANES], BF16, on="w_window1")
+        nc.scalar.copy(w_grouped[:, :, 0:2], w_pair[:].rearrange("p j i -> p i j"))
         factor_first = sbuf("factor_first", [P, 2, SLOT_CHUNK, LANES], F32)
         for c in range(2):
             interleave(nc.scalar.copy, factor_first[:, c], by_lane[:, :, slots(c)])
 
-        w_grouped = sbuf("w_grouped", [P, I, LANES], BF16, on="ts_window")
-        nc.vector.tensor_copy(w_grouped[:, :, 1], w_window[1][:].indirect(offsets[:]))
-        nc.vector.tensor_copy(w_grouped[:, :, 0], w_first[:])
         nc.vector.tensor_copy(w_grouped[:, :, 2], w_window[2][:].indirect(offsets[:]))
         for h in range(2):
             nc.vector.tensor_copy(w_grouped[:, half_slots(h), 3], w_window[3][:].indirect(offsets[:, half_entries(h)]))
@@ -163,11 +168,11 @@ def tile_attend_gfisher_sq_pl_kernel(tc, xT, wT, us, ts, wt, x2, y, offs, out_0,
             values = w_grouped[:, half_slots(h)].rearrange("p i j -> p (i j)")
             nc.vector.quantize_mx(w_codes[:, half_slots(h)].bitcast(E4M3X4), w_scales[:, half_slots(h)], values)
 
-        factor_second = sbuf("factor_second", [P, 2, SLOT_CHUNK, LANES], F32, on="w_first")
+        factor_second = sbuf("factor_second", [P, 2, SLOT_CHUNK, LANES], F32)
         for c in range(2):
             nc.gpsimd.tensor_tensor(
                 factor_second[:, c],
-                ts_squared[:, slots(2 + c)].unsqueeze(2).to_broadcast([P, SLOT_CHUNK, LANES]),
+                ts_squared[1][:, slots(c)].unsqueeze(2).to_broadcast([P, SLOT_CHUNK, LANES]),
                 row_factor[:].unsqueeze(1).to_broadcast([P, SLOT_CHUNK, LANES]),
                 MULT,
             )
@@ -186,10 +191,12 @@ def tile_attend_gfisher_sq_pl_kernel(tc, xT, wT, us, ts, wt, x2, y, offs, out_0,
             deal_x(nc.vector.tensor_copy, tiles, 0, share)
             deal_x(nc.scalar.copy, tiles, share, P)
 
-        x2_words = placed_at("x2_words", [P, 2, P, 2], BF16, X_PLACE)
-        nc.scalar.copy(
-            x2_words[:].rearrange("p u s e -> p s u e"), x2_plane[0][:].rearrange("p (s u e) -> p s u e", u=2, e=2)
-        )
+        x2_words = placed_at("x2_words", [P, 2, 2, P, 2], BF16, X_PLACE)
+        for j in range(2):
+            nc.scalar.copy(
+                x2_words[:, j].rearrange("p u s e -> p s u e"),
+                x2_plane[j][:].rearrange("p (s u e) -> p s u e", u=2, e=2),
+            )
 
         x_codes = sbuf("x_codes", [P, LANES, P], U32)
         x_scales = sbuf("x_scales", [P, LANES, P], U8)
@@ -208,24 +215,27 @@ def tile_attend_gfisher_sq_pl_kernel(tc, xT, wT, us, ts, wt, x2, y, offs, out_0,
                 w_scales[:, half_slots(0)],
             )
             scores.append(bank)
-        by_slot = []
+        slot_sums = [psum(f"scores_by_slot{c}", [P, R], 4 + c)[:] for c in range(2)]
         for c in range(2):
-            bank = psum(f"scores_by_slot{c}", [P, R], 4 + c)
             product(
-                bank[:],
+                slot_sums[c],
                 w_codes[:, slots(2 + c)].bitcast(E4M3X4),
                 w_scales[:, slots(2 + c)],
                 x_codes[:].rearrange("p t s -> p (t s)").bitcast(E4M3X4),
                 x_scales[:].rearrange("p t s -> p (t s)"),
             )
-            scaled = sbuf(f"scaled_by_slot{c}", [P, LANES, P], F32)
+
+        def scale_by_slot(c, on=None):
+            scaled = sbuf(f"scaled_by_slot{c}", [P, LANES, P], F32, on=on)
             nc.scalar.activation(
-                scaled[:].rearrange("i t s -> i (t s)"), bank[:], COPY, scale=ts_by_slot[:, c : c + 1]
+                scaled[:].rearrange("i t s -> i (t s)"), slot_sums[c], COPY, scale=ts_by_slot[:, c : c + 1]
             )
-            by_slot.append(scaled)
+            return scaled
+
+        by_slot = [scale_by_slot(0)]
 
         def scale_scores(target, t, cols):
-            nc.vector.scalar_tensor_tensor(target, scores[t][:, cols], us_sb[:, t : t + 1], ts_all[:, cols], MULT, MULT)
+            nc.vector.scalar_tensor_tensor(target, scores[t][:, cols], us_sb[:, t : t + 1], ts_first[:, cols], MULT, MULT)
 
         scale_scores(z_first[:], 0, half_slots(0))
         for t in range(1, LANES - 1):
@@ -247,16 +257,17 @@ def tile_attend_gfisher_sq_pl_kernel(tc, xT, wT, us, ts, wt, x2, y, offs, out_0,
             return turned
 
         turned_back = [turn_back(0, 7)]
-        words = x2_words[:].rearrange("p u s e -> p u (s e)").bitcast(F32)
-        word_bank = psum("x2_turned_words", [P, 2, P], 4)
-        for u in range(2):
-            nc.tensor.transpose(word_bank[:, u, :], words[:, u, :], identity[:])
-        turned_back.append(turn_back(1, 0))
-        x2_turned = [None, turn_x2("x2_turned1", x2_plane[1][:], 5)]
+        words = x2_words[:].rearrange("p j u s e -> p (j u) (s e)").bitcast(F32)
+        word_bank = psum("x2_turned_words", [P, 2, 2, P], 4)
+        for j in range(2):
+            for u in range(2):
+                nc.tensor.transpose(word_bank[:, j, u, :], words[:, 2 * j + u, :], identity[:])
 
         error_first = sbuf("error_first", [P, LANES, HALF], F32)
         nc.gpsimd.tensor_tensor(error_first[:, 0, :], z_first[:], y_sb[:, 0, half_slots(0)], SUBTRACT)
-        squared = [[(sbuf(f"squared{c}", [P, SLOT_CHUNK, LANES], F32), slice(0, SLOT_CHUNK))] for c in range(3)]
+        squared_first = sbuf("squared_first", [P, HALF, LANES], F32)
+        squared = [[(squared_first[:, slots(c)], slice(0, SLOT_CHUNK))] for c in range(2)]
+        squared.append([(sbuf("squared2", [P, SLOT_CHUNK, LANES], F32), slice(0, SLOT_CHUNK))])
         cut = SLOT_CHUNK - LAST_SLOTS
         squared.append(
             [
@@ -313,37 +324,46 @@ def tile_attend_gfisher_sq_pl_kernel(tc, xT, wT, us, ts, wt, x2, y, offs, out_0,
         x2_codes = [codes[:] for codes in first_codes]
         x2_scales = [scales[:] for scales in first_scales]
 
+        def group_words(j):
+            nc.scalar.copy(
+                x2_grouped[j][:].bitcast(F32).rearrange("s (p u) -> s p u", u=2),
+                word_bank[:, j].rearrange("s u p -> s p u"),
+            )
+
         def quantise_x2(j):
             nc.vector.quantize_mx(x2_codes[j].bitcast(E4M3X4), x2_scales[j], x2_grouped[j][:])
 
         square(0, subtract(0))
         square(1, subtract(1))
-        nc.scalar.copy(
-            x2_grouped[0][:].bitcast(F32).rearrange("s (p u) -> s p u", u=2), word_bank[:].rearrange("s u p -> s p u")
-        )
+        group_words(0)
+        by_slot.append(scale_by_slot(1, on="error_first"))
+        turned_back.append(turn_back(1, 0))
         square(2, scale_and_subtract(2))
-        nc.scalar.copy(
-            x2_grouped[1][:].rearrange("s (p t) -> s p t", t=LANES), x2_turned[1][:].rearrange("s t p -> s p t")
-        )
-        weigh(nc.vector, 0)
-        weigh(nc.vector, 1)
+        group_words(1)
+        for engine, part in [(nc.gpsimd, slice(0, GPSIMD_WEIGHS)), (nc.vector, slice(GPSIMD_WEIGHS, HALF))]:
+            engine.tensor_tensor(
+                g_first[:].rearrange("p c i t -> p (c i) t")[:, part],
+                squared_first[:, part],
+                factor_first[:].rearrange("p c i t -> p (c i) t")[:, part],
+                MULT,
+            )
         quantise_x2(0)
         quantise_g(half_slots(0), g_first[:].rearrange("p c i t -> p (c i t)"))
         early_sums = [second_product("early_sum0", 0, padded_codes[:, :I], padded_scales[:, :I], 2)]
+        last_errors = scale_and_subtract(3, on="squared_first")
         quantise_x2(1)
         early_sums.append(second_product("early_sum1", 1, padded_codes[:, :I], padded_scales[:, :I], 3))
-        last_errors = scale_and_subtract(3, on="squared1")
-        early = [leave_bank("early0", early_sums[0], half_slots(1), on="x2_grouped1")]
+        early = [leave_bank("early0", early_sums[0], half_slots(1))]
         square(3, last_errors)
         g_second = sbuf("g_second", [P, 2, SLOT_CHUNK, LANES], BF16, on="g_first")
         g_grouped.extend([g_second[:, 0], g_second[:, 1]])
         weigh(nc.gpsimd, 2)
         weigh(nc.gpsimd, 3)
         early.append(leave_bank("early1", early_sums[1], half_slots(1), on="squared3"))
-        x2_turned.append(turn_x2("x2_turned2", x2_rest[:, 0, :], 0))
-        x2_turned.append(turn_x2("x2_turned3", x2_rest[:, 1, :], 2))
+        x2_turned = [turn_x2(f"x2_turned{j}", x2_rest[:, j, :], bank) for j, bank in enumerate([0, 2])]
         nc.vector.tensor_copy(out_window[0][:].indirect(offsets[:, half_entries(0)]), early[0][:])
-        quantise_g(half_slots(1), g_second[:].rearrange("p c i t -> p (c i t)"))
+        for c in range(2, 4):
+            quantise_g(slots(c), g_grouped[c].rearrange("p i t -> p (i t)"))
         nc.vector.tensor_copy(out_window[1][:].indirect(offsets[:, half_entries(0)]), early[1][:])
 
         rest_codes = placed_at("rest_codes", [P, T * LANES * 2 // (P * 4), P], U32, PAIRS_PLACE)[:, 0:2]
@@ -352,7 +372,7 @@ def tile_attend_gfisher_sq_pl_kernel(tc, xT, wT, us, ts, wt, x2, y, offs, out_0,
         x2_scales.extend([rest_scales[:, 0], rest_scales[:, 1]])
         rest_grouped = sbuf("rest_grouped", [P, 2, P, LANES], BF16, on="g_first")
         for j in range(2):
-            nc.scalar.copy(rest_grouped[:, j], x2_turned[2 + j][:].rearrange("s t p -> s p t"))
+            nc.scalar.copy(rest_grouped[:, j], x2_turned[j][:].rearrange("s t p -> s p t"))
         late = [
             leave_bank(f"late{j}", second_product(f"late_sum{j}", j, g_codes, g_scales, bank), half_slots(1))
             for j, bank in enumerate([1, 6])

@@ -30,7 +30,7 @@ SCALE_GROUP = T // 4
 
 VECTOR_DEALS = [96, 72]
 LAST_SLOTS = 32
-GPSIMD_WEIGHS = 96
+GPSIMD_WEIGHS = 64
 COL_WIDTHS = [128, 128, 256, 256, 256, 256, 256, 256, 128, 128]
 COL_STARTS = [sum(COL_WIDTHS[:k]) for k in range(len(COL_WIDTHS) + 1)]
 DIRECT_CHUNKS = [0, 1]
@@ -226,10 +226,9 @@ def tile_attend_gfisher_sq_pl_kernel(tc, xT, wT, us, ts, wt, x2, y, offs, out_0,
             )
 
         def scale_by_slot(c, on=None):
-            scaled = sbuf(f"scaled_by_slot{c}", [P, LANES, P], F32, on=on)
-            nc.scalar.activation(
-                scaled[:].rearrange("i t s -> i (t s)"), slot_sums[c], COPY, scale=ts_by_slot[:, c : c + 1]
-            )
+            scaled = sbuf(f"scaled_by_slot{c}", [P, 2, HALF], F32, on=on)
+            for h in range(2):
+                nc.scalar.activation(scaled[:, h], slot_sums[c][:, half_slots(h)], COPY, scale=ts_by_slot[:, c : c + 1])
             return scaled
 
         by_slot = [scale_by_slot(0)]
@@ -243,10 +242,13 @@ def tile_attend_gfisher_sq_pl_kernel(tc, xT, wT, us, ts, wt, x2, y, offs, out_0,
         for c in range(2):
             scale_scores(z_rest[:, LANES - 2, slots(c)], LANES - 1, slots(c))
 
-        def turn_back(c, bank):
-            turned = psum(f"turned_back{c}", [P, LANES, SLOT_CHUNK], bank)
-            for t in range(LANES):
-                nc.tensor.transpose(turned[:, t, :], by_slot[c][:, t, :], identity[:])
+        def turn_back(c, first_bank):
+            turned = []
+            for h in range(2):
+                pair = psum(f"turned_back{c}{h}", [P, 2, SLOT_CHUNK], first_bank + h)
+                for e in range(2):
+                    nc.tensor.transpose(pair[:, e, :], by_slot[c][:, h, slots(e)], identity[:])
+                    turned.append(pair[:, e, :])
             return turned
 
         def turn_x2(name, plane, bank):
@@ -256,7 +258,7 @@ def tile_attend_gfisher_sq_pl_kernel(tc, xT, wT, us, ts, wt, x2, y, offs, out_0,
                 nc.tensor.transpose(turned[:, t, :], rows[:, t, :], identity[:])
             return turned
 
-        turned_back = [turn_back(0, 7)]
+        turned_back = [turn_back(0, 6)]
         words = x2_words[:].rearrange("p j u s e -> p (j u) (s e)").bitcast(F32)
         word_bank = psum("x2_turned_words", [P, 2, 2, P], 4)
         for j in range(2):
@@ -297,7 +299,7 @@ def tile_attend_gfisher_sq_pl_kernel(tc, xT, wT, us, ts, wt, x2, y, offs, out_0,
             errors = sbuf(f"error{c}", [P, LANES, SLOT_CHUNK], F32, on=on)
             for t in range(LANES):
                 nc.vector.scalar_tensor_tensor(
-                    errors[:, t, :], turned_back[c - 2][:, t, :], us_sb[:, t : t + 1], y_sb[:, t, slots(c)], MULT, SUBTRACT
+                    errors[:, t, :], turned_back[c - 2][t], us_sb[:, t : t + 1], y_sb[:, t, slots(c)], MULT, SUBTRACT
                 )
             return errors[:]
 
@@ -338,8 +340,8 @@ def tile_attend_gfisher_sq_pl_kernel(tc, xT, wT, us, ts, wt, x2, y, offs, out_0,
         group_words(0)
         by_slot.append(scale_by_slot(1, on="error_first"))
         turned_back.append(turn_back(1, 0))
-        square(2, scale_and_subtract(2))
         group_words(1)
+        square(2, scale_and_subtract(2))
         for engine, part in [(nc.gpsimd, slice(0, GPSIMD_WEIGHS)), (nc.vector, slice(GPSIMD_WEIGHS, HALF))]:
             engine.tensor_tensor(
                 g_first[:].rearrange("p c i t -> p (c i) t")[:, part],
@@ -350,17 +352,17 @@ def tile_attend_gfisher_sq_pl_kernel(tc, xT, wT, us, ts, wt, x2, y, offs, out_0,
         quantise_x2(0)
         quantise_g(half_slots(0), g_first[:].rearrange("p c i t -> p (c i t)"))
         early_sums = [second_product("early_sum0", 0, padded_codes[:, :I], padded_scales[:, :I], 2)]
-        last_errors = scale_and_subtract(3, on="squared_first")
         quantise_x2(1)
         early_sums.append(second_product("early_sum1", 1, padded_codes[:, :I], padded_scales[:, :I], 3))
+        last_errors = scale_and_subtract(3, on="squared_first")
         early = [leave_bank("early0", early_sums[0], half_slots(1))]
         square(3, last_errors)
-        g_second = sbuf("g_second", [P, 2, SLOT_CHUNK, LANES], BF16, on="g_first")
+        g_second = sbuf("g_second", [P, 2, SLOT_CHUNK, LANES], BF16, on="x2_grouped1")
         g_grouped.extend([g_second[:, 0], g_second[:, 1]])
         weigh(nc.gpsimd, 2)
         weigh(nc.gpsimd, 3)
         early.append(leave_bank("early1", early_sums[1], half_slots(1), on="squared3"))
-        x2_turned = [turn_x2(f"x2_turned{j}", x2_rest[:, j, :], bank) for j, bank in enumerate([0, 2])]
+        x2_turned = [turn_x2(f"x2_turned{j}", x2_rest[:, j, :], bank) for j, bank in enumerate([1, 2])]
         nc.vector.tensor_copy(out_window[0][:].indirect(offsets[:, half_entries(0)]), early[0][:])
         for c in range(2, 4):
             quantise_g(slots(c), g_grouped[c].rearrange("p i t -> p (i t)"))
@@ -370,12 +372,12 @@ def tile_attend_gfisher_sq_pl_kernel(tc, xT, wT, us, ts, wt, x2, y, offs, out_0,
         rest_scales = sbuf("rest_scales", [P, 2, P], U8)
         x2_codes.extend([rest_codes[:, 0], rest_codes[:, 1]])
         x2_scales.extend([rest_scales[:, 0], rest_scales[:, 1]])
-        rest_grouped = sbuf("rest_grouped", [P, 2, P, LANES], BF16, on="g_first")
+        rest_grouped = sbuf("rest_grouped", [P, 2, P, LANES], BF16, on="x2_grouped1")
         for j in range(2):
             nc.scalar.copy(rest_grouped[:, j], x2_turned[j][:].rearrange("s t p -> s p t"))
         late = [
             leave_bank(f"late{j}", second_product(f"late_sum{j}", j, g_codes, g_scales, bank), half_slots(1))
-            for j, bank in enumerate([1, 6])
+            for j, bank in enumerate([0, 6])
         ]
         nc.vector.quantize_mx(
             rest_codes.rearrange("s j p -> s (j p)").bitcast(E4M3X4),

@@ -1,7 +1,6 @@
 from contextlib import ExitStack
 
 import concourse.mybir as mybir
-from concourse.masks import make_identity
 
 D, R, I, T = 512, 512, 512, 2048
 FLOPS = 2 * 2 * D * R * I
@@ -40,6 +39,7 @@ GPSIMD_PAIRED = 384
 
 X_PLACE = 0
 PAIRS_PLACE = X_PLACE + LANES * R * 4
+WINDOW_PLACE = PAIRS_PLACE + T * LANES * 2
 
 
 def tile_attend_gfisher_sq_pl_kernel(tc, xT, wT, us, ts, wt, x2, y, offs, out_0, out_1, out_2):
@@ -116,8 +116,20 @@ def tile_attend_gfisher_sq_pl_kernel(tc, xT, wT, us, ts, wt, x2, y, offs, out_0,
         nc.sync.dma_start(x2_rest[:], x2_rows[:, 2:4, :])
 
         identity = sbuf("identity", [P, P], F32)
-        make_identity(nc, identity[:])
-        out_window = [sbuf(f"out_window{j}", [P, T], F32) for j in range(LANES)]
+        zeros = placed_at("zeros", [P, T + 2 * P], F32, WINDOW_PLACE + (T - P) * 4)[:, :P]
+        nc.gpsimd.memset(zeros, 0.0)
+        nc.gpsimd.affine_select(
+            out=identity[:],
+            in_=zeros,
+            compare_op=mybir.AluOpType.not_equal,
+            fill=1.0,
+            base=0,
+            pattern=[[-1, P]],
+            channel_multiplier=1,
+        )
+        out_window = [sbuf("out_window0", [P, T], F32)]
+        for j in range(1, LANES):
+            out_window.append(placed_at(f"out_window{j}", [P, T], F32, WINDOW_PLACE + (j - 1) * T * 4))
         nc.vector.memset(out_window[0][:], 0.0)
         for j in range(1, LANES):
             nc.gpsimd.memset(out_window[j][:], 0.0)
@@ -128,8 +140,7 @@ def tile_attend_gfisher_sq_pl_kernel(tc, xT, wT, us, ts, wt, x2, y, offs, out_0,
             for c in range(4):
                 column = ts_columns[:, 4 * b + c : 4 * b + c + 1]
                 nc.tensor.transpose(bank[:, c, :], column.to_broadcast([P, P]), identity[:])
-            copy = nc.scalar.copy if b % 2 else nc.vector.tensor_copy
-            copy(window_by_row[:, :, 4 * b : 4 * b + 4], bank[:].rearrange("p c k -> p k c"))
+            nc.scalar.copy(window_by_row[:, :, 4 * b : 4 * b + 4], bank[:].rearrange("p c k -> p k c"))
         w_pair = sbuf("w_pair", [P, 2, I], BF16)
         nc.vector.tensor_copy(w_pair[:, 0], w_window[0][:].indirect(offsets[:]))
         ts_first = sbuf("ts_first", [P, HALF], F32)

@@ -353,6 +353,7 @@ def tile_attend_gfisher_sq_pl_kernel(tc, xT, wT, us, ts, wt, x2, y, offs, out_0,
         turned_back.append(turn_back(1, 0))
         group_words(1)
         square(2, scale_and_subtract(2))
+        x2_turned = [turn_x2("x2_turned2", x2_rest[:, 0, :], 6)]
         for engine, part in [(nc.gpsimd, slice(0, GPSIMD_WEIGHS)), (nc.vector, slice(GPSIMD_WEIGHS, HALF))]:
             engine.tensor_tensor(
                 g_first[:].rearrange("p c i t -> p (c i) t")[:, part],
@@ -373,7 +374,7 @@ def tile_attend_gfisher_sq_pl_kernel(tc, xT, wT, us, ts, wt, x2, y, offs, out_0,
         weigh(nc.gpsimd, 2)
         weigh(nc.gpsimd, 3)
         early.append(leave_bank("early1", early_sums[1], half_slots(1), on="squared3"))
-        x2_turned = [turn_x2(f"x2_turned{j}", x2_rest[:, j, :], bank) for j, bank in enumerate([1, 2])]
+        x2_turned.append(turn_x2("x2_turned3", x2_rest[:, 1, :], 2))
         nc.vector.tensor_copy(out_window[0][:].indirect(offsets[:, half_entries(0)]), early[0][:])
         for c in range(2, 4):
             quantise_g(slots(c), g_grouped[c].rearrange("p i t -> p (i t)"))
@@ -388,7 +389,7 @@ def tile_attend_gfisher_sq_pl_kernel(tc, xT, wT, us, ts, wt, x2, y, offs, out_0,
             nc.scalar.copy(rest_grouped[:, j], x2_turned[j][:].rearrange("s t p -> s p t"))
         late = [
             leave_bank(f"late{j}", second_product(f"late_sum{j}", j, g_codes, g_scales, bank), half_slots(1))
-            for j, bank in enumerate([0, 6])
+            for j, bank in enumerate([0, 1])
         ]
         nc.vector.quantize_mx(
             rest_codes.rearrange("s j p -> s (j p)").bitcast(E4M3X4),

@@ -40,6 +40,7 @@ GPSIMD_PAIRED = 384
 X_PLACE = 0
 PAIRS_PLACE = X_PLACE + LANES * R * 4
 WINDOW_PLACE = PAIRS_PLACE + T * LANES * 2
+GATHER_PLACE = WINDOW_PLACE + (LANES - 1) * T * 4
 
 
 def tile_attend_gfisher_sq_pl_kernel(tc, xT, wT, us, ts, wt, x2, y, offs, out_0, out_1, out_2):
@@ -91,7 +92,10 @@ def tile_attend_gfisher_sq_pl_kernel(tc, xT, wT, us, ts, wt, x2, y, offs, out_0,
         y_rows = y.rearrange("(s t) i -> s t i", t=LANES)
         out_rows = out_0.rearrange("(p j) c -> p j c", j=LANES)
 
-        w_window = [sbuf(f"w_window{j}", [P, T], F32) for j in range(LANES)]
+        w_window = [
+            placed_at("w_window1", [P, T], F32, GATHER_PLACE) if j == 1 else sbuf(f"w_window{j}", [P, T], F32)
+            for j in range(LANES)
+        ]
         x_sb = placed_at("x_sb", [P, LANES, R], F32, X_PLACE)
         x2_plane = [sbuf(f"x2_plane{j}", [P, R], F32) for j in range(2)]
         x2_rest = sbuf("x2_rest", [P, 2, R], F32)
@@ -164,19 +168,24 @@ def tile_attend_gfisher_sq_pl_kernel(tc, xT, wT, us, ts, wt, x2, y, offs, out_0,
         by_lane = sbuf("factor_by_lane", [P, LANES, HALF], F32)
         for t in range(LANES):
             nc.scalar.activation(by_lane[:, t, :], ts_squared[0][:], COPY, scale=row_factor[:, t : t + 1])
-        w_grouped = sbuf("w_grouped", [P, I, LANES], BF16, on="w_window1")
-        nc.scalar.copy(w_grouped[:, :, 0:2], w_pair[:].rearrange("p j i -> p i j"))
+        w_grouped = [
+            placed_at(f"w_grouped{h}", [P, HALF, LANES], BF16, GATHER_PLACE + h * HALF * LANES * 2) for h in range(2)
+        ]
+        for h in range(2):
+            nc.scalar.copy(w_grouped[h][:, :, 0:2], w_pair[:, :, half_slots(h)].rearrange("p j i -> p i j"))
         factor_first = sbuf("factor_first", [P, 2, SLOT_CHUNK, LANES], F32)
         for c in range(2):
             interleave(nc.scalar.copy, factor_first[:, c], by_lane[:, :, slots(c)])
 
-        nc.vector.tensor_copy(w_grouped[:, :, 2], w_window[2][:].indirect(offsets[:]))
-        for h in range(2):
-            nc.vector.tensor_copy(w_grouped[:, half_slots(h), 3], w_window[3][:].indirect(offsets[:, half_entries(h)]))
+        w_last = placed_at("w_last", [P, 2, HALF], BF16, GATHER_PLACE + I * LANES * 2)
+        for j in range(2, LANES):
+            nc.vector.tensor_copy(w_last[:, j - 2], w_window[j][:].indirect(offsets[:, half_entries(1)]))
+            nc.vector.tensor_copy(w_grouped[0][:, :, j], w_window[j][:].indirect(offsets[:, half_entries(0)]))
+        nc.scalar.copy(w_grouped[1][:, :, 2:4], w_last[:].rearrange("p j i -> p i j"))
         w_codes = sbuf("w_codes", [P, I], U32)
         w_scales = sbuf("w_scales", [P, I], U8)
-        for h in range(2):
-            values = w_grouped[:, half_slots(h)].rearrange("p i j -> p (i j)")
+        for h in [1, 0]:
+            values = w_grouped[h][:].rearrange("p i j -> p (i j)")
             nc.vector.quantize_mx(w_codes[:, half_slots(h)].bitcast(E4M3X4), w_scales[:, half_slots(h)], values)
 
         factor_second = sbuf("factor_second", [P, 2, SLOT_CHUNK, LANES], F32)

@@ -25,21 +25,16 @@ BANK_BYTES = 2048
 LINE = 4
 HALF = I // 2
 SLOT_CHUNK = 128
-SCALE_GROUP = T // 4
+GROUP = T // 4
 
 VECTOR_DEALS = [96, 72]
-LAST_SLOTS = 32
-GPSIMD_WEIGHS = 64
-COL_WIDTHS = [128, 128, 256, 256, 256, 256, 256, 256, 128, 128]
+GPSIMD_WEIGHS = 192
+GPSIMD_ROUNDS = 1792
+COL_WIDTHS = [256, 256, 256, 256, 256, 256, 256, 128, 128]
 COL_STARTS = [sum(COL_WIDTHS[:k]) for k in range(len(COL_WIDTHS) + 1)]
-DIRECT_CHUNKS = [0, 1]
-VECTOR_JOINED = [2, 3, 4, 5, 6]
-SCALAR_JOINED = [7, 8, 9]
-GPSIMD_PAIRED = 384
 
 X_PLACE = 0
-PAIRS_PLACE = X_PLACE + LANES * R * 4
-WINDOW_PLACE = PAIRS_PLACE + T * LANES * 2
+WINDOW_PLACE = X_PLACE + LANES * R * 4
 GATHER_PLACE = WINDOW_PLACE + (LANES - 1) * T * 4
 
 
@@ -66,14 +61,7 @@ def tile_attend_gfisher_sq_pl_kernel(tc, xT, wT, us, ts, wt, x2, y, offs, out_0,
             return slice(h * HALF, (h + 1) * HALF)
 
         def half_entries(h):
-            return slice(h * HALF // 16, (h + 1) * HALF // 16)
-
-        def interleave(instruction, grouped, by_lane, *function):
-            instruction(
-                grouped.rearrange("p (q i) t -> p q t i", i=LINE),
-                by_lane.rearrange("p t (q i) -> p q t i", i=LINE),
-                *function,
-            )
+            return offsets[:, h * HALF // 16 : (h + 1) * HALF // 16]
 
         def product(bank, stationary_codes, stationary_scales, moving_codes, moving_scales):
             nc.tensor.matmul_mx(
@@ -99,7 +87,7 @@ def tile_attend_gfisher_sq_pl_kernel(tc, xT, wT, us, ts, wt, x2, y, offs, out_0,
         x_sb = placed_at("x_sb", [P, LANES, R], F32, X_PLACE)
         x2_plane = [sbuf(f"x2_plane{j}", [P, R], F32) for j in range(2)]
         x2_rest = sbuf("x2_rest", [P, 2, R], F32)
-        y_sb = sbuf("y_sb", [P, LANES, I], F32)
+        y_half = [sbuf(f"y_half{h}", [P, LANES, HALF], F32) for h in range(2)]
         us_sb = sbuf("us_sb", [P, LANES], F32)
         wt_sb = sbuf("wt_sb", [P, LANES], F32)
         ts_window = sbuf("ts_window", [P, T], F32)
@@ -113,10 +101,10 @@ def tile_attend_gfisher_sq_pl_kernel(tc, xT, wT, us, ts, wt, x2, y, offs, out_0,
         for j in range(1, LANES):
             nc.sync.dma_start(w_window[j][:], w_rows[:, j, :])
         nc.sync.dma_start(x_sb[:], xT.rearrange("(p j) r -> p j r", j=LANES))
-        nc.sync.dma_start(y_sb[:, 0:2, :], y_rows[:, 0:2, :])
+        nc.sync.dma_start(y_half[0][:], y_rows[:, :, half_slots(0)])
         for j in range(2):
             nc.sync.dma_start(x2_plane[j][:], x2_rows[:, j, :])
-        nc.sync.dma_start(y_sb[:, 2:4, :], y_rows[:, 2:4, :])
+        nc.sync.dma_start(y_half[1][:], y_rows[:, :, half_slots(1)])
         nc.sync.dma_start(x2_rest[:], x2_rows[:, 2:4, :])
 
         identity = sbuf("identity", [P, P], F32)
@@ -145,13 +133,14 @@ def tile_attend_gfisher_sq_pl_kernel(tc, xT, wT, us, ts, wt, x2, y, offs, out_0,
                 column = ts_columns[:, 4 * b + c : 4 * b + c + 1]
                 nc.tensor.transpose(bank[:, c, :], column.to_broadcast([P, P]), identity[:])
             nc.scalar.copy(window_by_row[:, :, 4 * b : 4 * b + 4], bank[:].rearrange("p c k -> p k c"))
+
         w_pair = sbuf("w_pair", [P, 2, I], BF16)
         nc.vector.tensor_copy(w_pair[:, 0], w_window[0][:].indirect(offsets[:]))
         ts_first = sbuf("ts_first", [P, HALF], F32)
         ts_second = w_pair[:, 1].bitcast(F32)
         ts_squared = [sbuf(f"ts_squared{h}", [P, HALF], F32) for h in range(2)]
         for h, values in [(1, ts_second), (0, ts_first[:])]:
-            nc.vector.tensor_copy(values, ts_window[:].indirect(offsets[:, half_entries(h)]))
+            nc.vector.tensor_copy(values, ts_window[:].indirect(half_entries(h)))
             nc.scalar.activation(ts_squared[h][:], values, SQUARE)
 
         ts_turned = psum("ts_turned", [P, 2, P], 0)
@@ -165,40 +154,34 @@ def tile_attend_gfisher_sq_pl_kernel(tc, xT, wT, us, ts, wt, x2, y, offs, out_0,
         row_factor = sbuf("row_factor", [P, LANES], F32)
         nc.vector.tensor_tensor(us_squared[:], us_sb[:], us_sb[:], MULT)
         nc.vector.tensor_tensor(row_factor[:], us_squared[:], wt_sb[:], MULT)
-        by_lane = sbuf("factor_by_lane", [P, LANES, HALF], F32)
-        for t in range(LANES):
-            nc.scalar.activation(by_lane[:, t, :], ts_squared[0][:], COPY, scale=row_factor[:, t : t + 1])
+        factor = [sbuf(f"factor{h}", [P, HALF, LANES], F32) for h in range(2)]
+
+        def make_factor(h):
+            nc.vector.tensor_tensor(
+                factor[h][:],
+                ts_squared[h][:].unsqueeze(2).to_broadcast([P, HALF, LANES]),
+                row_factor[:].unsqueeze(1).to_broadcast([P, HALF, LANES]),
+                MULT,
+            )
+
         w_grouped = [
             placed_at(f"w_grouped{h}", [P, HALF, LANES], BF16, GATHER_PLACE + h * HALF * LANES * 2) for h in range(2)
         ]
         for h in range(2):
             nc.scalar.copy(w_grouped[h][:, :, 0:2], w_pair[:, :, half_slots(h)].rearrange("p j i -> p i j"))
-        factor_first = sbuf("factor_first", [P, 2, SLOT_CHUNK, LANES], F32)
-        for c in range(2):
-            interleave(nc.scalar.copy, factor_first[:, c], by_lane[:, :, slots(c)])
-
         w_last = placed_at("w_last", [P, 2, HALF], BF16, GATHER_PLACE + I * LANES * 2)
         for j in range(2, LANES):
-            nc.vector.tensor_copy(w_last[:, j - 2], w_window[j][:].indirect(offsets[:, half_entries(1)]))
-            nc.vector.tensor_copy(w_grouped[0][:, :, j], w_window[j][:].indirect(offsets[:, half_entries(0)]))
+            make_factor(j - 2)
+            nc.scalar.activation(w_last[:, j - 2], w_window[j][:].indirect(half_entries(1)), COPY)
+            nc.vector.tensor_copy(w_grouped[0][:, :, j], w_window[j][:].indirect(half_entries(0)))
         nc.scalar.copy(w_grouped[1][:, :, 2:4], w_last[:].rearrange("p j i -> p i j"))
         w_codes = sbuf("w_codes", [P, I], U32)
         w_scales = sbuf("w_scales", [P, I], U8)
-        for h in [1, 0]:
+        for h in range(2):
             values = w_grouped[h][:].rearrange("p i j -> p (i j)")
             nc.vector.quantize_mx(w_codes[:, half_slots(h)].bitcast(E4M3X4), w_scales[:, half_slots(h)], values)
 
-        factor_second = sbuf("factor_second", [P, 2, SLOT_CHUNK, LANES], F32)
-        for c in range(2):
-            nc.gpsimd.tensor_tensor(
-                factor_second[:, c],
-                ts_squared[1][:, slots(c)].unsqueeze(2).to_broadcast([P, SLOT_CHUNK, LANES]),
-                row_factor[:].unsqueeze(1).to_broadcast([P, SLOT_CHUNK, LANES]),
-                MULT,
-            )
-        factor = [factor_first[:, 0], factor_first[:, 1], factor_second[:, 0], factor_second[:, 1]]
-
-        x_grouped = sbuf("x_grouped", [P, LANES, P, LANES], BF16, on="factor_by_lane")
+        x_grouped = sbuf("x_grouped", [P, LANES, P, LANES], BF16)
 
         def deal_x(copy, tiles, first, end):
             copy(
@@ -220,8 +203,6 @@ def tile_attend_gfisher_sq_pl_kernel(tc, xT, wT, us, ts, wt, x2, y, offs, out_0,
 
         x_codes = sbuf("x_codes", [P, LANES, P], U32)
         x_scales = sbuf("x_scales", [P, LANES, P], U8)
-        z_rest = sbuf("z_rest", [P, LANES - 1, HALF], F32)
-        z_first = sbuf("z_first", [P, HALF], F32)
         scores = []
         for t in range(LANES):
             values = x_grouped[:, t, :, :].rearrange("p s j -> p (s j)")
@@ -251,221 +232,218 @@ def tile_attend_gfisher_sq_pl_kernel(tc, xT, wT, us, ts, wt, x2, y, offs, out_0,
                 nc.scalar.activation(scaled[:, h], slot_sums[c][:, half_slots(h)], COPY, scale=ts_by_slot[:, c : c + 1])
             return scaled
 
-        by_slot = [scale_by_slot(0)]
+        def turn_back(c, scaled, first_bank):
+            turned = []
+            for h in range(2):
+                pair = psum(f"turned_back{c}{h}", [P, 2, SLOT_CHUNK], first_bank + h)
+                for e in range(2):
+                    nc.tensor.transpose(pair[:, e, :], scaled[:, h, slots(e)], identity[:])
+                    turned.append(pair[:, e, :])
+            return turned
 
         def scale_scores(target, t, cols):
             nc.vector.scalar_tensor_tensor(target, scores[t][:, cols], us_sb[:, t : t + 1], ts_first[:, cols], MULT, MULT)
 
+        z_first = sbuf("z_first", [P, HALF], F32)
+        z_rest = sbuf("z_rest", [P, LANES - 1, HALF], F32)
+        error_first = sbuf("error_first", [P, LANES, HALF], F32)
+        squared = [sbuf(f"squared{c}", [P, SLOT_CHUNK, LANES], F32) for c in range(4)]
+        g_first = sbuf("g_first", [P, HALF, LANES], BF16)
+        g_late = [sbuf(f"g_late{c}", [P, SLOT_CHUNK, LANES], BF16) for c in range(2)]
+        g_codes = sbuf("g_codes", [P, I], U32)
+        g_scales = sbuf("g_scales", [P, I], U8)
+
+        def subtract(c):
+            errors = error_first[:, :, slots(c)]
+            nc.vector.tensor_tensor(errors[:, 1:], z_rest[:, :, slots(c)], y_half[0][:, 1:, slots(c)], SUBTRACT)
+            return errors
+
+        def scale_and_subtract(c, turned):
+            errors = sbuf(f"error_late{c}", [P, LANES, SLOT_CHUNK], F32)
+            for t in range(LANES):
+                nc.vector.scalar_tensor_tensor(
+                    errors[:, t, :], turned[t], us_sb[:, t : t + 1], y_half[1][:, t, slots(c)], MULT, SUBTRACT
+                )
+            return errors[:]
+
+        def square(c, errors):
+            nc.scalar.activation(
+                squared[c][:].rearrange("p (q i) t -> p q t i", i=LINE),
+                errors.rearrange("p t (q i) -> p q t i", i=LINE),
+                SQUARE,
+            )
+
+        def weigh_first(engine, first, end):
+            c = first // SLOT_CHUNK
+            part = slice(first - c * SLOT_CHUNK, end - c * SLOT_CHUNK)
+            engine.tensor_tensor(g_first[:, first:end], squared[c][:, part], factor[0][:, first:end], MULT)
+
+        def quantise_g(cols, values):
+            nc.vector.quantize_mx(
+                g_codes[:, cols].bitcast(E5M2X4), g_scales[:, cols], values.rearrange("p i t -> p (i t)")
+            )
+
+        x2_codes = [sbuf(f"x2_codes{u}", [P, n, P], U32) for u, n in enumerate([2, 1, 1])]
+        x2_scales = [sbuf(f"x2_scales{u}", [P, n, P], U8) for u, n in enumerate([2, 1, 1])]
+        plane_codes = [x2_codes[0][:, 0], x2_codes[0][:, 1], x2_codes[1][:, 0], x2_codes[2][:, 0]]
+        plane_scales = [x2_scales[0][:, 0], x2_scales[0][:, 1], x2_scales[1][:, 0], x2_scales[2][:, 0]]
+
+        def quantise_x2(u, grouped):
+            nc.vector.quantize_mx(
+                x2_codes[u][:].rearrange("s j p -> s (j p)").bitcast(E4M3X4),
+                x2_scales[u][:].rearrange("s j p -> s (j p)"),
+                grouped,
+            )
+
+        def turn_x2(j, bank):
+            turned = psum(f"x2_turned{j}", [P, LANES, P], bank)
+            rows = x2_rest[:, j - 2, :].rearrange("p (s t) -> p t s", t=LANES)
+            for t in range(LANES):
+                nc.tensor.transpose(turned[:, t, :], rows[:, t, :], identity[:])
+            return turned
+
+        def group_x2(copy, j, turned, on):
+            grouped = sbuf(f"x2_grouped{j}", [P, P, LANES], BF16, on=on)
+            copy(grouped[:], turned[:].rearrange("s t p -> s p t"))
+            return grouped[:].rearrange("s p t -> s (p t)")
+
+        def second_product(sums, j, h):
+            cols = half_slots(h)
+            product(
+                sums, plane_codes[j].bitcast(E4M3X4), plane_scales[j], g_codes[:, cols].bitcast(E5M2X4), g_scales[:, cols]
+            )
+
+        def leave_bank(copy, name, planes, h, bank):
+            sums = psum(name + "_sums", [P, len(planes), HALF], bank)
+            for e, j in enumerate(planes):
+                second_product(sums[:, e], j, h)
+            values = sbuf(name, [P, len(planes), HALF], F32)
+            copy(values[:], sums[:])
+            return values
+
+        def scatter_first(j, values):
+            nc.scalar.activation(out_window[j][:].indirect(half_entries(0)), values, COPY)
+
+        def scatter_second(j, values):
+            nc.vector.tensor_copy(out_window[j][:].indirect(half_entries(1)), values)
+
+        turned = [turn_back(0, scale_by_slot(0), 6)]
         scale_scores(z_first[:], 0, half_slots(0))
         for t in range(1, LANES - 1):
             scale_scores(z_rest[:, t - 1, :], t, half_slots(0))
         for c in range(2):
             scale_scores(z_rest[:, LANES - 2, slots(c)], LANES - 1, slots(c))
-
-        def turn_back(c, first_bank):
-            turned = []
-            for h in range(2):
-                pair = psum(f"turned_back{c}{h}", [P, 2, SLOT_CHUNK], first_bank + h)
-                for e in range(2):
-                    nc.tensor.transpose(pair[:, e, :], by_slot[c][:, h, slots(e)], identity[:])
-                    turned.append(pair[:, e, :])
-            return turned
-
-        def turn_x2(name, plane, bank):
-            turned = psum(name, [P, LANES, P], bank)
-            rows = plane.rearrange("p (s t) -> p t s", t=LANES)
-            for t in range(LANES):
-                nc.tensor.transpose(turned[:, t, :], rows[:, t, :], identity[:])
-            return turned
-
-        turned_back = [turn_back(0, 6)]
+        nc.gpsimd.tensor_tensor(error_first[:, 0, :], z_first[:], y_half[0][:, 0, :], SUBTRACT)
         words = x2_words[:].rearrange("p j u s e -> p (j u) (s e)").bitcast(F32)
-        word_bank = psum("x2_turned_words", [P, 2, 2, P], 4)
+        word_bank = psum("x2_turned_words", [P, 2, 2, P], 3)
         for j in range(2):
             for u in range(2):
                 nc.tensor.transpose(word_bank[:, j, u, :], words[:, 2 * j + u, :], identity[:])
-
-        error_first = sbuf("error_first", [P, LANES, HALF], F32)
-        nc.gpsimd.tensor_tensor(error_first[:, 0, :], z_first[:], y_sb[:, 0, half_slots(0)], SUBTRACT)
-        squared_first = sbuf("squared_first", [P, HALF, LANES], F32)
-        squared = [[(squared_first[:, slots(c)], slice(0, SLOT_CHUNK))] for c in range(2)]
-        squared.append([(sbuf("squared2", [P, SLOT_CHUNK, LANES], F32), slice(0, SLOT_CHUNK))])
-        cut = SLOT_CHUNK - LAST_SLOTS
-        squared.append(
-            [
-                (sbuf("squared3", [P, cut, LANES], F32), slice(0, cut)),
-                (sbuf("squared_last", [P, LAST_SLOTS, LANES], F32), slice(cut, SLOT_CHUNK)),
-            ]
-        )
-        g_first = sbuf("g_first", [P, 2, SLOT_CHUNK, LANES], BF16)
-        g_grouped = [g_first[:, 0], g_first[:, 1]]
-        padded_codes = sbuf("padded_codes", [P, HALF + I], U32)
-        padded_scales = sbuf("padded_scales", [P, HALF + I], U8)
-        nc.gpsimd.memset(padded_codes[:, :HALF], 0)
-        nc.gpsimd.memset(padded_scales[:, :HALF], 0)
-        g_codes = padded_codes[:, HALF:]
-        g_scales = padded_scales[:, HALF:]
-
-        def square(c, errors):
-            for squares, part in squared[c]:
-                interleave(nc.scalar.activation, squares[:], errors[:, :, part], SQUARE)
-
-        def subtract(c):
-            errors = error_first[:, :, slots(c)]
-            nc.vector.tensor_tensor(errors[:, 1:], z_rest[:, :, slots(c)], y_sb[:, 1:, slots(c)], SUBTRACT)
-            return errors
-
-        def scale_and_subtract(c, on=None):
-            errors = sbuf(f"error{c}", [P, LANES, SLOT_CHUNK], F32, on=on)
-            for t in range(LANES):
-                nc.vector.scalar_tensor_tensor(
-                    errors[:, t, :], turned_back[c - 2][t], us_sb[:, t : t + 1], y_sb[:, t, slots(c)], MULT, SUBTRACT
-                )
-            return errors[:]
-
-        def weigh(engine, c):
-            for squares, part in squared[c]:
-                engine.tensor_tensor(g_grouped[c][:, part], squares[:], factor[c][:, part], MULT)
-
-        def quantise_g(cols, values):
-            nc.vector.quantize_mx(g_codes[:, cols].bitcast(E5M2X4), g_scales[:, cols], values)
-
-        def second_product(name, j, codes, scales, bank):
-            sums = psum(name, [P, I], bank)
-            product(sums[:], x2_codes[j].bitcast(E4M3X4), x2_scales[j], codes.bitcast(E5M2X4), scales)
-            return sums
-
-        def leave_bank(name, bank, cols, on=None):
-            values = sbuf(name, [P, cols.stop - cols.start], F32, on=on)
-            nc.scalar.copy(values[:], bank[:, cols])
-            return values
-
-        x2_grouped = [sbuf(f"x2_grouped{j}", [P, P * LANES], BF16) for j in range(2)]
-        first_codes = [sbuf(f"x2_codes{j}", [P, P], U32) for j in range(2)]
-        first_scales = [sbuf(f"x2_scales{j}", [P, P], U8) for j in range(2)]
-        x2_codes = [codes[:] for codes in first_codes]
-        x2_scales = [scales[:] for scales in first_scales]
-
-        def group_words(j):
-            nc.scalar.copy(
-                x2_grouped[j][:].bitcast(F32).rearrange("s (p u) -> s p u", u=2),
-                word_bank[:, j].rearrange("s u p -> s p u"),
-            )
-
-        def quantise_x2(j):
-            nc.vector.quantize_mx(x2_codes[j].bitcast(E4M3X4), x2_scales[j], x2_grouped[j][:])
-
         square(0, subtract(0))
+        turned.append(turn_back(1, scale_by_slot(1), 0))
         square(1, subtract(1))
-        group_words(0)
-        by_slot.append(scale_by_slot(1, on="error_first"))
-        turned_back.append(turn_back(1, 0))
-        group_words(1)
-        square(2, scale_and_subtract(2))
-        x2_turned = [turn_x2("x2_turned2", x2_rest[:, 0, :], 6)]
-        for engine, part in [(nc.gpsimd, slice(0, GPSIMD_WEIGHS)), (nc.vector, slice(GPSIMD_WEIGHS, HALF))]:
-            engine.tensor_tensor(
-                g_first[:].rearrange("p c i t -> p (c i) t")[:, part],
-                squared_first[:, part],
-                factor_first[:].rearrange("p c i t -> p (c i) t")[:, part],
-                MULT,
-            )
-        quantise_x2(0)
-        quantise_g(half_slots(0), g_first[:].rearrange("p c i t -> p (c i t)"))
-        early_sums = [second_product("early_sum0", 0, padded_codes[:, :I], padded_scales[:, :I], 2)]
-        quantise_x2(1)
-        early_sums.append(second_product("early_sum1", 1, padded_codes[:, :I], padded_scales[:, :I], 3))
-        last_errors = scale_and_subtract(3, on="squared_first")
-        early = [leave_bank("early0", early_sums[0], half_slots(1))]
-        square(3, last_errors)
-        g_second = sbuf("g_second", [P, 2, SLOT_CHUNK, LANES], BF16, on="x2_grouped1")
-        g_grouped.extend([g_second[:, 0], g_second[:, 1]])
-        weigh(nc.gpsimd, 2)
-        weigh(nc.gpsimd, 3)
-        early.append(leave_bank("early1", early_sums[1], half_slots(1), on="squared3"))
-        x2_turned.append(turn_x2("x2_turned3", x2_rest[:, 1, :], 2))
-        nc.vector.tensor_copy(out_window[0][:].indirect(offsets[:, half_entries(0)]), early[0][:])
-        for c in range(2, 4):
-            quantise_g(slots(c), g_grouped[c].rearrange("p i t -> p (i t)"))
-        nc.vector.tensor_copy(out_window[1][:].indirect(offsets[:, half_entries(0)]), early[1][:])
-
-        rest_codes = placed_at("rest_codes", [P, T * LANES * 2 // (P * 4), P], U32, PAIRS_PLACE)[:, 0:2]
-        rest_scales = sbuf("rest_scales", [P, 2, P], U8)
-        x2_codes.extend([rest_codes[:, 0], rest_codes[:, 1]])
-        x2_scales.extend([rest_scales[:, 0], rest_scales[:, 1]])
-        rest_grouped = sbuf("rest_grouped", [P, 2, P, LANES], BF16, on="x2_grouped1")
-        for j in range(2):
-            nc.scalar.copy(rest_grouped[:, j], x2_turned[j][:].rearrange("s t p -> s p t"))
-        late = [
-            leave_bank(f"late{j}", second_product(f"late_sum{j}", j, g_codes, g_scales, bank), half_slots(1))
-            for j, bank in enumerate([0, 1])
-        ]
-        nc.vector.quantize_mx(
-            rest_codes.rearrange("s j p -> s (j p)").bitcast(E4M3X4),
-            rest_scales[:].rearrange("s j p -> s (j p)"),
-            rest_grouped[:].rearrange("s j p t -> s (j p t)"),
+        weigh_first(nc.gpsimd, 0, SLOT_CHUNK)
+        square(2, scale_and_subtract(0, turned[0]))
+        first_grouped = sbuf("x2_grouped01", [P, 2, P * LANES], BF16)
+        nc.vector.tensor_copy(
+            first_grouped[:].bitcast(F32).rearrange("s j (p u) -> s j p u", u=2),
+            word_bank[:].rearrange("s j u p -> s j p u"),
         )
-        whole = [
-            leave_bank(f"fisher{j}", second_product(f"whole_sum{j}", j, g_codes, g_scales, bank), slice(0, I))
-            for j, bank in [(2, 4), (3, 7)]
-        ]
-        last_pieces = [(values, half_entries(1)) for values in late] + [(values, slice(0, I // 16)) for values in whole]
+        weigh_first(nc.gpsimd, SLOT_CHUNK, GPSIMD_WEIGHS)
+        square(3, scale_and_subtract(1, turned[1]))
+        x2_turned = [turn_x2(2, 6)]
+        weigh_first(nc.vector, GPSIMD_WEIGHS, HALF)
+        quantise_x2(0, first_grouped[:].rearrange("s j w -> s (j w)"))
+        quantise_g(half_slots(0), g_first[:])
+        grouped2 = group_x2(nc.scalar.copy, 2, x2_turned[0], None)
+        first0 = leave_bank(nc.scalar.copy, "first0", [0], 0, 4)
+        scatter_first(0, first0[:, 0])
+        for c in range(2):
+            nc.vector.tensor_tensor(g_late[c][:], squared[2 + c][:], factor[1][:, slots(c)], MULT)
+        for c in range(2):
+            quantise_g(slots(2 + c), g_late[c][:])
+        first1_sums = psum("first1_sums", [P, HALF], 5)
+        second_product(first1_sums[:], 1, 0)
+        x2_turned.append(turn_x2(3, 6))
+        grouped3 = group_x2(nc.vector.tensor_copy, 3, x2_turned[1], "g_late1")
+        second0 = leave_bank(nc.vector.tensor_copy, "second0", [0], 1, 0)
+        first1 = sbuf("first1", [P, HALF], F32)
+        nc.scalar.copy(first1[:], first1_sums[:])
+        quantise_x2(1, grouped2)
+        quantise_x2(2, grouped3)
+        scatter_second(0, second0[:, 0])
+        nc.sync.dma_start(out_rows[:, 0, :], out_window[0][:])
+        scatter_first(1, first1[:])
+        second1 = leave_bank(nc.vector.tensor_copy, "second1", [1], 1, 1)
+        scatter_second(1, second1[:, 0])
+        nc.sync.dma_start(out_rows[:, 1, :], out_window[1][:])
+        first23 = leave_bank(nc.scalar.copy, "first23", [2, 3], 0, 3)
+        second23 = leave_bank(nc.vector.tensor_copy, "second23", [2, 3], 1, 7)
+        for j in range(2, LANES):
+            scatter_first(j, first23[:, j - 2])
+        for j in range(2, LANES):
+            scatter_second(j, second23[:, j - 2])
+        nc.sync.dma_start(out_rows[:, 2, :], out_window[2][:])
 
-        out_pairs = placed_at("out_pairs", [P, T * LANES], BF16, PAIRS_PLACE)
-        pair_lanes = out_pairs[:].rearrange("p (u c e) -> p u c e", u=2, e=2)
-        pair_words = out_pairs[:].bitcast(F32).rearrange("p (u c) -> p c u", u=2)
+        pairs = [sbuf(f"pairs{g}", [P, GROUP * LANES], BF16) for g in range(4)]
         out_grouped = [sbuf(f"out_grouped{k}", [P, width * LANES], BF16) for k, width in enumerate(COL_WIDTHS)]
         out_codes = sbuf("out_codes", [P, T], U32)
-        out_scales = sbuf("out_scales", [P, SCALE_GROUP], U8)
+        out_scales = sbuf("out_scales", [P, GROUP], U8)
         words_out = out_1.rearrange("a p c l -> p (a c l)").bitcast(I32)
         scales_out = out_2.rearrange("a q c -> q (a c)").bitcast(I32).rearrange("q (g c) -> g q c", g=4)
-
-        def columns(k):
-            return slice(COL_STARTS[k], COL_STARTS[k + 1])
 
         def round_on_gpsimd(rounded, values):
             nc.gpsimd.tensor_scalar(rounded, values, 1.0, 0.0, MULT, ADD)
 
+        def round_lane(copy, j, first, end):
+            g, place = divmod(first, GROUP)
+            lanes = pairs[g][:].rearrange("p (u c e) -> p u c e", u=2, e=2)
+            copy(lanes[:, j // 2, place : place + end - first, j % 2], out_window[j][:, first:end])
+
         def join_pairs(copy, k):
-            copy(out_grouped[k][:].bitcast(F32).rearrange("p (c u) -> p c u", u=2), pair_words[:, columns(k)])
+            g, place = divmod(COL_STARTS[k], GROUP)
+            pair_words = pairs[g][:].bitcast(F32).rearrange("p (u c) -> p c u", u=2)
+            copy(
+                out_grouped[k][:].bitcast(F32).rearrange("p (c u) -> p c u", u=2),
+                pair_words[:, place : place + COL_WIDTHS[k]],
+            )
 
         def quantise_out(k):
-            group, place = divmod(COL_STARTS[k], SCALE_GROUP)
-            plane = out_scales[4 * group :, place : place + COL_WIDTHS[k]]
-            nc.vector.quantize_mx(out_codes[:, columns(k)].bitcast(E4M3X4), plane, out_grouped[k][:])
+            first, end = COL_STARTS[k], COL_STARTS[k + 1]
+            g, place = divmod(first, GROUP)
+            plane = out_scales[4 * g :, place : place + end - first]
+            nc.vector.quantize_mx(out_codes[:, first:end].bitcast(E4M3X4), plane, out_grouped[k][:])
 
-        paired = VECTOR_JOINED + SCALAR_JOINED
-        for j in range(LANES):
-            last = j == LANES - 1
-            values, entries = last_pieces[j]
-            nc.vector.tensor_copy(out_window[j][:].indirect(offsets[:, entries]), values[:])
-            queue = nc.scalar if last else nc.sync
-            queue.dma_start(out_rows[:, j, :], out_window[j][:])
-            for k in DIRECT_CHUNKS:
-                lanes = out_grouped[k][:].rearrange("p (c l) -> p c l", l=LANES)
-                window_part = out_window[j][:, columns(k)]
-                if last:
-                    nc.vector.tensor_copy(lanes[:, :, j], window_part)
-                elif j == LANES - 2:
-                    round_on_gpsimd(lanes[:, :, j:], window_part.unsqueeze(2).to_broadcast([P, COL_WIDTHS[k], 2]))
-                else:
-                    round_on_gpsimd(lanes[:, :, j], window_part)
-            scalar_end = T
-            if j < 2:
-                scalar_end = T - GPSIMD_PAIRED
-                round_on_gpsimd(pair_lanes[:, 0, scalar_end:, j], out_window[j][:, scalar_end:])
-            for cols in [columns(k) for k in paired] if last else [slice(COL_STARTS[paired[0]], scalar_end)]:
-                nc.scalar.copy(pair_lanes[:, j // 2, cols, j % 2], out_window[j][:, cols])
-        for k in SCALAR_JOINED:
+        def store_words(first, end):
+            nc.sync.dma_start(words_out[:, first:end], out_codes[:, first:end].bitcast(I32))
+
+        for j in range(2):
+            for g in range(4):
+                round_lane(round_on_gpsimd, j, g * GROUP, min((g + 1) * GROUP, GPSIMD_ROUNDS))
+        for g in range(2, 4):
+            round_lane(nc.scalar.copy, 2, g * GROUP, (g + 1) * GROUP)
+        nc.scalar.dma_start(out_rows[:, 3, :], out_window[3][:])
+        round_lane(nc.scalar.copy, 3, 2 * GROUP, 3 * GROUP)
+        for k in [4, 5]:
             join_pairs(nc.scalar.copy, k)
+        for j in range(2):
+            round_lane(nc.scalar.copy, j, GPSIMD_ROUNDS, T)
+        round_lane(nc.scalar.copy, 3, 3 * GROUP, T)
+        for k in [6, 7, 8]:
+            join_pairs(nc.scalar.copy, k)
+        for g in range(2):
+            round_lane(nc.vector.tensor_copy, 2, g * GROUP, (g + 1) * GROUP)
+        for g in range(2):
+            round_lane(nc.vector.tensor_copy, 3, g * GROUP, (g + 1) * GROUP)
+        join_pairs(nc.vector.tensor_copy, 0)
         stored = 0
         for k in range(len(COL_WIDTHS)):
-            if k + 1 in VECTOR_JOINED:
+            if k + 1 < 4:
                 join_pairs(nc.vector.tensor_copy, k + 1)
             quantise_out(k)
             done = COL_STARTS[k + 1]
-            if done % SCALE_GROUP == 0 or done == T - SCALE_GROUP // 2:
-                nc.sync.dma_start(words_out[:, stored:done], out_codes[:, stored:done].bitcast(I32))
+            if done % GROUP == 0 or done == T - GROUP // 2:
+                store_words(stored, done)
                 stored = done
         for q in range(4):
             queue = nc.scalar if q % 2 else nc.sync

@@ -29,13 +29,14 @@ GROUP = T // 4
 
 VECTOR_DEALS = [96, 72]
 GPSIMD_WEIGHS = 192
-GPSIMD_ROUNDS = 1792
 COL_WIDTHS = [256, 256, 256, 256, 256, 256, 256, 128, 128]
 COL_STARTS = [sum(COL_WIDTHS[:k]) for k in range(len(COL_WIDTHS) + 1)]
 
 X_PLACE = 0
 WINDOW_PLACE = X_PLACE + LANES * R * 4
 GATHER_PLACE = WINDOW_PLACE + (LANES - 1) * T * 4
+PAIRS_PLACE = GATHER_PLACE + T * 4
+PAIR_BYTES = GROUP * LANES * 2
 
 
 def tile_attend_gfisher_sq_pl_kernel(tc, xT, wT, us, ts, wt, x2, y, offs, out_0, out_1, out_2):
@@ -313,11 +314,12 @@ def tile_attend_gfisher_sq_pl_kernel(tc, xT, wT, us, ts, wt, x2, y, offs, out_0,
                 sums, plane_codes[j].bitcast(E4M3X4), plane_scales[j], g_codes[:, cols].bitcast(E5M2X4), g_scales[:, cols]
             )
 
-        def leave_bank(copy, name, planes, h, bank):
+        def leave_bank(copy, name, planes, h, bank, place=None):
             sums = psum(name + "_sums", [P, len(planes), HALF], bank)
             for e, j in enumerate(planes):
                 second_product(sums[:, e], j, h)
-            values = sbuf(name, [P, len(planes), HALF], F32)
+            shape = [P, len(planes), HALF]
+            values = sbuf(name, shape, F32) if place is None else placed_at(name, shape, F32, place)
             copy(values[:], sums[:])
             return values
 
@@ -377,15 +379,15 @@ def tile_attend_gfisher_sq_pl_kernel(tc, xT, wT, us, ts, wt, x2, y, offs, out_0,
         second1 = leave_bank(nc.vector.tensor_copy, "second1", [1], 1, 1)
         scatter_second(1, second1[:, 0])
         nc.sync.dma_start(out_rows[:, 1, :], out_window[1][:])
-        first23 = leave_bank(nc.scalar.copy, "first23", [2, 3], 0, 3)
-        second23 = leave_bank(nc.vector.tensor_copy, "second23", [2, 3], 1, 7)
+        first23 = leave_bank(nc.scalar.copy, "first23", [2, 3], 0, 3, PAIRS_PLACE + 3 * PAIR_BYTES - HALF * 4)
+        second23 = leave_bank(nc.vector.tensor_copy, "second23", [2, 3], 1, 7, PAIRS_PLACE + PAIR_BYTES)
         for j in range(2, LANES):
             scatter_first(j, first23[:, j - 2])
         for j in range(2, LANES):
             scatter_second(j, second23[:, j - 2])
         nc.sync.dma_start(out_rows[:, 2, :], out_window[2][:])
 
-        pairs = [sbuf(f"pairs{g}", [P, GROUP * LANES], BF16) for g in range(4)]
+        pairs = [placed_at(f"pairs{g}", [P, GROUP * LANES], BF16, PAIRS_PLACE + g * PAIR_BYTES) for g in range(4)]
         out_grouped = [sbuf(f"out_grouped{k}", [P, width * LANES], BF16) for k, width in enumerate(COL_WIDTHS)]
         out_codes = sbuf("out_codes", [P, T], U32)
         out_scales = sbuf("out_scales", [P, GROUP], U8)
@@ -418,23 +420,21 @@ def tile_attend_gfisher_sq_pl_kernel(tc, xT, wT, us, ts, wt, x2, y, offs, out_0,
             nc.sync.dma_start(words_out[:, first:end], out_codes[:, first:end].bitcast(I32))
 
         for j in range(2):
-            for g in range(4):
-                round_lane(round_on_gpsimd, j, g * GROUP, min((g + 1) * GROUP, GPSIMD_ROUNDS))
-        for g in range(2, 4):
-            round_lane(nc.scalar.copy, 2, g * GROUP, (g + 1) * GROUP)
+            round_lane(round_on_gpsimd, j, 0, GROUP)
+        for j in range(3):
+            round_lane(nc.scalar.copy, j, 2 * GROUP, 3 * GROUP)
         nc.scalar.dma_start(out_rows[:, 3, :], out_window[3][:])
         round_lane(nc.scalar.copy, 3, 2 * GROUP, 3 * GROUP)
         for k in [4, 5]:
             join_pairs(nc.scalar.copy, k)
-        for j in range(2):
-            round_lane(nc.scalar.copy, j, GPSIMD_ROUNDS, T)
-        round_lane(nc.scalar.copy, 3, 3 * GROUP, T)
+        for j in range(LANES):
+            round_lane(nc.scalar.copy, j, 3 * GROUP, T)
         for k in [6, 7, 8]:
             join_pairs(nc.scalar.copy, k)
-        for g in range(2):
-            round_lane(nc.vector.tensor_copy, 2, g * GROUP, (g + 1) * GROUP)
-        for g in range(2):
-            round_lane(nc.vector.tensor_copy, 3, g * GROUP, (g + 1) * GROUP)
+        for j in range(2, LANES):
+            round_lane(nc.vector.tensor_copy, j, 0, GROUP)
+        for j in range(LANES):
+            round_lane(nc.vector.tensor_copy, j, GROUP, 2 * GROUP)
         join_pairs(nc.vector.tensor_copy, 0)
         stored = 0
         for k in range(len(COL_WIDTHS)):

@@ -29,14 +29,15 @@ GROUP = T // 4
 
 VECTOR_DEALS = [96, 72]
 GPSIMD_WEIGHS = 192
-COL_WIDTHS = [256, 256, 256, 256, 256, 256, 256, 128, 128]
+COL_WIDTHS = [256, 256, 256, 256, 256, 128, 128, 256, 128, 128]
 COL_STARTS = [sum(COL_WIDTHS[:k]) for k in range(len(COL_WIDTHS) + 1)]
 
 X_PLACE = 0
 WINDOW_PLACE = X_PLACE + LANES * R * 4
 GATHER_PLACE = WINDOW_PLACE + (LANES - 1) * T * 4
 PAIRS_PLACE = GATHER_PLACE + T * 4
-PAIR_BYTES = GROUP * LANES * 2
+PAIR_WIDTHS = [512, 512, 384, 128, 512]
+PAIR_STARTS = [sum(PAIR_WIDTHS[:n]) for n in range(len(PAIR_WIDTHS) + 1)]
 
 
 def tile_attend_gfisher_sq_pl_kernel(tc, xT, wT, us, ts, wt, x2, y, offs, out_0, out_1, out_2):
@@ -156,33 +157,38 @@ def tile_attend_gfisher_sq_pl_kernel(tc, xT, wT, us, ts, wt, x2, y, offs, out_0,
         nc.vector.tensor_tensor(us_squared[:], us_sb[:], us_sb[:], MULT)
         nc.vector.tensor_tensor(row_factor[:], us_squared[:], wt_sb[:], MULT)
         factor = [sbuf(f"factor{h}", [P, HALF, LANES], F32) for h in range(2)]
-
-        def make_factor(h):
-            nc.vector.tensor_tensor(
-                factor[h][:],
-                ts_squared[h][:].unsqueeze(2).to_broadcast([P, HALF, LANES]),
-                row_factor[:].unsqueeze(1).to_broadcast([P, HALF, LANES]),
-                MULT,
-            )
-
+        by_lane = sbuf("factor_by_lane", [P, LANES, HALF], F32)
+        for t in range(LANES):
+            nc.scalar.activation(by_lane[:, t, :], ts_squared[0][:], COPY, scale=row_factor[:, t : t + 1])
         w_grouped = [
             placed_at(f"w_grouped{h}", [P, HALF, LANES], BF16, GATHER_PLACE + h * HALF * LANES * 2) for h in range(2)
         ]
         for h in range(2):
             nc.scalar.copy(w_grouped[h][:, :, 0:2], w_pair[:, :, half_slots(h)].rearrange("p j i -> p i j"))
+        for c in range(2):
+            nc.scalar.copy(
+                factor[0][:, slots(c)].rearrange("p (q i) t -> p q t i", i=LINE),
+                by_lane[:, :, slots(c)].rearrange("p t (q i) -> p q t i", i=LINE),
+            )
         w_last = placed_at("w_last", [P, 2, HALF], BF16, GATHER_PLACE + I * LANES * 2)
         for j in range(2, LANES):
-            make_factor(j - 2)
-            nc.scalar.activation(w_last[:, j - 2], w_window[j][:].indirect(half_entries(1)), COPY)
+            nc.vector.tensor_copy(w_last[:, j - 2], w_window[j][:].indirect(half_entries(1)))
             nc.vector.tensor_copy(w_grouped[0][:, :, j], w_window[j][:].indirect(half_entries(0)))
         nc.scalar.copy(w_grouped[1][:, :, 2:4], w_last[:].rearrange("p j i -> p i j"))
         w_codes = sbuf("w_codes", [P, I], U32)
         w_scales = sbuf("w_scales", [P, I], U8)
-        for h in range(2):
+        for h in [1, 0]:
             values = w_grouped[h][:].rearrange("p i j -> p (i j)")
             nc.vector.quantize_mx(w_codes[:, half_slots(h)].bitcast(E4M3X4), w_scales[:, half_slots(h)], values)
+        for c in range(2):
+            nc.gpsimd.tensor_tensor(
+                factor[1][:, slots(c)],
+                ts_squared[1][:, slots(c)].unsqueeze(2).to_broadcast([P, SLOT_CHUNK, LANES]),
+                row_factor[:].unsqueeze(1).to_broadcast([P, SLOT_CHUNK, LANES]),
+                MULT,
+            )
 
-        x_grouped = sbuf("x_grouped", [P, LANES, P, LANES], BF16)
+        x_grouped = sbuf("x_grouped", [P, LANES, P, LANES], BF16, on="factor_by_lane")
 
         def deal_x(copy, tiles, first, end):
             copy(
@@ -323,11 +329,12 @@ def tile_attend_gfisher_sq_pl_kernel(tc, xT, wT, us, ts, wt, x2, y, offs, out_0,
             copy(values[:], sums[:])
             return values
 
-        def scatter_first(j, values):
-            nc.scalar.activation(out_window[j][:].indirect(half_entries(0)), values, COPY)
-
-        def scatter_second(j, values):
-            nc.vector.tensor_copy(out_window[j][:].indirect(half_entries(1)), values)
+        def scatter(engine, j, h, values):
+            places = out_window[j][:].indirect(half_entries(h))
+            if engine == "scalar":
+                nc.scalar.activation(places, values, COPY)
+            else:
+                nc.vector.tensor_copy(places, values)
 
         turned = [turn_back(0, scale_by_slot(0), 6)]
         scale_scores(z_first[:], 0, half_slots(0))
@@ -359,7 +366,7 @@ def tile_attend_gfisher_sq_pl_kernel(tc, xT, wT, us, ts, wt, x2, y, offs, out_0,
         quantise_g(half_slots(0), g_first[:])
         grouped2 = group_x2(nc.scalar.copy, 2, x2_turned[0], None)
         first0 = leave_bank(nc.scalar.copy, "first0", [0], 0, 4)
-        scatter_first(0, first0[:, 0])
+        scatter("scalar", 0, 0, first0[:, 0])
         for c in range(2):
             nc.vector.tensor_tensor(g_late[c][:], squared[2 + c][:], factor[1][:, slots(c)], MULT)
         for c in range(2):
@@ -373,21 +380,25 @@ def tile_attend_gfisher_sq_pl_kernel(tc, xT, wT, us, ts, wt, x2, y, offs, out_0,
         nc.scalar.copy(first1[:], first1_sums[:])
         quantise_x2(1, grouped2)
         quantise_x2(2, grouped3)
-        scatter_second(0, second0[:, 0])
+        scatter("vector", 0, 1, second0[:, 0])
         nc.sync.dma_start(out_rows[:, 0, :], out_window[0][:])
-        scatter_first(1, first1[:])
+        scatter("scalar", 1, 0, first1[:])
         second1 = leave_bank(nc.vector.tensor_copy, "second1", [1], 1, 1)
-        scatter_second(1, second1[:, 0])
+        scatter("vector", 1, 1, second1[:, 0])
         nc.sync.dma_start(out_rows[:, 1, :], out_window[1][:])
-        first23 = leave_bank(nc.scalar.copy, "first23", [2, 3], 0, 3, PAIRS_PLACE + 3 * PAIR_BYTES - HALF * 4)
-        second23 = leave_bank(nc.vector.tensor_copy, "second23", [2, 3], 1, 7, PAIRS_PLACE + PAIR_BYTES)
+        first23 = leave_bank(nc.scalar.copy, "first23", [2, 3], 0, 3)
+        second2 = leave_bank(nc.vector.tensor_copy, "second2", [2], 1, 7, PAIRS_PLACE)
+        second3 = leave_bank(nc.scalar.copy, "second3", [3], 1, 2)
         for j in range(2, LANES):
-            scatter_first(j, first23[:, j - 2])
-        for j in range(2, LANES):
-            scatter_second(j, second23[:, j - 2])
+            scatter("scalar", j, 0, first23[:, j - 2])
+        scatter("vector", 2, 1, second2[:, 0])
         nc.sync.dma_start(out_rows[:, 2, :], out_window[2][:])
+        scatter("scalar", 3, 1, second3[:, 0])
+        nc.scalar.dma_start(out_rows[:, 3, :], out_window[3][:])
 
-        pairs = [placed_at(f"pairs{g}", [P, GROUP * LANES], BF16, PAIRS_PLACE + g * PAIR_BYTES) for g in range(4)]
+        vector_pairs = placed_at("vector_pairs", [P, PAIR_STARTS[3] * LANES], BF16, PAIRS_PLACE)
+        pairs = [vector_pairs[:, PAIR_STARTS[n] * LANES : PAIR_STARTS[n + 1] * LANES] for n in range(3)]
+        pairs.extend(sbuf(f"pairs{n}", [P, PAIR_WIDTHS[n] * LANES], BF16)[:] for n in range(3, 5))
         out_grouped = [sbuf(f"out_grouped{k}", [P, width * LANES], BF16) for k, width in enumerate(COL_WIDTHS)]
         out_codes = sbuf("out_codes", [P, T], U32)
         out_scales = sbuf("out_scales", [P, GROUP], U8)
@@ -397,14 +408,14 @@ def tile_attend_gfisher_sq_pl_kernel(tc, xT, wT, us, ts, wt, x2, y, offs, out_0,
         def round_on_gpsimd(rounded, values):
             nc.gpsimd.tensor_scalar(rounded, values, 1.0, 0.0, MULT, ADD)
 
-        def round_lane(copy, j, first, end):
-            g, place = divmod(first, GROUP)
-            lanes = pairs[g][:].rearrange("p (u c e) -> p u c e", u=2, e=2)
-            copy(lanes[:, j // 2, place : place + end - first, j % 2], out_window[j][:, first:end])
+        def round_lane(copy, j, n):
+            lanes = pairs[n].rearrange("p (u c e) -> p u c e", u=2, e=2)
+            copy(lanes[:, j // 2, :, j % 2], out_window[j][:, PAIR_STARTS[n] : PAIR_STARTS[n + 1]])
 
         def join_pairs(copy, k):
-            g, place = divmod(COL_STARTS[k], GROUP)
-            pair_words = pairs[g][:].bitcast(F32).rearrange("p (u c) -> p c u", u=2)
+            n = max(m for m in range(len(PAIR_WIDTHS)) if PAIR_STARTS[m] <= COL_STARTS[k])
+            place = COL_STARTS[k] - PAIR_STARTS[n]
+            pair_words = pairs[n].bitcast(F32).rearrange("p (u c) -> p c u", u=2)
             copy(
                 out_grouped[k][:].bitcast(F32).rearrange("p (c u) -> p c u", u=2),
                 pair_words[:, place : place + COL_WIDTHS[k]],
@@ -420,21 +431,20 @@ def tile_attend_gfisher_sq_pl_kernel(tc, xT, wT, us, ts, wt, x2, y, offs, out_0,
             nc.sync.dma_start(words_out[:, first:end], out_codes[:, first:end].bitcast(I32))
 
         for j in range(2):
-            round_lane(round_on_gpsimd, j, 0, GROUP)
-        for j in range(3):
-            round_lane(nc.scalar.copy, j, 2 * GROUP, 3 * GROUP)
-        nc.scalar.dma_start(out_rows[:, 3, :], out_window[3][:])
-        round_lane(nc.scalar.copy, 3, 2 * GROUP, 3 * GROUP)
-        for k in [4, 5]:
-            join_pairs(nc.scalar.copy, k)
-        for j in range(LANES):
-            round_lane(nc.scalar.copy, j, 3 * GROUP, T)
-        for k in [6, 7, 8]:
-            join_pairs(nc.scalar.copy, k)
+            for n in [3, 4]:
+                round_lane(round_on_gpsimd, j, n)
+        for n, chunks in [(2, [4, 5]), (3, [6]), (4, [7, 8, 9])]:
+            for j in range(2, LANES):
+                round_lane(nc.scalar.copy, j, n)
+            if n == 2:
+                for m in range(3):
+                    for j in range(2):
+                        round_lane(nc.vector.tensor_copy, j, m)
+            for k in chunks:
+                join_pairs(nc.scalar.copy, k)
         for j in range(2, LANES):
-            round_lane(nc.vector.tensor_copy, j, 0, GROUP)
-        for j in range(LANES):
-            round_lane(nc.vector.tensor_copy, j, GROUP, 2 * GROUP)
+            for n in range(2):
+                round_lane(nc.vector.tensor_copy, j, n)
         join_pairs(nc.vector.tensor_copy, 0)
         stored = 0
         for k in range(len(COL_WIDTHS)):

@@ -27,8 +27,8 @@ HALF = I // 2
 SLOT_CHUNK = 128
 GROUP = T // 4
 
-VECTOR_DEALS = [96, 72]
-GPSIMD_WEIGHS = 192
+VECTOR_DEALS = [96, 56]
+GPSIMD_WEIGHS = 128
 COL_WIDTHS = [256, 256, 256, 256, 256, 128, 128, 256, 128, 128]
 COL_STARTS = [sum(COL_WIDTHS[:k]) for k in range(len(COL_WIDTHS) + 1)]
 
@@ -352,13 +352,12 @@ def tile_attend_gfisher_sq_pl_kernel(tc, xT, wT, us, ts, wt, x2, y, offs, out_0,
         turned.append(turn_back(1, scale_by_slot(1), 0))
         square(1, subtract(1))
         weigh_first(nc.gpsimd, 0, SLOT_CHUNK)
-        square(2, scale_and_subtract(0, turned[0]))
         first_grouped = sbuf("x2_grouped01", [P, 2, P * LANES], BF16)
-        nc.vector.tensor_copy(
+        nc.scalar.copy(
             first_grouped[:].bitcast(F32).rearrange("s j (p u) -> s j p u", u=2),
             word_bank[:].rearrange("s j u p -> s j p u"),
         )
-        weigh_first(nc.gpsimd, SLOT_CHUNK, GPSIMD_WEIGHS)
+        square(2, scale_and_subtract(0, turned[0]))
         square(3, scale_and_subtract(1, turned[1]))
         x2_turned = [turn_x2(2, 6)]
         weigh_first(nc.vector, GPSIMD_WEIGHS, HALF)

@@ -29,14 +29,16 @@ GROUP = T // 4
 
 VECTOR_DEALS = [96, 56]
 GPSIMD_WEIGHS = 128
-COL_WIDTHS = [256, 256, 256, 256, 256, 128, 128, 256, 128, 128]
+COL_WIDTHS = [256, 256, 512, 128, 128, 256, 256, 128, 128]
 COL_STARTS = [sum(COL_WIDTHS[:k]) for k in range(len(COL_WIDTHS) + 1)]
+
+WORD_STORE_ENDS = [512, 1024, 1536, 1792, 2048]
 
 X_PLACE = 0
 WINDOW_PLACE = X_PLACE + LANES * R * 4
 GATHER_PLACE = WINDOW_PLACE + (LANES - 1) * T * 4
 PAIRS_PLACE = GATHER_PLACE + T * 4
-PAIR_WIDTHS = [512, 512, 384, 128, 512]
+PAIR_WIDTHS = [1024, 256, 256, 512]
 PAIR_STARTS = [sum(PAIR_WIDTHS[:n]) for n in range(len(PAIR_WIDTHS) + 1)]
 
 
@@ -395,9 +397,9 @@ def tile_attend_gfisher_sq_pl_kernel(tc, xT, wT, us, ts, wt, x2, y, offs, out_0,
         scatter("scalar", 3, 1, second3[:, 0])
         nc.scalar.dma_start(out_rows[:, 3, :], out_window[3][:])
 
-        vector_pairs = placed_at("vector_pairs", [P, PAIR_STARTS[3] * LANES], BF16, PAIRS_PLACE)
-        pairs = [vector_pairs[:, PAIR_STARTS[n] * LANES : PAIR_STARTS[n + 1] * LANES] for n in range(3)]
-        pairs.extend(sbuf(f"pairs{n}", [P, PAIR_WIDTHS[n] * LANES], BF16)[:] for n in range(3, 5))
+        vector_pairs = placed_at("vector_pairs", [P, PAIR_STARTS[2] * LANES], BF16, PAIRS_PLACE)
+        pairs = [vector_pairs[:, PAIR_STARTS[n] * LANES : PAIR_STARTS[n + 1] * LANES] for n in range(2)]
+        pairs.extend(sbuf(f"pairs{n}", [P, PAIR_WIDTHS[n] * LANES], BF16)[:] for n in range(2, 4))
         out_grouped = [sbuf(f"out_grouped{k}", [P, width * LANES], BF16) for k, width in enumerate(COL_WIDTHS)]
         out_codes = sbuf("out_codes", [P, T], U32)
         out_scales = sbuf("out_scales", [P, GROUP], U8)
@@ -407,9 +409,9 @@ def tile_attend_gfisher_sq_pl_kernel(tc, xT, wT, us, ts, wt, x2, y, offs, out_0,
         def round_on_gpsimd(rounded, values):
             nc.gpsimd.tensor_scalar(rounded, values, 1.0, 0.0, MULT, ADD)
 
-        def round_lane(copy, j, n):
+        def round_lane(copy, j, n, part=slice(None)):
             lanes = pairs[n].rearrange("p (u c e) -> p u c e", u=2, e=2)
-            copy(lanes[:, j // 2, :, j % 2], out_window[j][:, PAIR_STARTS[n] : PAIR_STARTS[n + 1]])
+            copy(lanes[:, j // 2, part, j % 2], out_window[j][:, PAIR_STARTS[n] : PAIR_STARTS[n + 1]][:, part])
 
         def join_pairs(copy, k):
             n = max(m for m in range(len(PAIR_WIDTHS)) if PAIR_STARTS[m] <= COL_STARTS[k])
@@ -430,20 +432,20 @@ def tile_attend_gfisher_sq_pl_kernel(tc, xT, wT, us, ts, wt, x2, y, offs, out_0,
             nc.sync.dma_start(words_out[:, first:end], out_codes[:, first:end].bitcast(I32))
 
         for j in range(2):
-            for n in [3, 4]:
+            for n in [2, 3]:
                 round_lane(round_on_gpsimd, j, n)
-        for n, chunks in [(2, [4, 5]), (3, [6]), (4, [7, 8, 9])]:
+        for n, chunks in [(1, [4]), (2, [5]), (3, [6, 7, 8])]:
             for j in range(2, LANES):
                 round_lane(nc.scalar.copy, j, n)
-            if n == 2:
-                for m in range(3):
+            if n == 1:
+                for m in [1, 0]:
                     for j in range(2):
                         round_lane(nc.vector.tensor_copy, j, m)
             for k in chunks:
                 join_pairs(nc.scalar.copy, k)
-        for j in range(2, LANES):
-            for n in range(2):
-                round_lane(nc.vector.tensor_copy, j, n)
+        round_lane(nc.vector.tensor_copy, 2, 0)
+        for g in range(2):
+            round_lane(nc.vector.tensor_copy, 3, 0, slice(g * GROUP, (g + 1) * GROUP))
         join_pairs(nc.vector.tensor_copy, 0)
         stored = 0
         for k in range(len(COL_WIDTHS)):
@@ -451,7 +453,7 @@ def tile_attend_gfisher_sq_pl_kernel(tc, xT, wT, us, ts, wt, x2, y, offs, out_0,
                 join_pairs(nc.vector.tensor_copy, k + 1)
             quantise_out(k)
             done = COL_STARTS[k + 1]
-            if done % GROUP == 0 or done == T - GROUP // 2:
+            if done in WORD_STORE_ENDS:
                 store_words(stored, done)
                 stored = done
         for q in range(4):

@@ -29,7 +29,7 @@ GROUP = T // 4
 
 VECTOR_DEALS = [96, 56]
 GPSIMD_WEIGHS = 128
-COL_WIDTHS = [256, 256, 512, 128, 128, 256, 256, 128, 128]
+COL_WIDTHS = [256, 256, 256, 256, 256, 128, 128, 256, 128, 128]
 COL_STARTS = [sum(COL_WIDTHS[:k]) for k in range(len(COL_WIDTHS) + 1)]
 
 WORD_STORE_ENDS = [512, 1024, 1536, 1792, 2048]
@@ -38,7 +38,7 @@ X_PLACE = 0
 WINDOW_PLACE = X_PLACE + LANES * R * 4
 GATHER_PLACE = WINDOW_PLACE + (LANES - 1) * T * 4
 PAIRS_PLACE = GATHER_PLACE + T * 4
-PAIR_WIDTHS = [1024, 256, 256, 512]
+PAIR_WIDTHS = [1024, 384, 128, 512]
 PAIR_STARTS = [sum(PAIR_WIDTHS[:n]) for n in range(len(PAIR_WIDTHS) + 1)]
 
 
@@ -105,9 +105,9 @@ def tile_attend_gfisher_sq_pl_kernel(tc, xT, wT, us, ts, wt, x2, y, offs, out_0,
         for j in range(1, LANES):
             nc.sync.dma_start(w_window[j][:], w_rows[:, j, :])
         nc.sync.dma_start(x_sb[:], xT.rearrange("(p j) r -> p j r", j=LANES))
-        nc.sync.dma_start(y_half[0][:], y_rows[:, :, half_slots(0)])
         for j in range(2):
             nc.sync.dma_start(x2_plane[j][:], x2_rows[:, j, :])
+        nc.sync.dma_start(y_half[0][:], y_rows[:, :, half_slots(0)])
         nc.sync.dma_start(y_half[1][:], y_rows[:, :, half_slots(1)])
         nc.sync.dma_start(x2_rest[:], x2_rows[:, 2:4, :])
 
@@ -374,7 +374,7 @@ def tile_attend_gfisher_sq_pl_kernel(tc, xT, wT, us, ts, wt, x2, y, offs, out_0,
             quantise_g(slots(2 + c), g_late[c][:])
         first1_sums = psum("first1_sums", [P, HALF], 5)
         second_product(first1_sums[:], 1, 0)
-        x2_turned.append(turn_x2(3, 6))
+        x2_turned.append(turn_x2(3, 7))
         grouped3 = group_x2(nc.vector.tensor_copy, 3, x2_turned[1], "g_late1")
         second0 = leave_bank(nc.vector.tensor_copy, "second0", [0], 1, 0)
         first1 = sbuf("first1", [P, HALF], F32)
@@ -388,7 +388,7 @@ def tile_attend_gfisher_sq_pl_kernel(tc, xT, wT, us, ts, wt, x2, y, offs, out_0,
         scatter("vector", 1, 1, second1[:, 0])
         nc.sync.dma_start(out_rows[:, 1, :], out_window[1][:])
         first23 = leave_bank(nc.scalar.copy, "first23", [2, 3], 0, 3)
-        second2 = leave_bank(nc.vector.tensor_copy, "second2", [2], 1, 7, PAIRS_PLACE)
+        second2 = leave_bank(nc.vector.tensor_copy, "second2", [2], 1, 6, PAIRS_PLACE)
         second3 = leave_bank(nc.scalar.copy, "second3", [3], 1, 2)
         for j in range(2, LANES):
             scatter("scalar", j, 0, first23[:, j - 2])
@@ -434,7 +434,7 @@ def tile_attend_gfisher_sq_pl_kernel(tc, xT, wT, us, ts, wt, x2, y, offs, out_0,
         for j in range(2):
             for n in [2, 3]:
                 round_lane(round_on_gpsimd, j, n)
-        for n, chunks in [(1, [4]), (2, [5]), (3, [6, 7, 8])]:
+        for n, chunks in [(1, [4, 5]), (2, [6]), (3, [7, 8, 9])]:
             for j in range(2, LANES):
                 round_lane(nc.scalar.copy, j, n)
             if n == 1:

@@ -28,7 +28,7 @@ SLOT_CHUNK = 128
 GROUP = T // 4
 
 VECTOR_DEALS = [96, 56]
-GPSIMD_WEIGHS = 128
+GPSIMD_WEIGHS = 176
 COL_WIDTHS = [256, 256, 256, 256, 256, 128, 128, 256, 128, 128]
 COL_STARTS = [sum(COL_WIDTHS[:k]) for k in range(len(COL_WIDTHS) + 1)]
 
@@ -38,7 +38,7 @@ X_PLACE = 0
 WINDOW_PLACE = X_PLACE + LANES * R * 4
 GATHER_PLACE = WINDOW_PLACE + (LANES - 1) * T * 4
 PAIRS_PLACE = GATHER_PLACE + T * 4
-PAIR_WIDTHS = [1024, 384, 128, 512]
+PAIR_WIDTHS = [1024, 384, 640]
 PAIR_STARTS = [sum(PAIR_WIDTHS[:n]) for n in range(len(PAIR_WIDTHS) + 1)]
 
 
@@ -360,6 +360,7 @@ def tile_attend_gfisher_sq_pl_kernel(tc, xT, wT, us, ts, wt, x2, y, offs, out_0,
             word_bank[:].rearrange("s j u p -> s j p u"),
         )
         square(2, scale_and_subtract(0, turned[0]))
+        weigh_first(nc.gpsimd, SLOT_CHUNK, GPSIMD_WEIGHS)
         square(3, scale_and_subtract(1, turned[1]))
         x2_turned = [turn_x2(2, 6)]
         weigh_first(nc.vector, GPSIMD_WEIGHS, HALF)
@@ -399,7 +400,7 @@ def tile_attend_gfisher_sq_pl_kernel(tc, xT, wT, us, ts, wt, x2, y, offs, out_0,
 
         vector_pairs = placed_at("vector_pairs", [P, PAIR_STARTS[2] * LANES], BF16, PAIRS_PLACE)
         pairs = [vector_pairs[:, PAIR_STARTS[n] * LANES : PAIR_STARTS[n + 1] * LANES] for n in range(2)]
-        pairs.extend(sbuf(f"pairs{n}", [P, PAIR_WIDTHS[n] * LANES], BF16)[:] for n in range(2, 4))
+        pairs.extend(sbuf(f"pairs{n}", [P, PAIR_WIDTHS[n] * LANES], BF16)[:] for n in range(2, 3))
         out_grouped = [sbuf(f"out_grouped{k}", [P, width * LANES], BF16) for k, width in enumerate(COL_WIDTHS)]
         out_codes = sbuf("out_codes", [P, T], U32)
         out_scales = sbuf("out_scales", [P, GROUP], U8)
@@ -432,11 +433,10 @@ def tile_attend_gfisher_sq_pl_kernel(tc, xT, wT, us, ts, wt, x2, y, offs, out_0,
             nc.sync.dma_start(words_out[:, first:end], out_codes[:, first:end].bitcast(I32))
 
         for j in range(2):
-            for n in [2, 3]:
-                round_lane(round_on_gpsimd, j, n)
-        for n, chunks in [(1, [4, 5]), (2, [6]), (3, [7, 8, 9])]:
+            round_lane(round_on_gpsimd, j, 2)
+        for n, part, chunks in [(1, slice(0, 384), [4, 5]), (2, slice(0, 384), [6, 7]), (2, slice(384, 640), [8, 9])]:
             for j in range(2, LANES):
-                round_lane(nc.scalar.copy, j, n)
+                round_lane(nc.scalar.copy, j, n, part)
             if n == 1:
                 for m in [1, 0]:
                     for j in range(2):

@@ -29,7 +29,7 @@ GROUP = T // 4
 
 VECTOR_DEALS = [96, 56]
 GPSIMD_WEIGHS = 176
-COL_WIDTHS = [256, 256, 256, 256, 256, 128, 128, 256, 128, 128]
+COL_WIDTHS = [256, 256, 256, 256, 256, 256, 256, 128, 128]
 COL_STARTS = [sum(COL_WIDTHS[:k]) for k in range(len(COL_WIDTHS) + 1)]
 
 WORD_STORE_ENDS = [512, 1024, 1536, 1792, 2048]
@@ -37,9 +37,8 @@ WORD_STORE_ENDS = [512, 1024, 1536, 1792, 2048]
 X_PLACE = 0
 WINDOW_PLACE = X_PLACE + LANES * R * 4
 GATHER_PLACE = WINDOW_PLACE + (LANES - 1) * T * 4
-PAIRS_PLACE = GATHER_PLACE + T * 4
-PAIR_WIDTHS = [1024, 384, 640]
-PAIR_STARTS = [sum(PAIR_WIDTHS[:n]) for n in range(len(PAIR_WIDTHS) + 1)]
+SIDE = T // 2
+VECTOR_HELPS = 256
 
 
 def tile_attend_gfisher_sq_pl_kernel(tc, xT, wT, us, ts, wt, x2, y, offs, out_0, out_1, out_2):
@@ -322,13 +321,13 @@ def tile_attend_gfisher_sq_pl_kernel(tc, xT, wT, us, ts, wt, x2, y, offs, out_0,
                 sums, plane_codes[j].bitcast(E4M3X4), plane_scales[j], g_codes[:, cols].bitcast(E5M2X4), g_scales[:, cols]
             )
 
-        def leave_bank(copy, name, planes, h, bank, place=None):
+        def leave_bank(copy, name, planes, h, bank, values=None):
             sums = psum(name + "_sums", [P, len(planes), HALF], bank)
             for e, j in enumerate(planes):
                 second_product(sums[:, e], j, h)
-            shape = [P, len(planes), HALF]
-            values = sbuf(name, shape, F32) if place is None else placed_at(name, shape, F32, place)
-            copy(values[:], sums[:])
+            if values is None:
+                values = sbuf(name, [P, len(planes), HALF], F32)[:]
+            copy(values, sums[:])
             return values
 
         def scatter(engine, j, h, values):
@@ -389,7 +388,9 @@ def tile_attend_gfisher_sq_pl_kernel(tc, xT, wT, us, ts, wt, x2, y, offs, out_0,
         scatter("vector", 1, 1, second1[:, 0])
         nc.sync.dma_start(out_rows[:, 1, :], out_window[1][:])
         first23 = leave_bank(nc.scalar.copy, "first23", [2, 3], 0, 3)
-        second2 = leave_bank(nc.vector.tensor_copy, "second2", [2], 1, 6, PAIRS_PLACE)
+        rounded = [sbuf(f"rounded{n}", [P, LANES * SIDE], BF16) for n in range(2)]
+        in_lane1 = rounded[0][:, SIDE : SIDE + 2 * HALF].bitcast(F32).unsqueeze(1)
+        second2 = leave_bank(nc.vector.tensor_copy, "second2", [2], 1, 6, in_lane1)
         second3 = leave_bank(nc.scalar.copy, "second3", [3], 1, 2)
         for j in range(2, LANES):
             scatter("scalar", j, 0, first23[:, j - 2])
@@ -398,29 +399,25 @@ def tile_attend_gfisher_sq_pl_kernel(tc, xT, wT, us, ts, wt, x2, y, offs, out_0,
         scatter("scalar", 3, 1, second3[:, 0])
         nc.scalar.dma_start(out_rows[:, 3, :], out_window[3][:])
 
-        vector_pairs = placed_at("vector_pairs", [P, PAIR_STARTS[2] * LANES], BF16, PAIRS_PLACE)
-        pairs = [vector_pairs[:, PAIR_STARTS[n] * LANES : PAIR_STARTS[n + 1] * LANES] for n in range(2)]
-        pairs.extend(sbuf(f"pairs{n}", [P, PAIR_WIDTHS[n] * LANES], BF16)[:] for n in range(2, 3))
         out_grouped = [sbuf(f"out_grouped{k}", [P, width * LANES], BF16) for k, width in enumerate(COL_WIDTHS)]
         out_codes = sbuf("out_codes", [P, T], U32)
         out_scales = sbuf("out_scales", [P, GROUP], U8)
         words_out = out_1.rearrange("a p c l -> p (a c l)").bitcast(I32)
         scales_out = out_2.rearrange("a q c -> q (a c)").bitcast(I32).rearrange("q (g c) -> g q c", g=4)
 
-        def round_on_gpsimd(rounded, values):
-            nc.gpsimd.tensor_scalar(rounded, values, 1.0, 0.0, MULT, ADD)
+        def round_on_gpsimd(target, values):
+            nc.gpsimd.tensor_scalar(target, values, 1.0, 0.0, MULT, ADD)
 
-        def round_lane(copy, j, n, part=slice(None)):
-            lanes = pairs[n].rearrange("p (u c e) -> p u c e", u=2, e=2)
-            copy(lanes[:, j // 2, part, j % 2], out_window[j][:, PAIR_STARTS[n] : PAIR_STARTS[n + 1]][:, part])
+        def round_lane(copy, j, first, end):
+            n, place = divmod(first, SIDE)
+            copy(rounded[n][:, j * SIDE + place : j * SIDE + place + end - first], out_window[j][:, first:end])
 
-        def join_pairs(copy, k):
-            n = max(m for m in range(len(PAIR_WIDTHS)) if PAIR_STARTS[m] <= COL_STARTS[k])
-            place = COL_STARTS[k] - PAIR_STARTS[n]
-            pair_words = pairs[n].bitcast(F32).rearrange("p (u c) -> p c u", u=2)
+        def interleave(copy, k):
+            n, place = divmod(COL_STARTS[k], SIDE)
+            lanes = rounded[n][:].rearrange("p (t c) -> p t c", t=LANES)[:, :, place : place + COL_WIDTHS[k]]
             copy(
-                out_grouped[k][:].bitcast(F32).rearrange("p (c u) -> p c u", u=2),
-                pair_words[:, place : place + COL_WIDTHS[k]],
+                out_grouped[k][:].rearrange("p (q i t) -> p q t i", i=LINE, t=LANES),
+                lanes.rearrange("p t (q i) -> p q t i", i=LINE),
             )
 
         def quantise_out(k):
@@ -432,25 +429,22 @@ def tile_attend_gfisher_sq_pl_kernel(tc, xT, wT, us, ts, wt, x2, y, offs, out_0,
         def store_words(first, end):
             nc.sync.dma_start(words_out[:, first:end], out_codes[:, first:end].bitcast(I32))
 
-        for j in range(2):
-            round_lane(round_on_gpsimd, j, 2)
-        for n, part, chunks in [(1, slice(0, 384), [4, 5]), (2, slice(0, 384), [6, 7]), (2, slice(384, 640), [8, 9])]:
-            for j in range(2, LANES):
-                round_lane(nc.scalar.copy, j, n, part)
-            if n == 1:
-                for m in [1, 0]:
-                    for j in range(2):
-                        round_lane(nc.vector.tensor_copy, j, m)
-            for k in chunks:
-                join_pairs(nc.scalar.copy, k)
-        round_lane(nc.vector.tensor_copy, 2, 0)
-        for g in range(2):
-            round_lane(nc.vector.tensor_copy, 3, 0, slice(g * GROUP, (g + 1) * GROUP))
-        join_pairs(nc.vector.tensor_copy, 0)
+        for j, n in [(0, 0), (0, 1), (1, 1)]:
+            round_lane(round_on_gpsimd, j, n * SIDE, (n + 1) * SIDE)
+        for j, n in [(1, 0), (2, 1), (2, 0)]:
+            round_lane(nc.vector.tensor_copy, j, n * SIDE, (n + 1) * SIDE)
+        round_lane(nc.vector.tensor_copy, 3, 0, GROUP)
+        round_lane(nc.vector.tensor_copy, 3, GROUP, SIDE)
+        round_lane(nc.vector.tensor_copy, 3, T - VECTOR_HELPS, T)
+        for k in range(4, len(COL_WIDTHS)):
+            if COL_STARTS[k] < T - VECTOR_HELPS:
+                round_lane(nc.scalar.copy, 3, COL_STARTS[k], COL_STARTS[k + 1])
+            interleave(nc.scalar.copy, k)
+        interleave(nc.vector.tensor_copy, 0)
         stored = 0
         for k in range(len(COL_WIDTHS)):
             if k + 1 < 4:
-                join_pairs(nc.vector.tensor_copy, k + 1)
+                interleave(nc.vector.tensor_copy, k + 1)
             quantise_out(k)
             done = COL_STARTS[k + 1]
             if done in WORD_STORE_ENDS:

@@ -28,7 +28,7 @@ SLOT_CHUNK = 128
 GROUP = T // 4
 
 VECTOR_DEALS = [96, 56]
-GPSIMD_WEIGHS = 176
+GPSIMD_WEIGHS = 224
 COL_WIDTHS = [256, 256, 256, 256, 256, 256, 256, 128, 128]
 COL_STARTS = [sum(COL_WIDTHS[:k]) for k in range(len(COL_WIDTHS) + 1)]
 
@@ -352,7 +352,7 @@ def tile_attend_gfisher_sq_pl_kernel(tc, xT, wT, us, ts, wt, x2, y, offs, out_0,
         square(0, subtract(0))
         turned.append(turn_back(1, scale_by_slot(1), 0))
         square(1, subtract(1))
-        weigh_first(nc.gpsimd, 0, SLOT_CHUNK)
+        weigh_first(nc.vector, 0, SLOT_CHUNK)
         first_grouped = sbuf("x2_grouped01", [P, 2, P * LANES], BF16)
         nc.scalar.copy(
             first_grouped[:].bitcast(F32).rearrange("s j (p u) -> s j p u", u=2),

@@ -88,8 +88,7 @@ def tile_attend_gfisher_sq_pl_kernel(tc, xT, wT, us, ts, wt, x2, y, offs, out_0,
             for j in range(LANES)
         ]
         x_sb = placed_at("x_sb", [P, LANES, R], F32, X_PLACE)
-        x2_plane = [sbuf(f"x2_plane{j}", [P, R], F32) for j in range(2)]
-        x2_rest = sbuf("x2_rest", [P, 2, R], F32)
+        x2_plane = [sbuf(f"x2_plane{j}", [P, R], F32) for j in range(LANES)]
         y_half = [sbuf(f"y_half{h}", [P, LANES, HALF], F32) for h in range(2)]
         us_sb = sbuf("us_sb", [P, LANES], F32)
         wt_sb = sbuf("wt_sb", [P, LANES], F32)
@@ -108,7 +107,8 @@ def tile_attend_gfisher_sq_pl_kernel(tc, xT, wT, us, ts, wt, x2, y, offs, out_0,
             nc.sync.dma_start(x2_plane[j][:], x2_rows[:, j, :])
         nc.sync.dma_start(y_half[0][:], y_rows[:, :, half_slots(0)])
         nc.sync.dma_start(y_half[1][:], y_rows[:, :, half_slots(1)])
-        nc.sync.dma_start(x2_rest[:], x2_rows[:, 2:4, :])
+        for j in range(2, LANES):
+            nc.sync.dma_start(x2_plane[j][:], x2_rows[:, j, :])
 
         identity = sbuf("identity", [P, P], F32)
         zeros = placed_at("zeros", [P, T + 2 * P], F32, WINDOW_PLACE + (T - P) * 4)[:, :P]
@@ -305,7 +305,7 @@ def tile_attend_gfisher_sq_pl_kernel(tc, xT, wT, us, ts, wt, x2, y, offs, out_0,
 
         def turn_x2(j, bank):
             turned = psum(f"x2_turned{j}", [P, LANES, P], bank)
-            rows = x2_rest[:, j - 2, :].rearrange("p (s t) -> p t s", t=LANES)
+            rows = x2_plane[j][:].rearrange("p (s t) -> p t s", t=LANES)
             for t in range(LANES):
                 nc.tensor.transpose(turned[:, t, :], rows[:, t, :], identity[:])
             return turned

@@ -88,7 +88,8 @@ def tile_attend_gfisher_sq_pl_kernel(tc, xT, wT, us, ts, wt, x2, y, offs, out_0,
             for j in range(LANES)
         ]
         x_sb = placed_at("x_sb", [P, LANES, R], F32, X_PLACE)
-        x2_plane = [sbuf(f"x2_plane{j}", [P, R], F32) for j in range(LANES)]
+        x2_first = sbuf("x2_first", [P, 2, R], F32)
+        x2_late = [sbuf(f"x2_late{j}", [P, R], F32) for j in range(2)]
         y_half = [sbuf(f"y_half{h}", [P, LANES, HALF], F32) for h in range(2)]
         us_sb = sbuf("us_sb", [P, LANES], F32)
         wt_sb = sbuf("wt_sb", [P, LANES], F32)
@@ -103,12 +104,11 @@ def tile_attend_gfisher_sq_pl_kernel(tc, xT, wT, us, ts, wt, x2, y, offs, out_0,
         for j in range(1, LANES):
             nc.sync.dma_start(w_window[j][:], w_rows[:, j, :])
         nc.sync.dma_start(x_sb[:], xT.rearrange("(p j) r -> p j r", j=LANES))
-        for j in range(2):
-            nc.sync.dma_start(x2_plane[j][:], x2_rows[:, j, :])
+        nc.sync.dma_start(x2_first[:], x2_rows[:, 0:2, :])
         nc.sync.dma_start(y_half[0][:], y_rows[:, :, half_slots(0)])
         nc.sync.dma_start(y_half[1][:], y_rows[:, :, half_slots(1)])
-        for j in range(2, LANES):
-            nc.sync.dma_start(x2_plane[j][:], x2_rows[:, j, :])
+        for j in range(2):
+            nc.sync.dma_start(x2_late[j][:], x2_rows[:, 2 + j, :])
 
         identity = sbuf("identity", [P, P], F32)
         zeros = placed_at("zeros", [P, T + 2 * P], F32, WINDOW_PLACE + (T - P) * 4)[:, :P]
@@ -206,7 +206,7 @@ def tile_attend_gfisher_sq_pl_kernel(tc, xT, wT, us, ts, wt, x2, y, offs, out_0,
         for j in range(2):
             nc.scalar.copy(
                 x2_words[:, j].rearrange("p u s e -> p s u e"),
-                x2_plane[j][:].rearrange("p (s u e) -> p s u e", u=2, e=2),
+                x2_first[:, j].rearrange("p (s u e) -> p s u e", u=2, e=2),
             )
 
         x_codes = sbuf("x_codes", [P, LANES, P], U32)
@@ -305,7 +305,7 @@ def tile_attend_gfisher_sq_pl_kernel(tc, xT, wT, us, ts, wt, x2, y, offs, out_0,
 
         def turn_x2(j, bank):
             turned = psum(f"x2_turned{j}", [P, LANES, P], bank)
-            rows = x2_plane[j][:].rearrange("p (s t) -> p t s", t=LANES)
+            rows = x2_late[j - 2][:].rearrange("p (s t) -> p t s", t=LANES)
             for t in range(LANES):
                 nc.tensor.transpose(turned[:, t, :], rows[:, t, :], identity[:])
             return turned
@@ -361,7 +361,7 @@ def tile_attend_gfisher_sq_pl_kernel(tc, xT, wT, us, ts, wt, x2, y, offs, out_0,
         square(2, scale_and_subtract(0, turned[0]))
         weigh_first(nc.gpsimd, SLOT_CHUNK, GPSIMD_WEIGHS)
         square(3, scale_and_subtract(1, turned[1]))
-        x2_turned = [turn_x2(2, 6)]
+        x2_turned = [turn_x2(2, 0)]
         weigh_first(nc.vector, GPSIMD_WEIGHS, HALF)
         quantise_x2(0, first_grouped[:].rearrange("s j w -> s (j w)"))
         quantise_g(half_slots(0), g_first[:])
@@ -374,9 +374,9 @@ def tile_attend_gfisher_sq_pl_kernel(tc, xT, wT, us, ts, wt, x2, y, offs, out_0,
             quantise_g(slots(2 + c), g_late[c][:])
         first1_sums = psum("first1_sums", [P, HALF], 5)
         second_product(first1_sums[:], 1, 0)
-        x2_turned.append(turn_x2(3, 7))
+        x2_turned.append(turn_x2(3, 0))
         grouped3 = group_x2(nc.vector.tensor_copy, 3, x2_turned[1], "g_late1")
-        second0 = leave_bank(nc.vector.tensor_copy, "second0", [0], 1, 0)
+        second0 = leave_bank(nc.vector.tensor_copy, "second0", [0], 1, 7)
         first1 = sbuf("first1", [P, HALF], F32)
         nc.scalar.copy(first1[:], first1_sums[:])
         quantise_x2(1, grouped2)

from contextlib import ExitStack

import concourse.mybir as mybir

D, R, I, T = 512, 512, 512, 2048
FLOPS = 2 * 2 * D * R * I

F32 = mybir.dt.float32
BF16 = mybir.dt.bfloat16
U32 = mybir.dt.uint32
I32 = mybir.dt.int32
U16 = mybir.dt.uint16
U8 = mybir.dt.uint8
E4M3X4 = mybir.dt.float8_e4m3fn_x4
E5M2X4 = mybir.dt.float8_e5m2_x4
MULT = mybir.AluOpType.mult
ADD = mybir.AluOpType.add
SUBTRACT = mybir.AluOpType.subtract
COPY = mybir.ActivationFunctionType.Copy
SQUARE = mybir.ActivationFunctionType.Square

P = 128
LANES = 4
BANK_BYTES = 2048
LINE = 4
HALF = I // 2
SLOT_CHUNK = 128
GROUP = T // 4

VECTOR_DEALS = [96, 56]
GPSIMD_WEIGHS = 224
COL_WIDTHS = [256, 256, 256, 256, 256, 256, 256, 128, 128]
COL_STARTS = [sum(COL_WIDTHS[:k]) for k in range(len(COL_WIDTHS) + 1)]

WORD_STORE_ENDS = [512, 1024, 1536, 1792, 2048]

X_PLACE = 0
WINDOW_PLACE = X_PLACE + LANES * R * 4
GATHER_PLACE = WINDOW_PLACE + (LANES - 1) * T * 4
SIDE = T // 2
VECTOR_HELPS = 256


def tile_attend_gfisher_sq_pl_kernel(tc, xT, wT, us, ts, wt, x2, y, offs, out_0, out_1, out_2):
    nc = tc.nc
    with ExitStack() as ctx:
        keep = ctx.enter_context(tc.tile_pool(name="keep", bufs=1))
        placed = ctx.enter_context(tc.tile_pool(name="placed", bufs=1))
        banks = ctx.enter_context(tc.psum_pool(name="banks", bufs=1))

        def psum(name, shape, bank):
            return banks.tile(shape, F32, name=name, offset=bank * BANK_BYTES)

        def sbuf(name, shape, dtype, on=None):
            return keep.tile(shape, dtype, name=name, tag=on or name, align_bytes=64)

        def placed_at(name, shape, dtype, offset):
            return placed.tile(shape, dtype, name=name, align_bytes=64, offset=offset)

        def slots(c):
            return slice(c * SLOT_CHUNK, (c + 1) * SLOT_CHUNK)

        def half_slots(h):
            return slice(h * HALF, (h + 1) * HALF)

        def half_entries(h):
            return offsets[:, h * HALF // 16 : (h + 1) * HALF // 16]

        def product(bank, stationary_codes, stationary_scales, moving_codes, moving_scales):
            nc.tensor.matmul_mx(
                bank,
                lhsT=stationary_codes,
                lhsT_scale=stationary_scales,
                rhs=moving_codes,
                rhs_scale=moving_scales,
                start=True,
                stop=True,
            )

        offsets = keep.tile([P, I // 16], U16, name="offsets")
        w_rows = wT.rearrange("(p j) c -> p j c", j=LANES)
        x2_rows = x2.rearrange("(p j) r -> p j r", j=LANES)
        y_rows = y.rearrange("(s t) i -> s t i", t=LANES)
        out_rows = out_0.rearrange("(p j) c -> p j c", j=LANES)

        w_window = [
            placed_at("w_window1", [P, T], F32, GATHER_PLACE) if j == 1 else sbuf(f"w_window{j}", [P, T], F32)
            for j in range(LANES)
        ]
        x_sb = placed_at("x_sb", [P, LANES, R], F32, X_PLACE)
        x2_first = sbuf("x2_first", [P, 2, R], F32)
        x2_late = [sbuf(f"x2_late{j}", [P, R], F32) for j in range(2)]
        y_half = [sbuf(f"y_half{h}", [P, LANES, HALF], F32) for h in range(2)]
        us_sb = sbuf("us_sb", [P, LANES], F32)
        wt_sb = sbuf("wt_sb", [P, LANES], F32)
        ts_window = sbuf("ts_window", [P, T], F32)
        ts_columns = sbuf("ts_columns", [P, T // P], F32)

        nc.sync.dma_start(ts_columns[:], ts[0:1, :].rearrange("o (k c) -> (o k) c", k=P))
        nc.sync.dma_start(w_window[0][:], w_rows[:, 0, :])
        nc.sync.dma_start(offsets[:], offs)
        nc.scalar.dma_start(us_sb[:], us.rearrange("(s t) o -> s (t o)", t=LANES))
        nc.scalar.dma_start(wt_sb[:], wt.rearrange("(s t) o -> s (t o)", t=LANES))
        for j in range(1, LANES):
            nc.sync.dma_start(w_window[j][:], w_rows[:, j, :])
        nc.sync.dma_start(x_sb[:], xT.rearrange("(p j) r -> p j r", j=LANES))
        nc.sync.dma_start(x2_first[:], x2_rows[:, 0:2, :])
        nc.sync.dma_start(y_half[0][:], y_rows[:, :, half_slots(0)])
        nc.sync.dma_start(y_half[1][:], y_rows[:, :, half_slots(1)])
        for j in range(2):
            nc.sync.dma_start(x2_late[j][:], x2_rows[:, 2 + j, :])

        identity = sbuf("identity", [P, P], F32)
        zeros = placed_at("zeros", [P, T + 2 * P], F32, WINDOW_PLACE + (T - P) * 4)[:, :P]
        nc.gpsimd.memset(zeros, 0.0)
        nc.gpsimd.affine_select(
            out=identity[:],
            in_=zeros,
            compare_op=mybir.AluOpType.not_equal,
            fill=1.0,
            base=0,
            pattern=[[-1, P]],
            channel_multiplier=1,
        )
        out_window = [sbuf("out_window0", [P, T], F32)]
        for j in range(1, LANES):
            out_window.append(placed_at(f"out_window{j}", [P, T], F32, WINDOW_PLACE + (j - 1) * T * 4))
        nc.vector.memset(out_window[0][:], 0.0)
        for j in range(1, LANES):
            nc.gpsimd.memset(out_window[j][:], 0.0)

        window_by_row = ts_window[:].rearrange("p (k c) -> p k c", k=P)
        for b in range(T // P // 4):
            bank = psum(f"ts_spread{b}", [P, 4, P], 4 + b)
            for c in range(4):
                column = ts_columns[:, 4 * b + c : 4 * b + c + 1]
                nc.tensor.transpose(bank[:, c, :], column.to_broadcast([P, P]), identity[:])
            nc.scalar.copy(window_by_row[:, :, 4 * b : 4 * b + 4], bank[:].rearrange("p c k -> p k c"))

        w_pair = sbuf("w_pair", [P, 2, I], BF16)
        nc.vector.tensor_copy(w_pair[:, 0], w_window[0][:].indirect(offsets[:]))
        ts_first = sbuf("ts_first", [P, HALF], F32)
        ts_second = w_pair[:, 1].bitcast(F32)
        ts_squared = [sbuf(f"ts_squared{h}", [P, HALF], F32) for h in range(2)]
        for h, values in [(1, ts_second), (0, ts_first[:])]:
            nc.vector.tensor_copy(values, ts_window[:].indirect(half_entries(h)))
            nc.scalar.activation(ts_squared[h][:], values, SQUARE)

        ts_turned = psum("ts_turned", [P, 2, P], 0)
        for c in range(2):
            nc.tensor.transpose(ts_turned[:, c, :], ts_second[:, slots(c)], identity[:])
        nc.vector.tensor_copy(w_pair[:, 1], w_window[1][:].indirect(offsets[:]))
        ts_by_slot = sbuf("ts_by_slot", [P, 2], F32)
        nc.scalar.copy(ts_by_slot[:], ts_turned[:, :, 0])

        us_squared = sbuf("us_squared", [P, LANES], F32)
        row_factor = sbuf("row_factor", [P, LANES], F32)
        nc.vector.tensor_tensor(us_squared[:], us_sb[:], us_sb[:], MULT)
        nc.vector.tensor_tensor(row_factor[:], us_squared[:], wt_sb[:], MULT)
        factor = [sbuf(f"factor{h}", [P, HALF, LANES], F32) for h in range(2)]
        by_lane = sbuf("factor_by_lane", [P, LANES, HALF], F32)
        for t in range(LANES):
            nc.scalar.activation(by_lane[:, t, :], ts_squared[0][:], COPY, scale=row_factor[:, t : t + 1])
        w_grouped = [
            placed_at(f"w_grouped{h}", [P, HALF, LANES], BF16, GATHER_PLACE + h * HALF * LANES * 2) for h in range(2)
        ]
        for h in range(2):
            nc.scalar.copy(w_grouped[h][:, :, 0:2], w_pair[:, :, half_slots(h)].rearrange("p j i -> p i j"))
        for c in range(2):
            nc.scalar.copy(
                factor[0][:, slots(c)].rearrange("p (q i) t -> p q t i", i=LINE),
                by_lane[:, :, slots(c)].rearrange("p t (q i) -> p q t i", i=LINE),
            )
        w_last = placed_at("w_last", [P, 2, HALF], BF16, GATHER_PLACE + I * LANES * 2)
        for j in range(2, LANES):
            nc.vector.tensor_copy(w_last[:, j - 2], w_window[j][:].indirect(half_entries(1)))
            nc.vector.tensor_copy(w_grouped[0][:, :, j], w_window[j][:].indirect(half_entries(0)))
        nc.scalar.copy(w_grouped[1][:, :, 2:4], w_last[:].rearrange("p j i -> p i j"))
        w_codes = sbuf("w_codes", [P, I], U32)
        w_scales = sbuf("w_scales", [P, I], U8)
        for h in [1, 0]:
            values = w_grouped[h][:].rearrange("p i j -> p (i j)")
            nc.vector.quantize_mx(w_codes[:, half_slots(h)].bitcast(E4M3X4), w_scales[:, half_slots(h)], values)
        for c in range(2):
            nc.gpsimd.tensor_tensor(
                factor[1][:, slots(c)],
                ts_squared[1][:, slots(c)].unsqueeze(2).to_broadcast([P, SLOT_CHUNK, LANES]),
                row_factor[:].unsqueeze(1).to_broadcast([P, SLOT_CHUNK, LANES]),
                MULT,
            )

        x_grouped = sbuf("x_grouped", [P, LANES, P, LANES], BF16, on="factor_by_lane")

        def deal_x(copy, tiles, first, end):
            copy(
                x_grouped[:, tiles, first:end, :].rearrange("p t s j -> p s j t"),
                x_sb[:].rearrange("p j (s t) -> p s j t", t=LANES)[:, first:end, :, tiles],
            )

        for pair, share in enumerate(VECTOR_DEALS):
            tiles = slice(2 * pair, 2 * pair + 2)
            deal_x(nc.vector.tensor_copy, tiles, 0, share)
            deal_x(nc.scalar.copy, tiles, share, P)

        x2_words = placed_at("x2_words", [P, 2, 2, P, 2], BF16, X_PLACE)
        for j in range(2):
            nc.scalar.copy(
                x2_words[:, j].rearrange("p u s e -> p s u e"),
                x2_first[:, j].rearrange("p (s u e) -> p s u e", u=2, e=2),
            )

        x_codes = sbuf("x_codes", [P, LANES, P], U32)
        x_scales = sbuf("x_scales", [P, LANES, P], U8)
        scores = []
        for t in range(LANES):
            values = x_grouped[:, t, :, :].rearrange("p s j -> p (s j)")
            nc.vector.quantize_mx(x_codes[:, t, :].bitcast(E4M3X4), x_scales[:, t, :], values)
            bank = psum(f"scores{t}", [P, HALF], t)
            product(
                bank[:],
                x_codes[:, t, :].bitcast(E4M3X4),
                x_scales[:, t, :],
                w_codes[:, half_slots(0)].bitcast(E4M3X4),
                w_scales[:, half_slots(0)],
            )
            scores.append(bank)
        slot_sums = [psum(f"scores_by_slot{c}", [P, R], 4 + c)[:] for c in range(2)]
        for c in range(2):
            product(
                slot_sums[c],
                w_codes[:, slots(2 + c)].bitcast(E4M3X4),
                w_scales[:, slots(2 + c)],
                x_codes[:].rearrange("p t s -> p (t s)").bitcast(E4M3X4),
                x_scales[:].rearrange("p t s -> p (t s)"),
            )

        def scale_by_slot(c, on=None):
            scaled = sbuf(f"scaled_by_slot{c}", [P, 2, HALF], F32, on=on)
            for h in range(2):
                nc.scalar.activation(scaled[:, h], slot_sums[c][:, half_slots(h)], COPY, scale=ts_by_slot[:, c : c + 1])
            return scaled

        def turn_back(c, scaled, first_bank):
            turned = []
            for h in range(2):
                pair = psum(f"turned_back{c}{h}", [P, 2, SLOT_CHUNK], first_bank + h)
                for e in range(2):
                    nc.tensor.transpose(pair[:, e, :], scaled[:, h, slots(e)], identity[:])
                    turned.append(pair[:, e, :])
            return turned

        def scale_scores(target, t, cols):
            nc.vector.scalar_tensor_tensor(target, scores[t][:, cols], us_sb[:, t : t + 1], ts_first[:, cols], MULT, MULT)

        z_first = sbuf("z_first", [P, HALF], F32)
        z_rest = sbuf("z_rest", [P, LANES - 1, HALF], F32)
        error_first = sbuf("error_first", [P, LANES, HALF], F32)
        squared = [sbuf(f"squared{c}", [P, SLOT_CHUNK, LANES], F32) for c in range(4)]
        g_first = sbuf("g_first", [P, HALF, LANES], BF16)
        g_late = [sbuf(f"g_late{c}", [P, SLOT_CHUNK, LANES], BF16) for c in range(2)]
        g_codes = sbuf("g_codes", [P, I], U32)
        g_scales = sbuf("g_scales", [P, I], U8)

        def subtract(c):
            errors = error_first[:, :, slots(c)]
            nc.vector.tensor_tensor(errors[:, 1:], z_rest[:, :, slots(c)], y_half[0][:, 1:, slots(c)], SUBTRACT)
            return errors

        def scale_and_subtract(c, turned):
            errors = sbuf(f"error_late{c}", [P, LANES, SLOT_CHUNK], F32)
            for t in range(LANES):
                nc.vector.scalar_tensor_tensor(
                    errors[:, t, :], turned[t], us_sb[:, t : t + 1], y_half[1][:, t, slots(c)], MULT, SUBTRACT
                )
            return errors[:]

        def square(c, errors):
            nc.scalar.activation(
                squared[c][:].rearrange("p (q i) t -> p q t i", i=LINE),
                errors.rearrange("p t (q i) -> p q t i", i=LINE),
                SQUARE,
            )

        def weigh_first(engine, first, end):
            c = first // SLOT_CHUNK
            part = slice(first - c * SLOT_CHUNK, end - c * SLOT_CHUNK)
            engine.tensor_tensor(g_first[:, first:end], squared[c][:, part], factor[0][:, first:end], MULT)

        def quantise_g(cols, values):
            nc.vector.quantize_mx(
                g_codes[:, cols].bitcast(E5M2X4), g_scales[:, cols], values.rearrange("p i t -> p (i t)")
            )

        x2_codes = [sbuf(f"x2_codes{u}", [P, n, P], U32) for u, n in enumerate([2, 1, 1])]
        x2_scales = [sbuf(f"x2_scales{u}", [P, n, P], U8) for u, n in enumerate([2, 1, 1])]
        plane_codes = [x2_codes[0][:, 0], x2_codes[0][:, 1], x2_codes[1][:, 0], x2_codes[2][:, 0]]
        plane_scales = [x2_scales[0][:, 0], x2_scales[0][:, 1], x2_scales[1][:, 0], x2_scales[2][:, 0]]

        def quantise_x2(u, grouped):
            nc.vector.quantize_mx(
                x2_codes[u][:].rearrange("s j p -> s (j p)").bitcast(E4M3X4),
                x2_scales[u][:].rearrange("s j p -> s (j p)"),
                grouped,
            )

        def turn_x2(j, bank):
            turned = psum(f"x2_turned{j}", [P, LANES, P], bank)
            rows = x2_late[j - 2][:].rearrange("p (s t) -> p t s", t=LANES)
            for t in range(LANES):
                nc.tensor.transpose(turned[:, t, :], rows[:, t, :], identity[:])
            return turned

        def group_x2(copy, j, turned, on):
            grouped = sbuf(f"x2_grouped{j}", [P, P, LANES], BF16, on=on)
            copy(grouped[:], turned[:].rearrange("s t p -> s p t"))
            return grouped[:].rearrange("s p t -> s (p t)")

        def second_product(sums, j, h):
            cols = half_slots(h)
            product(
                sums, plane_codes[j].bitcast(E4M3X4), plane_scales[j], g_codes[:, cols].bitcast(E5M2X4), g_scales[:, cols]
            )

        def leave_bank(copy, name, planes, h, bank, values=None):
            sums = psum(name + "_sums", [P, len(planes), HALF], bank)
            for e, j in enumerate(planes):
                second_product(sums[:, e], j, h)
            if values is None:
                values = sbuf(name, [P, len(planes), HALF], F32)[:]
            copy(values, sums[:])
            return values

        def scatter(engine, j, h, values):
            places = out_window[j][:].indirect(half_entries(h))
            if engine == "scalar":
                nc.scalar.activation(places, values, COPY)
            else:
                nc.vector.tensor_copy(places, values)

        turned = [turn_back(0, scale_by_slot(0), 6)]
        scale_scores(z_first[:], 0, half_slots(0))
        for t in range(1, LANES - 1):
            scale_scores(z_rest[:, t - 1, :], t, half_slots(0))
        for c in range(2):
            scale_scores(z_rest[:, LANES - 2, slots(c)], LANES - 1, slots(c))
        nc.gpsimd.tensor_tensor(error_first[:, 0, :], z_first[:], y_half[0][:, 0, :], SUBTRACT)
        words = x2_words[:].rearrange("p j u s e -> p (j u) (s e)").bitcast(F32)
        word_bank = psum("x2_turned_words", [P, 2, 2, P], 3)
        for j in range(2):
            for u in range(2):
                nc.tensor.transpose(word_bank[:, j, u, :], words[:, 2 * j + u, :], identity[:])
        square(0, subtract(0))
        turned.append(turn_back(1, scale_by_slot(1), 0))
        square(1, subtract(1))
        weigh_first(nc.vector, 0, SLOT_CHUNK)
        first_grouped = sbuf("x2_grouped01", [P, 2, P * LANES], BF16)
        nc.scalar.copy(
            first_grouped[:].bitcast(F32).rearrange("s j (p u) -> s j p u", u=2),
            word_bank[:].rearrange("s j u p -> s j p u"),
        )
        square(2, scale_and_subtract(0, turned[0]))
        weigh_first(nc.gpsimd, SLOT_CHUNK, GPSIMD_WEIGHS)
        square(3, scale_and_subtract(1, turned[1]))
        x2_turned = [turn_x2(2, 0)]
        weigh_first(nc.vector, GPSIMD_WEIGHS, HALF)
        quantise_x2(0, first_grouped[:].rearrange("s j w -> s (j w)"))
        quantise_g(half_slots(0), g_first[:])
        grouped2 = group_x2(nc.scalar.copy, 2, x2_turned[0], None)
        first0 = leave_bank(nc.scalar.copy, "first0", [0], 0, 4)
        scatter("scalar", 0, 0, first0[:, 0])
        for c in range(2):
            nc.vector.tensor_tensor(g_late[c][:], squared[2 + c][:], factor[1][:, slots(c)], MULT)
        for c in range(2):
            quantise_g(slots(2 + c), g_late[c][:])
        first1_sums = psum("first1_sums", [P, HALF], 5)
        second_product(first1_sums[:], 1, 0)
        x2_turned.append(turn_x2(3, 0))
        grouped3 = group_x2(nc.vector.tensor_copy, 3, x2_turned[1], "g_late1")
        second0 = leave_bank(nc.vector.tensor_copy, "second0", [0], 1, 7)
        first1 = sbuf("first1", [P, HALF], F32)
        nc.scalar.copy(first1[:], first1_sums[:])
        quantise_x2(1, grouped2)
        quantise_x2(2, grouped3)
        scatter("vector", 0, 1, second0[:, 0])
        nc.sync.dma_start(out_rows[:, 0, :], out_window[0][:])
        scatter("scalar", 1, 0, first1[:])
        second1 = leave_bank(nc.vector.tensor_copy, "second1", [1], 1, 1)
        scatter("vector", 1, 1, second1[:, 0])
        nc.sync.dma_start(out_rows[:, 1, :], out_window[1][:])
        first23 = leave_bank(nc.scalar.copy, "first23", [2, 3], 0, 3)
        rounded = [sbuf(f"rounded{n}", [P, LANES * SIDE], BF16) for n in range(2)]
        in_lane1 = rounded[0][:, SIDE : SIDE + 2 * HALF].bitcast(F32).unsqueeze(1)
        second2 = leave_bank(nc.vector.tensor_copy, "second2", [2], 1, 6, in_lane1)
        second3 = leave_bank(nc.scalar.copy, "second3", [3], 1, 2)
        for j in range(2, LANES):
            scatter("scalar", j, 0, first23[:, j - 2])
        scatter("vector", 2, 1, second2[:, 0])
        nc.sync.dma_start(out_rows[:, 2, :], out_window[2][:])
        scatter("scalar", 3, 1, second3[:, 0])
        nc.scalar.dma_start(out_rows[:, 3, :], out_window[3][:])

        out_grouped = [sbuf(f"out_grouped{k}", [P, width * LANES], BF16) for k, width in enumerate(COL_WIDTHS)]
        out_codes = sbuf("out_codes", [P, T], U32)
        out_scales = sbuf("out_scales", [P, GROUP], U8)
        words_out = out_1.rearrange("a p c l -> p (a c l)").bitcast(I32)
        scales_out = out_2.rearrange("a q c -> q (a c)").bitcast(I32).rearrange("q (g c) -> g q c", g=4)

        def round_on_gpsimd(target, values):
            nc.gpsimd.tensor_scalar(target, values, 1.0, 0.0, MULT, ADD)

        def round_lane(copy, j, first, end):
            n, place = divmod(first, SIDE)
            copy(rounded[n][:, j * SIDE + place : j * SIDE + place + end - first], out_window[j][:, first:end])

        def interleave(copy, k):
            n, place = divmod(COL_STARTS[k], SIDE)
            lanes = rounded[n][:].rearrange("p (t c) -> p t c", t=LANES)[:, :, place : place + COL_WIDTHS[k]]
            copy(
                out_grouped[k][:].rearrange("p (q i t) -> p q t i", i=LINE, t=LANES),
                lanes.rearrange("p t (q i) -> p q t i", i=LINE),
            )

        def quantise_out(k):
            first, end = COL_STARTS[k], COL_STARTS[k + 1]
            g, place = divmod(first, GROUP)
            plane = out_scales[4 * g :, place : place + end - first]
            nc.vector.quantize_mx(out_codes[:, first:end].bitcast(E4M3X4), plane, out_grouped[k][:])

        def store_words(first, end):
            nc.sync.dma_start(words_out[:, first:end], out_codes[:, first:end].bitcast(I32))

        for j, n in [(0, 0), (0, 1), (1, 1)]:
            round_lane(round_on_gpsimd, j, n * SIDE, (n + 1) * SIDE)
        for j, n in [(1, 0), (2, 1), (2, 0)]:
            round_lane(nc.vector.tensor_copy, j, n * SIDE, (n + 1) * SIDE)
        round_lane(nc.vector.tensor_copy, 3, 0, GROUP)
        round_lane(nc.vector.tensor_copy, 3, GROUP, SIDE)
        round_lane(nc.vector.tensor_copy, 3, T - VECTOR_HELPS, T)
        for k in range(4, len(COL_WIDTHS)):
            if COL_STARTS[k] < T - VECTOR_HELPS:
                round_lane(nc.scalar.copy, 3, COL_STARTS[k], COL_STARTS[k + 1])
            interleave(nc.scalar.copy, k)
        interleave(nc.vector.tensor_copy, 0)
        stored = 0
        for k in range(len(COL_WIDTHS)):
            if k + 1 < 4:
                interleave(nc.vector.tensor_copy, k + 1)
            quantise_out(k)
            done = COL_STARTS[k + 1]
            if done in WORD_STORE_ENDS:
                store_words(stored, done)
                stored = done
        for q in range(4):
            queue = nc.scalar if q % 2 else nc.sync
            queue.dma_start(scales_out[:, 4 * q : 4 * q + 4, :], out_scales[32 * q : 32 * q + 16, :].bitcast(I32))
